import numpy as np, ml_dtypes
CORES = [48,51,52,55]
N = 4
BF = ml_dtypes.bfloat16
def gentries(a):
    return np.ascontiguousarray(a.reshape(8, 16, -1).transpose(0, 2, 1)).reshape(8, -1)
def gtable(e):
    e = np.asarray(e); return np.ascontiguousarray(e.reshape(8, -1, 16).transpose(0, 2, 1)).reshape(128, -1).astype(np.int32)
V, G, SL, VI, RO, TH, A = 3328, 256, 1024, 5, 2, 16, 160
W = V + (N - 1) * G
def corners(rng, share, wild=False):
    cen = rng.integers(30, 226, (8, 3, 16)); k = np.arange(8)[None, :, None]; u = rng.random((N, 8, V))
    cen[6, 0] = rng.integers(246, 256, 16); cen[7, 0] = rng.integers(0, 10, 16)
    cl = (u > 0.6).astype(np.int64) + (u > 0.85)
    amp = np.exp2(7 * rng.random((N, 8, 1, V))).astype(np.int64) - 1 if wild else rng.integers(0, 25, (N, 8, 1, V))
    x = cen[k, cl].transpose(0, 1, 3, 2) + np.floor((2 * amp + 1) * rng.random((N, 8, 16, V))).astype(np.int64) - amp
    odd = (rng.random((N, 8, 1, V)) < 0.08) & (rng.random((N, 8, 16, V)) < 0.3)
    x = np.clip(np.where(odd, rng.integers(0, 256, x.shape), x), 0, 255)
    flat = rng.random((N, 8, 1, V)); x = np.where(flat < 0.01, 0, np.where(flat > 0.99, 255, x))
    ql = np.where(rng.random(cl.shape) < 0.85, cl, rng.integers(0, 3, cl.shape))
    q = np.ascontiguousarray(np.clip(cen[k, ql].transpose(0, 1, 3, 2) + rng.integers(-6, 7, (N, 8, 16, V)), 0, 255))
    lost = rng.random((N, 8, V)) < share
    nb = rng.integers(0, W, (N, 8, 4, W))
    snd = rng.integers(0, 4, (N, 8, (N - 1) * G)) * W + rng.integers(0, V, (N, 8, (N - 1) * G))
    return cen, np.ascontiguousarray(x), q, lost, nb, snd
def pack(x, q, lost, nb, snd):
    x = np.where(lost[:, :, None, :], -64, x)
    return {"xv": x.reshape(N, 128, V).astype(np.float32).astype(BF), "cq": q.reshape(N, 128, V).astype(np.float32).astype(BF),
            "nb": nb.reshape(N, 8, 4 * W).astype(np.int32), "snd": np.stack([gtable(a) for a in snd])}
def setup_inputs(rng):
    cen, x, q, lost, nb, snd = corners(rng, rng.choice(np.array([0.2, 0.3, 0.4, 0.5]), (N, 8, 1)))
    return pack(x, q, lost, nb, snd)
def setup_inputs_room(rng):
    cen, x, q, lost, nb, snd = corners(rng, 0.3)
    sizes = np.array([SL, SL + 1, SL - 1, 0, 1, V, SL + 64, SL + 2]); n = rng.choice(sizes, (N, 8)); n[:, 0] = SL; n[0] = sizes
    lost = np.argsort(rng.random((N, 8, V)), axis=-1) < n[..., None]
    return pack(x, q, lost, nb, snd)
def setup_inputs_chain(rng):
    cen, x, q, lost, nb, snd = corners(rng, 0.15); H = 32
    nb[:, 5] = np.where(rng.random((N, 4, W)) < 0.25, np.arange(W), nb[:, 5])
    nb[:, 6] = np.where(rng.random((N, 4, W)) < 0.125, rng.choice(np.array([0, V - 1, V, W - 1]), (N, 4, W)), nb[:, 6])
    for a in range(N):
        for g in range(8):
            o = rng.permutation(V); se = o[:128]; ci = o[128:128 + H * VI]; ta = o[128 + H * VI:192 + H * VI]; c = cen[g, 0][:, None]
            lost[a, g, se] = True; lost[a, g, ci] = True; lost[a, g, ta] = False
            x[a, g][:, ta] = np.clip(c + rng.integers(-4, 5, (16, 64)), 0, 255); q[a, g][:, se] = np.clip(c + rng.integers(-6, 7, (16, 128)), 0, 255)
            for k in range(4):
                ck = rng.permutation(ci).reshape(H, VI)
                nb[a, g, k][ck[:, :-1]] = ck[:, 1:]; nb[a, g, k][ck[:, -1]] = rng.choice(ta, H)
                i = rng.integers(1, VI + 1, 128); i[:32] = 1; i[32 + k:64:4] = 0
                nb[a, g, k][se] = np.where(i < VI, ck[rng.integers(0, H, 128), np.minimum(i, VI - 1)], rng.choice(ta, 128))
    return pack(x, q, lost, nb, snd)
def setup_inputs_ties(rng):
    cen, x, q, lost, nb, snd = corners(rng, 0.2); place = np.argsort(rng.random((N, 8, V)), axis=-1)
    for a in range(N):
        for g in range(8):
            lost[a, g, place[a, g, :48]] = True; lost[a, g, place[a, g, 48:240]] = False
    L = np.sum(lost, axis=(1, 2)); R = A - 8 * TH - 7
    base = np.array([TH] + [R // 8 + (1 if i < R % 8 else 0) for i in range(8)] + [TH + 1] * 7)
    for a in range(N):
        for g in range(8):
            for s in range(48):
                kind = s % 6; v = place[a, g, s]; mo = place[a, g, 48 + 4 * s:52 + 4 * s]
                if kind < 4:
                    c = rng.integers(30, 226, 16); e = np.array(base)
                    e[15] += (int(L[a]) & 7) + (1 if kind == 1 else 0)
                    e[0] += 1 if kind == 2 else 0
                    e = e[rng.permutation(16)]
                    m = np.stack([c + e, c - e, c, c + (1 if kind == 3 else 0)])[rng.permutation(4)]
                else:
                    m = np.zeros((4, 16), np.int64); c = np.zeros(16, np.int64); i = rng.permutation(16); kk = np.sort(rng.permutation(4)[:2])
                    m[kk[0], i[:7]] = rng.integers(160, 200, 7); m[kk[1], i[7:14]] = rng.integers(210, 256, 7)
                    if kind == 5: m = 255 - m; c = 255 - c
                x[a, g][:, mo] = m.T; q[a, g][:, v] = c; nb[a, g][:, v] = mo
    return pack(x, q, lost, nb, snd)
def point(rng, links, slots, bad):
    n = bad.size; S = (N - 1) * G
    pk = np.argsort(rng.random((4, n)), axis=1); back = np.argsort(pk, axis=1); links[:, bad] = bad[pk]
    t = rng.permutation(np.concatenate([np.arange(n), rng.integers(0, n, S - n)])); kk = rng.integers(0, 4, S)
    slots[:] = kk * W + bad[back[kk, t]]
def setup_inputs_flood(rng):
    cen, x, q, lost, nb, snd = corners(rng, 0.15); S = (N - 1) * G; B = 3 * S // 4; E = min(S, V - 2 * SL - 32); H = SL - SL % 256; M = min(SL, S)
    for a in range(N):
        for g in range(8):
            n = (SL + E if a == 0 else SL, 1, B if a == 0 else 0, 0, 8, 8, 8, B)[g]; m = G if g == 6 else SL; c = cen[g, 0][:, None]
            o = rng.permutation(V)
            if g == 0 and a == 0:
                s = int(rng.integers(0, V - SL + 1)); run = (o >= s) & (o < s + SL); rest = o[~run]
                o = np.concatenate([rest[:SL + 32], o[run], rest[SL + 32:]])
            se = o[:m]; good = o[SL:SL + 32]; bad = o[SL + 32:SL + 32 + n]
            lost[a, g] = False; lost[a, g, o[:SL]] = True
            x[a, g][:, good] = np.clip(c + rng.integers(-4, 5, (16, 32)), 0, 255); q[a, g][:, se] = np.clip(c + rng.integers(-6, 7, (16, m)), 0, 255)
            far = np.argsort(rng.random((16, n)), axis=0) < 6
            x[a, g][:, bad] = np.where(far, (c + 128) & 255, np.clip(c + rng.integers(-4, 5, (16, n)), 0, 255))
            nb[a, g][:, se] = rng.choice(good, (4, m)); k = rng.integers(0, 4, m)
            if g == 0:
                nb[a, g, k, se] = rng.permutation(bad[:SL])
                if a == 0: point(rng, nb[a, g], snd[a, g], bad[SL:])
                else: nb[a, g, k[:G], se[:G]] = V + (a - 1) * G + rng.permutation(G)
            elif g == 1: nb[a, g, k, se] = bad[0]
            elif g == 2 and a == 0: point(rng, nb[a, g], snd[a, g], bad)
            elif g == 2: nb[a, g, k[:G], se[:G]] = V + (a - 1) * G + rng.permutation(G)
            elif g == 4 or g == 5:
                sh = o[SL + 40:SL + 72]; kk = rng.integers(0, 4, 32); nb[a, g, kk, sh] = bad[0]
                snd[a, g] = (kk * W + sh)[rng.integers(0, 32, S)]
                if g == 4: nb[a, g, k[:G], se[:G]] = V + rng.permutation(G)
                else: nb[a, g, k[:H], se[:H]] = V + int(rng.integers(0, S))
            elif g == 6:
                sh = o[SL + 40:SL + 72]; kk = rng.integers(0, 4, 32); nb[a, g, kk, sh] = rng.choice(bad, 32)
                snd[a, g].reshape(N - 1, G)[:, :48] = (kk * W + sh)[rng.integers(0, 32, (N - 1, 48))]
                nb[a, g, k, se] = V + rng.integers(0, N - 1, G) * G + rng.integers(0, 4 if a & 1 else 48, G)
            elif g == 7:
                point(rng, nb[a, g], snd[a, g], bad)
                nb[a, g, k[:M], se[:M]] = V + rng.permutation(S)[:M]
    return pack(x, q, lost, nb, snd)
def setup_inputs_spread(rng):
    share = rng.choice(np.array([0.02, 0.1, 0.25, 0.4, 0.6, 0.9]), (N, 8, 1)); share[:, 3] = 0.3; share[int(rng.integers(0, N))] = 0
    cen, x, q, lost, nb, snd = corners(rng, share, True)
    return pack(x, q, lost, nb, snd)
def check_inputs(d):
    bad = []
    x = np.asarray(d["xv"]).astype(np.float32).reshape(N, 8, 16, V); q = np.asarray(d["cq"]).astype(np.float32)
    fine = (x >= 0) & (x <= 255) & (x == np.floor(x)); gone = x == -64
    if not np.all(np.all(fine, axis=2) | np.all(gone, axis=2)): bad.append("columns of xv")
    if not np.all((q >= 0) & (q <= 255) & (q == np.floor(q))): bad.append("range of cq")
    if np.min(d["nb"]) < 0 or np.max(d["nb"]) > W - 1: bad.append("range of nb")
    if np.min(d["snd"]) < 0 or np.max(d["snd"]) > 4 * W - 1 or np.max(np.asarray(d["snd"]) % W) > V - 1: bad.append("entries of snd")
    return bad
def reference(xv, cq, nb, snd):
    x = np.full((N, 8, 16, W), -64, np.int32); x[..., :V] = xv.astype(np.float32).astype(np.int32).reshape(N, 8, 16, V)
    q = cq.astype(np.float32).astype(np.int32).reshape(N, 8, 16, V)
    ln = nb.astype(np.int64).reshape(N, 8, 4, W); sl = np.stack([gentries(a) for a in snd]).astype(np.int64)
    for rnd in range(RO):
        shown = np.take_along_axis(ln.reshape(N, 8, 4 * W), sl, 2)
        col = np.take_along_axis(x, shown[:, :, None, :], 3).reshape(N, 8, 16, N - 1, G)
        x[..., V:] = np.stack([np.concatenate([col[(a - d) % N][:, :, d - 1] for d in range(1, N)], axis=2) for a in range(N)])
        lost = x[:, :, 0, :V] < 0; many = np.add.reduce(lost.astype(np.int64), axis=2)
        lim = A + (np.add.reduce(many, axis=1) & 7)
        nx = np.array(x); nl = np.array(ln); fall = np.zeros((N, 8, W), bool)
        for a in range(N):
            v = np.argsort(~lost[a], axis=1, kind="stable")[:, :SL]; there = np.arange(SL)[None, :] < many[a][:, None]
            qa = np.take_along_axis(q[a], v[:, None, :], 2)[:, :, None, :]
            j = np.take_along_axis(ln[a], np.broadcast_to(v[:, None, :], (8, 4, SL)), 2)
            for t in range(VI):
                m = np.take_along_axis(x[a], j.reshape(8, 1, 4 * SL), 2).reshape(8, 16, 4, SL)
                ok = np.add.reduce((np.abs(m - qa) <= TH).astype(np.int32), axis=1) >= 9
                if t < VI - 1: j = np.where(ok, j, np.take_along_axis(ln[a], j, 2))
            found = np.all(ok, axis=1) & there
            y = (np.add.reduce(m, axis=2) - np.max(m, axis=2) - np.min(m, axis=2)) >> 1
            D = np.add.reduce(np.abs(m - y[:, :, None, :]), axis=1)
            good = np.max(D, axis=1) <= lim[a]
            worst = np.take_along_axis(j, np.argmax(D, axis=1)[:, None, :], 1)[:, 0]
            for g in range(8):
                b = np.flatnonzero(found[g] & good[g]); c = v[g][b]
                nx[a, g][:, c] = y[g][:, b]; nl[a, g][:, c] = j[g][:, b]
                fall[a, g, worst[g][found[g] & ~good[g]]] = True
        for a in range(N):
            down = np.array(fall[a, :, :V])
            for d in range(1, N):
                flag = fall[(a + d) % N, :, V + (d - 1) * G:V + d * G]; s = shown[a, :, (d - 1) * G:d * G]
                for g in range(8):
                    h = s[g][flag[g]]; down[g, h[h < V]] = True
            nx[a, :, :, :V] = np.where(down[:, None, :], -64, nx[a, :, :, :V])
        x = nx; ln = nl
    return {"yx": np.ascontiguousarray(x[..., :V]).reshape(N, 128, V).astype(np.float32).astype(BF), "yn": np.ascontiguousarray(ln[..., :V]).reshape(N, 8, 4 * V).astype(np.float32)}

@@ -1,0 +1,574 @@
+from concourse.bass import DstId, RemoteDMATransfer
+from concourse.mybir import AluOpType as AL, AxisListType as AX, ActivationFunctionType as AF
+
+V, W, SL, GH = 3328, 4096, 1024, 768
+NC = V // 16
+XR = W + SL + 16
+X0 = [16, 16 + XR]
+LR = W + SL
+L0 = [0, LR]
+M32, M64, M1 = 1.5 * 2 ** 28, 1.5 * 2 ** 29, 1.5 * 2 ** 23
+ABLK = [(0, 2, 3), (0, 3, 3), (0, 4, 3), (1, 2, 3), (1, 3, 3), (1, 4, 3)]
+B, F, I, U = "bfloat16", "float32", "int32", "uint16"
+MN = {"C": 1.0, "C8": 8.0, "C16": 16.0, "C128": 128.0, "C512": 512.0, "L0": 0, "L1": 1, "L2": 2, "L3": 3, "FL": 0}
+IDN = {"p": 1.0, "n": -1.0, "h": 0.5, "nh": -0.5, "nf": -2.0 ** 22}
+SB = {"X": ([16 + 2 * XR], B), "LT": ([2 * LR], B), "Q": ([V + 16], B), "MS": ([144 * len(MN)], B), "ID": ([128 * len(IDN)], B),
+      "KY": ([4, 64], F), "GO": ([2, 64], B), "ZP": ([2, 224], B), "ZQ": ([2, 144], B), "JW": ([8, 64], B), "RC": ([8, 65], F)}
+for _d, _s in ((B, "HI1024 LO1024 ZR1024 MK768 SG768 MT16 OM144 BO128 BN128 PA256 ON256 CT512 QT512 D01024 D14096 RR8192 LW416 I11024 I21024 "
+                   "I31024 QS1024 NL208 F1208 WH48 S0768 S1768 G048 G148 N048 N148 LH1024 LG4096 DT2048 MG2048 IN8192 DD4096 SS512 R11024 "
+                   "R51024 R61024 R71024 R81024 YD1024 AB4096 NF64 AC64"),
+               (F, "IT144 IG128 PS16 IS1024 CX208 MM208 G88 MF16 DM256 M216 CC224 T2224 TM208 T3224 TH32 Z1208 Z2208 Z3208 FA208 WT96 RN256 "
+                   "J1256 DG512 K1128 DJ256 JS256 YN832 TA520 TB520 ZA128 ZB128"),
+               (I, "NB1024 SN48 SI96 PI8 LI8 WI192 JI256 JF256 JD768 K264 KD64"), (U, "SU96 BU192 UL208 UX208 WU48 JU1536")):
+    for _x in _s.split(): SB[_x[:2]] = ([int(_x[2:])], _d)
+SB = {k: ([128] + v[0], v[1]) for k, v in SB.items()}
+SCRATCH = {k: ("sbuf", v[0], v[1]) for k, v in SB.items()}
+for _b in range(8):
+    SCRATCH["ps%d" % _b] = ("psum", [128, 512], F)
+EXT = {"xv": ([128, V], B), "cq": ([128, V], B), "nb": ([8, 4 * W], I), "snd": ([128, 48], I), "yx": ([128, V], B), "yn": ([8, 4 * V], F)}
+SEMAPHORES = ["eV", "eA", "eT", "eG", "loc", "ar0", "ar1", "ar2", "ar3"] + ["d%d" % _i for _i in range(30)]
+SZ = {B: 2, F: 4, I: 4, U: 2}
+S_ = slice(None)
+CY, GA, PE, LAT, LOOK, TRIES, NPERT, AMP = 1.04, 1.56, 0.5, 120.0, 150.0, 1500, 10, 15000.0
+
+
+def shape_of(n):
+    return SB.get(n) or EXT.get(n) or ([128, 512], F)
+
+
+def ap(n, *ix):
+    if len(ix) == 2 and isinstance(ix[0], int) and isinstance(ix[1], int): ix = (S_, slice(ix[0], ix[1]))
+    return (n, ix or (S_,), None)
+
+
+def ind(win, off):
+    return (win[0], win[1], off)
+
+
+def extent(a):
+    shp = shape_of(a[0])[0]
+    ix = list(a[1]) + [S_] * (len(shp) - len(a[1]))
+    rs = [range(s)[x] if isinstance(x, slice) else range(x, x + 1) for s, x in zip(shp, ix)]
+    r = rs[-1]
+    m = ((1 << len(r)) - 1) << r[0] if r.step == 1 else sum(1 << j for j in r)
+    n, lo = len(r), r[0]
+    if len(shp) == 3:
+        m = sum(m << (shp[2] * j) for j in rs[1]); n *= len(rs[1]); lo += shp[2] * rs[1][0]
+    return m, sum(1 << j for j in rs[0]), n, len(rs[0]), lo
+
+
+def nel(a):
+    return 16 * extent(a[2])[2] if a[2] else extent(a)[2]
+
+
+def real(T, a):
+    if not isinstance(a, tuple): return a
+    x = T[a[0]][a[1] if len(a[1]) > 1 else a[1][0]]
+    return x.indirect(real(T, a[2])) if a[2] else x
+
+
+def build():
+    ops = []
+
+    def add(eng, kind, args, rd, wr, cost, whole=False):
+        R, Wr = {}, {}
+        for lst, out in ((rd, R), (wr, Wr)):
+            for a in lst:
+                if not isinstance(a, tuple): continue
+                for b, o in ((a, out), (a[2], R)):
+                    if b:
+                        e = extent(ap(b[0]) if whole and b[0] not in SB else b)
+                        o[(b[0], e[1])] = o.get((b[0], e[1]), 0) | e[0]
+        ops.append({"e": eng, "k": kind, "a": args, "r": R, "w": Wr, "c": cost})
+
+    def vc(out, *x):
+        n = nel(x[0]) if x else nel(out)
+        if x and x[0][2]: return 60 + n * GA * CY
+        return max(64, n * (0.5 if all(SZ[shape_of(a[0])[1]] == 2 for a in (out,) + x) else 1)) * CY
+
+    def ts(out, x, s1, o0, s2=None, o1=None): add("V", "ts", (out, x, s1, s2, o0, o1), [x, s1, s2], [out], vc(out, x))
+    def cp(out, x): add("V", "cp", (out, x), [x], [out], vc(out, x))
+    def ms(out, c): add("V", "ms", (out, c), [], [out], vc(out))
+    def scan(out, a, b, o0, o1): add("V", "scan", (out, a, b, o0, o1), [a, b], [out], vc(out, a, b))
+    def red(out, x, neg): add("V", "red", (out, x, neg), [x], [out], max(64, nel(x)) * CY)
+    def iota(out, pat, base, cm): add("G", "iota", (out, pat, base, cm), [], [out], 130 + 2 * nel(out) * CY)
+
+    def tt(out, x, y, o):
+        add("V", "tt", (out, x, y, o), [x, y], [out], vc(out, x) if x[2] else max(64, nel(x) * (2 if x[0] in SB and y[0] in SB else 1)) * CY)
+
+    def act(out, x, fn, bias=0.0, scale=1.0):
+        add("A", "act", (out, x, fn, bias, scale), [x, bias, scale], [out], 20 + vc(out, x) if x[2] else max(64, nel(x)) * CY)
+
+    def mm(out, terms, start=True, stop=True, whole=False):
+        c = sum(max(min(64, nel(l)), nel(r)) * (4 if shape_of(l[0])[1] == F else 1) for l, r in terms) * PE
+        add("T", "mm", (out, terms, start, stop), [x for t in terms for x in t] + ([] if start else [out]), [out], c, whole)
+
+    def dma(q, pairs, after=()):
+        by = sum(extent(o)[2] * extent(o)[3] * SZ[shape_of(o[0])[1]] for o, i in pairs)
+        add(q, "dma", pairs, [i for o, i in pairs] + list(after), [o for o, i in pairs], (100.0 * len(pairs), by / 250.0 + 40 * len(pairs)))
+
+    def send(src, dst, wid, back, sem):
+        add("G", "send", (src, dst, wid, back, sem), [src], [ap("loc" + sem)], 500.0)
+        add("R" + sem, "arr", (sem,), [ap("loc" + sem)], [dst], 2500.0)
+
+    def P(b, a=0, n=512, p=128): return ap("ps%d" % b, slice(0, p), slice(a, a + n))
+    def c(b, a, n): return ap(b, a, a + n)
+    def mast(m, i): return c("MS", 144 * list(MN).index(m) + 15 - i, 128)
+    def idm(m): return c("ID", 128 * list(IDN).index(m), 128)
+    def ps(j): return c("PS", j, 1)
+
+    def wrap(m, buf, a, n):
+        return [(mast(m, i), ap(buf, S_, slice(a + i, a + 16 * n, 16))) for i in range(16)]
+
+    pp, nn, hp, hn = idm("p"), idm("n"), idm("h"), idm("nh")
+    eq, mu, ad, su, mx = AL.is_equal, AL.mult, AL.add, AL.subtract, AL.max
+    sh, an = AL.arith_shift_right, AL.bitwise_and
+    dma("S", [(ap("NB"), ap("nb"))])
+    dma("S", [(ap("SN"), ap("snd"))])
+    dma("S", [(c("X", X0[0], V), ap("xv"))])
+    iota(c("PI", 0, 1), [[0, 1]], 0, 1)
+    iota(ap("IT"), [[1, 144]], 0, 0)
+    iota(ap("IG"), [[1, 8], [0, 16]], 0, 0)
+    iota(ap("MM"), [[0, 13], [1, 16]], 0, 0)
+    iota(ap("IS"), [[1, 64], [64, 16]], 0, 0)
+    iota(ap("CX"), [[16, NC]], 0, 1)
+    act(ap("IS"), ap("IS"), AF.Identity, bias=0.5)
+    ms(ap("ZR"), 0.0)
+    ms(c("LT", 0, W), 0.0)
+    p0 = c("PI", 0, 1)
+    for j, (o, s) in enumerate([(sh, 4), (an, 15), (sh, 1), (an, 1), (an, 3), (sh, 2)]): ts(c("PI", j + 1, 1), p0, s, o)
+    ts(c("PI", 7, 1), p0, 15, an, 2, sh)
+    cp(c("PS", 0, 8), ap("PI"))
+    ts(ps(8), ps(1), 16.0, mu)
+    ts(ps(9), ps(5), 2.0, AL.is_lt)
+    ts(ps(10), ps(2), 2.0, eq)
+    ts(ps(11), ps(4), -1.0, mu, 1.0, ad)
+    ts(ps(12), ps(2), 13.0, AL.min)
+    ts(ps(13), ps(6), 4.0, mu, 3.0, ad)
+    ts(ap("G8"), c("IT", 0, 8), ps(1), eq)
+    ts(ap("MT"), c("IT", 0, 16), ps(7), eq, ps(9), mu)
+    act(c("MF", 0, 4), c("MT", 0, 4), AF.Identity, scale=2.0 ** -15)
+    ts(c("MF", 4, 4), c("IT", 0, 4), ps(5), eq)
+    ms(ap("MS"), 0.0)
+    for j, m in enumerate(MN):
+        act(ap("MS", S_, slice(144 * j + 15, 144 * j + 143, 16)), ap("G8"), AF.Identity, scale=ps(10) if m == "FL" else c("MF", MN[m], 1) if m[0] == "L" else MN[m])
+    ts(pp, c("IT", 0, 128), ps(0), eq)
+    for m in list(IDN)[1:]: act(idm(m), pp, AF.Identity, scale=IDN[m])
+    ts(ap("OM"), ap("IT"), ps(13), eq, ps(9), mu)
+    ts(ap("BO"), ap("IG"), ps(1), eq)
+    ts(ap("BN"), c("IT", 0, 128), ps(0), AL.is_lt, -1.0, mu)
+    tt(ap("BN"), ap("BN"), ap("BO"), mu)
+    ts(c("PA", 0, 64), c("IT", 0, 64), ps(3), eq, ps(11), mu)
+    ts(c("PA", 64, 64), c("IT", 0, 64), ps(3), eq, ps(4), mu)
+    for j in range(4): ts(c("PA", 128 + 32 * j, 32), c("IT", 0, 32), ps(6), eq, c("MF", 4 + j, 1), mu)
+    ts(c("DM", 0, 64), c("IT", 0, 64), ps(0), eq)
+    ts(c("DM", 64, 64), c("IT", 1, 64), ps(0), eq, -2.0, mu)
+    ts(c("DM", 128, 64), c("IT", 2, 64), ps(0), eq)
+    tt(c("DM", 0, 64), c("DM", 0, 64), c("DM", 64, 64), ad)
+    tt(c("DM", 0, 64), c("DM", 0, 64), c("DM", 128, 64), ad)
+    act(c("DM", 192, 64), c("DM", 0, 64), AF.Identity, scale=-1.0)
+    ts(ap("M2"), c("IT", 0, 16), ps(12), eq)
+    ts(ap("MM"), ap("MM"), ps(2), eq)
+    ts(ap("CX"), ap("CX"), ps(8), su)
+    ms(ap("ON"), 1.0)
+    for t in range(1, 5): ms(c("CT", 128 * (t - 1), 128), (5 - t) / 8.0)
+    ms(ap("QT"), -0.25)
+    ms(ap("D0"), -1.0)
+    ms(ap("D0", S_, slice(0, 1024, 64)), -128.0)
+    ms(c("X", 0, 16), -64.0)
+    for r in range(2):
+        ms(c("X", X0[r] + W + SL, 16), -64.0)
+        act(c("LT", L0[r] + W, SL), ap("ZR"), AF.Copy)
+    ms(c("Q", V, 16), 1000.0)
+    for b in ("CC", "T2", "T3"): ms(c(b, NC, 16), 8192.0)
+    ms(ap("ZP"), 0.0); ms(ap("ZQ"), 0.0)
+    ms(ap("RC", S_, S_, 64), 0.0)
+    for b in "AB": ms(c("T" + b, 512, 8), 0.0); ms(ap("Z" + b), 0.0)
+    ts(ap("HI"), ap("NB"), M64, ad, M64, su)
+    tt(ap("LO"), ap("NB"), ap("HI"), su)
+    dma("S", [(ap("LT", slice(0, 128, 4), slice(0, W)), ap("HI"))])
+    dma("S", [(ap("LT", slice(1, 128, 4), slice(0, W)), ap("LO"))])
+    dma("S", [(c("Q", 0, V), ap("cq"))], [ap("LO")])
+    dma("S", [(c("LT", LR + V, GH), c("LT", V, GH))] + [(c("D1", 1024 * j, 1024), ap("ZR")) for j in range(4)], [ap("Q")])
+    ts(c("SI", 0, 48), ap("SN"), W - 1, an)
+    ts(c("SI", 48, 48), ap("SN"), 12, sh)
+    cp(ap("SU"), ap("SI"))
+    act(ap("MK"), ind(ap("MT"), c("SU", 48, 48)), AF.Copy)
+    mm(P(4, 0, NC), wrap("C", "X", X0[0], NC))
+    ts(c("LW", 0, NC), P(4, 0, NC), 0.0, AL.is_lt)
+
+    def shown(r):
+        tt(ap("SG"), ind(c("LT", L0[r], V), c("SU", 0, 48)), ap("MK"), mu)
+        w = P(6, 256, 48)
+        mm(w, wrap("C", "SG", 0, 48))
+        off = 16 if r == 0 else GH + SL + 16
+        ts(c("WT", 0, 48), w, float(V), AL.is_ge, -8192.0 if r == 0 else -float(off + V), mu)
+        tt(c("WT", 48, 48), w, c("WT", 0, 48), ad)
+        ts(ap("WU"), c("WT", 48, 48), float(off), ad)
+        cp(c("WI", 0, 48), w)
+
+    def ramps(ro, do, n, k):
+        scan(ap("RR", slice(0, k), slice(ro, ro + n)), ap("D0", slice(0, k), slice(0, n)), ap("D1", slice(0, k), slice(do, do + n)), ad, mx)
+
+    def pair(hi, lo, k): return (ap("RR", slice(0, k), slice(hi, hi + 64)), ap("RR", slice(0, k), slice(lo, lo + 64)))
+    H = slice(0, 64)
+
+    def steps(bank, tb):
+        act(ap("RC", H, S_, H), P(bank, 0, 512, 64), AF.Copy)
+        tt(ap("T" + tb, H, slice(0, 512)), P(bank, 0, 512, 64), ap("RC", H, S_, slice(1, 65)), su)
+        cp(ap("Z" + tb, H, slice(15, 112, 16)), ap("T" + tb, H, slice(64, 512, 64)))
+
+    def cells(tb, e, a, z):
+        return ([(ap("T" + tb, H, slice(e + j, 512 + j, 4)), ap("DM", H, slice(192 * j + a, 192 * j + z))) for j in range(2)]
+                + [(ap("Z" + tb, H, S_), ap("DM", H, slice(a, z)))] * (e == 3))
+
+    def notices(dg):
+        mm(P(2, 256, 64, 96), [(ap("ZQ", S_, dg, slice(48, 144)), c("PA", 0, 64)), (ap("ZQ", S_, dg, slice(0, 96)), c("PA", 64, 64))])
+        cp(ap("D1", slice(0, 96), slice(0, W, 64)), P(2, 256, 64, 96))
+
+    shown(0)
+    for r in range(2):
+        xo, lo = X0[r], L0[r]
+        xw, lw, Lw = c("X", xo, W), c("LT", lo, W), c("LW", NC * r, NC)
+        sw = c("X", 0, 16 + V) if r == 0 else ap("X", X0[0] + V, X0[1] + V)
+        act(ap("S%d" % r), ind(sw, ap("WU")), AF.Copy)
+        send(ap("S%d" % r), c("X", xo + V, GH), 256, False, "ar%d" % (2 * r))
+        ts(c("WI", 48, 48), c("WI", 0, 48), 6, sh)
+        ts(c("WI", 96, 48), c("WI", 0, 48), 15, an)
+        ts(c("WI", 144, 48), c("WI", 0, 48), 4, sh, 3, an)
+        ts(ap("WH"), c("WI", 48, 48), 1.0, ad)
+        ts(c("WI", 96, 48), c("WI", 96, 48), 4.0, mu, 1.0, ad)
+        tt(ap("ZQ", S_, 1, slice(48, 96)), c("WI", 96, 48), c("WI", 144, 48), ad)
+        mm(P(5, 0, NC), [(ap("BO"), Lw)])
+        mm(P(5, 256, NC), [(ap("BN"), Lw)])
+        mm(P(4, 0, NC), [(c("ON", 0, 128), Lw)])
+        scan(c("CC", 0, NC), c("ON", 0, NC), P(5, 0, NC), mu, ad)
+        tt(c("TH", 0, 14), ap("CC", S_, slice(15, 224, 16)), c("M2", 0, 14), mu)
+        red(c("TH", 16, 1), c("TH", 0, 14), True)
+        tt(ap("TM"), c("CC", 0, NC), ap("MM"), mu)
+        scan(c("T2", 0, NC), c("ON", 0, NC), ap("TM"), mu, mx)
+        tt(c("T3", 0, NC), P(5, 256, NC), c("CC", 0, NC), ad)
+        for h in range(2):
+            o, b = 512 * h, 32 * h
+            act(c("I1", o, 512), c("IS", o, 512), AF.Sign, bias=c("TH", 16, 1))
+            mm(P(6, b, 32), wrap("C", "I1", o, 32))
+            ts(c("BU", b, 32), P(6, b, 32), 8.0, mu, 143.0, ad)
+            mm(P(7, 0, 32), wrap("C8", "I1", o, 32), True, False, True)
+            mm(P(3, 0, 32), wrap("C128", "I1", o, 32), True, False, True)
+            tt(c("I2", o, 512), ind(ap("T2"), c("BU", b, 32)), c("IS", o, 512), AL.is_le)
+            mm(P(7, 0, 32), wrap("C", "I2", o, 32), False, True, True)
+            ts(c("BU", 64 + b, 32), P(7, 0, 32), 128.0, ad)
+            mm(P(3, 0, 32), wrap("C16", "I2", o, 32), False, False, True)
+            tt(c("I3", o, 512), ind(ap("T3"), c("BU", 64 + b, 32)), c("IS", o, 512), AL.is_le)
+            mm(P(3, 0, 32), wrap("C", "I3", o, 32), False, True, True)
+            ts(c("BU", 128 + b, 32), P(3, 0, 32), 2048.0, ad)
+            act(c("LH", o, 512), ind(lw, c("BU", 128 + b, 32)), AF.Copy)
+            act(c("QS", o, 512), ind(ap("Q"), c("BU", 128 + b, 32)), AF.Copy)
+        red(c("TH", 17, 1), P(4, 0, NC), False)
+        cp(c("LI", 0, 1), c("TH", 17, 1))
+        ts(c("LI", 1, 1), c("LI", 0, 1), 7, an)
+        lim = c("TH", 18, 1)
+        ts(lim, c("LI", 1, 1), 161.0, ad, 512.0, mu)
+        ts(ap("Z1"), c("T3", 0, NC), SL + 0.5, AL.is_le)
+        tt(ap("Z1"), ap("Z1"), Lw, mu)
+        act(ap("Z2"), c("T3", 0, NC), AF.Identity, bias=W - 1.0)
+        tt(ap("Z2"), ap("Z2"), ap("Z1"), mu)
+        tt(ap("Z1"), ap("Z2"), ap("CX"), mx)
+        cp(ap("UL"), ap("Z1"))
+        rot = [0, 0, 0]
+        mm(P(3, 0, 512, 64), [(c("ZR", 0, 64), c("ZR", 0, 512))], True, False, True)
+        for h in range(2):
+            ho, wo, qs = 2048 * h, 128 * h, c("QS", 512 * h, 512)
+            def z(t, k=0, n=128): return P((t - 1) // 2, 256 * ((t - 1) % 2) + wo + 32 * k, n)
+            def ju(t, k=0, n=128): return c("JU", 256 * (t - 1) + wo + 32 * k, n)
+            def dd(k): return c("DD", ho + 512 * k, 512)
+            def hf(b): return c(b, 512 * h, 512)
+            run = c("RN", wo, 128)
+
+            def hop(t):
+                if t == 1:
+                    for k in range(4): mm(z(1, k, 32), [(pp, c("CT", 0, 32))] + wrap("L%d" % k, "LH", 512 * h, 32))
+                else:
+                    for k in range(4): act(c("LG", ho + 512 * k, 512), ind(lw, ju(t - 1, k, 32)), AF.Identity, scale=c("MF", k, 1))
+                    for k in (0, 2): mm(z(t, k, 64), ([(pp, c("CT", 128 * (t - 1), 64))] if t < 5 else []) + wrap("C", "LG", ho + 512 * k, 64))
+                if t < 5:
+                    for k in (0, 2): ts(ju(t, k, 64), z(t, k, 64), 2.0 ** 15, mu, -4096.0 * (5 - t), ad)
+                if t == 1: act(c("J1", wo, 128), z(1), AF.Identity, bias=-16384.0, scale=2.0 ** 15)
+
+            def visit(t, k):
+                o = c("IN", W * (t % 2) + ho + 512 * k, 512)
+                if (h, t, k) in ABLK:
+                    m = c("MG", 512 * (rot[1] % 4), 512); bk = P(4 + rot[1] % 2); rot[1] += 1
+                    act(m, ind(xw, ju(t, k, 32)), AF.Copy)
+                    mm(bk, [(pp, m), (nn, qs)])
+                    ts(o, bk, M32, ad, M32, eq)
+                else:
+                    d = c("DT", 512 * (rot[0] % 4), 512) if t < 5 else dd(k)
+                    rot[0] += 1
+                    tt(d, ind(xw, ju(t if t < 5 else 6, k, 32)), qs, su)
+                    ts(o, d, M32, ad, M32, eq)
+                if k == 3:
+                    n = P(2, 256 + 128 * (rot[2] % 2), 128); rot[2] += 1
+                    mm(n, wrap("C", "IN", W * (t % 2) + ho, 128))
+                    s = c("SS", 256 * (t % 2) + wo, 128)
+                    act(s, n, AF.Sign, bias=-8.5)
+                    if t == 1: tt(run, z(1), s, ad)
+                    elif t < 5:
+                        tt(z(t), z(t), s, ad)
+                        tt(run, z(t), run, mx)
+                    if t == 4:
+                        tt(run, z(5), run, mx)
+                        ts(c("JI", wo, 128), run, 2.0 ** 15, mu)
+                        ts(c("JF", wo, 128), c("JI", wo, 128), W - 1, an)
+                        cp(ju(6), c("JF", wo, 128))
+
+            hop(1)
+            for t in range(1, 5):
+                hop(t + 1)
+                for k in range(4): visit(t, k)
+            ts(c("JD", 2 * wo, 128), c("JF", wo, 128), 6, sh)
+            ts(c("JD", 2 * wo + 128, 128), c("JF", wo, 128), 15, an)
+            ts(c("JD", 512 + wo, 128), c("JF", wo, 128), 4, sh, 3, an)
+            for j in range(8):
+                ts(c("DG", 2 * wo + 32 * j, 32), c("JD", 2 * wo + 32 * j, 32), 1.0 + 3 * (j // 4), mu, 1.0 + 128 * (3 - j % 4) + 2.0 ** 22, ad)
+            tt(c("DG", 2 * wo + 128, 128), c("DG", 2 * wo + 128, 128), c("JD", 512 + wo, 128), ad)
+            tt(c("DJ", wo, 128), c("JF", wo, 128), c("J1", wo, 128), su)
+            visit(5, 0); visit(5, 1)
+            mm(P(6), [(pp, dd(0)), (nn, dd(1))])
+            act(hf("R1"), P(6), AF.Relu)
+            visit(5, 2)
+            mm(P(7), [(pp, dd(1)), (pp, hf("R1")), (nn, dd(2))])
+            act(hf("R5"), P(7), AF.Relu)
+            mm(P(6), [(pp, hf("R1")), (nn, dd(0)), (pp, dd(2))])
+            act(hf("R6"), P(6), AF.Relu)
+            visit(5, 3)
+            mm(P(7 - 3 * h), [(pp, dd(2)), (pp, hf("R5")), (nn, dd(3))])
+            act(hf("R7"), P(7 - 3 * h), AF.Relu)
+            mm(P(6), [(nn, dd(2)), (pp, hf("R6")), (pp, dd(3))])
+            if h: ts(hf("R8"), P(6), 0.0, mx)
+            else: act(hf("R8"), P(6), AF.Relu)
+            mm(P(7), [(pp, ap("QT")), (hp, dd(0)), (hp, dd(1)), (hp, dd(2))], True, False, True)
+            mm(P(7), [(hn, dd(3))], False, False, True)
+            mm(P(7), [(hn, hf("R7")), (hp, hf("R8"))], False, True, True)
+            ts(hf("YD"), P(7), M1, ad, M1, su)
+            for k in range(4):
+                bk = P(4 + k if h else 6 + k % 2)
+                mm(bk, [(pp, dd(k)), (nn, hf("YD"))])
+                act(c("AB", ho + 512 * k, 512), bk, AF.Abs)
+            D = P(6, 0, 128)
+            mm(D, [(idm("nf"), c("SS", 256 + wo, 128))], True, False, True)
+            for k in (0, 2): mm(P(6, 32 * k, 64), wrap("C512", "AB", ho + 512 * k, 64), False, k == 2, True)
+            for dg in range(2): tt(ap("KY", S_, S_, slice(32 * dg, 32 * dg + 32)), D, c("DG", 2 * wo + 128 * dg, 128), ad)
+            tt(ap("K1"), ap("KY", S_, slice(0, 2), S_), ap("KY", S_, slice(2, 4), S_), mx)
+            tt(ap("K2"), c("K1", 0, 64), c("K1", 64, 64), mx)
+            go = ap("GO", S_, S_, slice(32 * h, 32 * h + 32))
+            ts(ap("KD"), ap("K2"), 127, an)
+            ts(go, ap("K2"), lim, AL.is_lt)
+            ts(ap("NF"), ap("K2"), 2.0 ** 22, AL.is_lt)
+            tt(ap("AC"), ap("NF"), go, su)
+            tt(ap("ZP", S_, S_, slice(96, 128)), ap("KD"), ap("AC"), mu)
+            for dg in range(2):
+                mm(P(7, 32 * dg, 32), [(ap("ZP", S_, dg, slice(96 - 32 * j, 224 - 32 * j)), c("PA", 128 + 32 * j, 32)) for j in range(4)])
+            cp(ap("D1", S_, slice(0, W, 64)), P(7, 0, 64))
+            for q in range(2):
+                ramps(W * h + 1024 * q, 1024 * q, 1024, 128); ramps(W * h + 2048 + 1024 * q, 2048 + 1024 * q, 1024, 128)
+                for gg in range(4 * q, 4 * q + 4):
+                    mm(P(3, 64 * gg, 64, 64), [pair(W * h + 64 * j, W * h + 2048 + 64 * j, 128) for j in range(4 * gg, 4 * gg + 4)], False, h == 1 and gg == 7, True)
+            for j in range(2): tt(c("JS", wo + 64 * j, 64), c("DJ", wo + 64 * j, 64), go, mu)
+            tt(c("JS", wo, 128), c("JS", wo, 128), c("J1", wo, 128), ad)
+            jh, jl = (ap("JW", S_, slice(4 * j, 4 * j + 4), slice(32 * h, 32 * h + 32)) for j in range(2))
+            ts(jh, c("JS", wo, 128), M64, ad, M64, su)
+            tt(jl, c("JS", wo, 128), jh, su)
+        steps(3, "A")
+        for e in range(4): mm(P(2, 12 * e, 12), cells("A", e, 52, 64))
+        for e in range(4): ts(ap("G%d" % r, S_, slice(e, 48, 4)), P(2, 12 * e, 12), 0.5, AL.is_gt)
+        send(ap("G%d" % r), ap("N%d" % r), 16, True, "ar%d" % (2 * r + 1))
+        mm(P(0, 0, 256), [(c("ZR", 0, 128), c("ZR", 0, 256))], True, False, True)
+        for e in range(4): mm(P(0, 64 * e, 52), cells("A", e, 0, 52), False, False, True)
+        notices(1)
+        for q in range(4): ramps(1024 * q, 1024 * q, 1024, 96)
+        jrow = lambda j: ap("LT", slice(j, 128, 16), slice(lo + W, lo + LR))
+        dma("S", [(jrow(2), ap("GO", S_, 0, S_))] + [(jrow(4 * (j % 4) + j // 4), ap("JW", S_, j, S_)) for j in range(8)])
+        ln = L0[1 - r]
+        for h in range(2):
+            for i in range(8 * h, 8 * h + 8):
+                mm(P(4 + h, 64 * (i % 8), 64), [(pp, ap("YD", S_, slice(i, SL, 16))), (pp, ap("QS", S_, slice(i, SL, 16)))])
+            act(c("X", xo + W + 512 * h, 512), P(4 + h), AF.Copy)
+        for h in range(2):
+            a = 104 * h
+            act(c("LT", ln + 16 * a, 1664), ind(c("LT", lo, LR), c("UL", a, 104)), AF.Copy)
+            mm(P(6 + h, 0, 104), wrap("FL", "LT", ln + 16 * a, 104))
+            tt(c("Z3", a, 104), P(6 + h, 0, 104), c("Z2", a, 104), mu)
+            if r == 0: tt(c("NL", a, 104), P(6 + h, 0, 104), c("LW", a, 104), AL.is_lt)
+        tt(ap("Z3"), ap("Z3"), ap("CX"), mx)
+        tt(ap("ZQ", S_, 0, slice(48, 96)), ap("N%d" % r), ap("WH"), mu)
+        notices(0)
+        for q in range(4):
+            ramps(W + 1024 * q, 1024 * q, 1024, 96)
+            for gg in (2 * q, 2 * q + 1): mm(P(1, 64 * gg, 64, 64), [pair(W + 64 * j, 64 * j, 96) for j in range(8 * gg, 8 * gg + 8)])
+        if r == 0: shown(1)
+        else:
+            for h in range(2):
+                mm(P(4 + h, 0, 416), [(c("OM", 3 - e, 128), c("LT", ln + 832 * e + 416 * h, 416)) for e in range(4)])
+                act(c("YN", 416 * h, 416), P(4 + h, 0, 416), AF.Copy)
+            dma("S", [(ap("yn"), ap("YN"))])
+        steps(1, "B")
+        for e in range(4): mm(P(0, 64 * e, 52), cells("B", e, 0, 52), False, e == 3, True)
+        for e in range(4): ts(ap("FA", S_, slice(e, NC, 4)), P(0, 64 * e, 52), 0.5, AL.is_gt, float(W + SL), mu)
+        if r == 0:
+            ts(ap("F1"), ap("FA"), 1.0, AL.min)
+            tt(c("LW", NC, NC), ap("F1"), ap("NL"), mx)
+        tt(ap("Z3"), ap("Z3"), ap("FA"), mx)
+        cp(ap("UX"), ap("Z3"))
+        xn = X0[1 - r]
+        cuts = [0, 16, NC] if r == 0 else [0, 60, 120, 164, NC]
+        for j in range(len(cuts) - 1):
+            a, n = cuts[j], cuts[j + 1] - cuts[j]
+            o, x = c("X", xn + 16 * a, 16 * n), ind(c("X", xo, XR), c("UX", a, n))
+            if j % 2: act(o, x, AF.Copy)
+            else: cp(o, x)
+            if r == 1: dma("S", [(c("yx", 16 * a, 16 * n), o)])
+    return ops
+
+
+def order(ops):
+    n = len(ops)
+    last = {}
+    for i, o in enumerate(ops):
+        dep = set()
+        for (nm, pm), m in o["r"].items():
+            dep.update(x[0] for x in last.get(nm, []) if x[3] and x[1] & m and x[2] & pm)
+        for (nm, pm), m in o["w"].items():
+            dep.update(x[0] for x in last.get(nm, []) if x[1] & m and x[2] & pm)
+            last[nm] = [x for x in last.get(nm, []) if x[1] & ~m or x[2] & ~pm]
+        for w, key in ((False, "r"), (True, "w")):
+            for (nm, pm), m in o[key].items(): last.setdefault(nm, []).append((i, m, pm, w))
+        dep.discard(i)
+        o["d"] = dep
+        o["b"] = {x[0] for x in list(o["r"]) + list(o["w"]) if x[0][:2] == "ps"}
+    succ = [[] for _ in ops]
+    for i, o in enumerate(ops):
+        for j in o["d"]: succ[j].append(i)
+    full = [(o["c"][0] + o["c"][1] + 1800.0) if o["k"] == "dma" else o["c"] for o in ops]
+    best, x = None, 12345
+    base = [0.0] * n
+    for i in range(n - 1, -1, -1): base[i] = full[i] + max([base[j] + LAT for j in succ[i]], default=0.0)
+    for it in range(TRIES):
+        pr = list(best[3]) if best else base
+        for _k in range(NPERT if it else 0):
+            x = (x * 1103515245 + 12345) % 2 ** 31
+            j = (x >> 8) % n
+            x = (x * 1103515245 + 12345) % 2 ** 31
+            pr[j] += AMP * (x / 2 ** 30 - 1)
+        left = [len(o["d"]) for o in ops]
+        ready = {i: 0.0 for i in range(n) if left[i] == 0}
+        free, bank, fin, sq, tm, pipe = {}, {}, [0.0] * n, [], {}, 0.0
+        while ready:
+            est = {}
+            for i, s in ready.items():
+                o = ops[i]
+                s = max(s, free.get(o["e"], 0.0))
+                for b in o["b"]:
+                    for e, y in bank.get(b, {}).items():
+                        if e != o["e"]: s = max(s, y + LAT)
+                est[i] = s
+            i0 = min(est, key=lambda i: (est[i], -pr[i]))
+            e0 = ops[i0]["e"]
+            i = max((i for i in est if ops[i]["e"] == e0 and est[i] <= est[i0] + min(LOOK, full[i0])), key=lambda i: (pr[i], -i))
+            o = ops[i]; s = est[i]
+            if o["k"] == "dma":
+                free[e0] = s + o["c"][0]
+                pipe = fin[i] = max(pipe, s + o["c"][0] + 1800.0) + o["c"][1]
+            else: free[e0] = fin[i] = s + o["c"]
+            tm[i] = (s, fin[i])
+            for b in o["b"]: bank.setdefault(b, {})[e0] = fin[i]
+            sq.append(i); del ready[i]
+            for j in succ[i]:
+                left[j] -= 1
+                if left[j] == 0: ready[j] = max(fin[y] + (0.0 if ops[y]["e"] == ops[j]["e"] == "T" else LAT) for y in ops[j]["d"])
+        if best is None or max(fin) <= best[0]: best = (max(fin), sq, tm, pr)
+    seq = best[1]
+    pos, cnt, clock, known, user, nd = {}, {}, {}, {}, {}, 0
+    for i in seq:
+        o = ops[i]; e = o["e"]; o["t"] = best[2][i]
+        if o["k"] == "dma": o["src"] = "d%d" % nd; nd += 1
+        else: o["src"] = o["a"][0] if o["k"] == "arr" else "e" + e
+        dep = set(o["d"])
+        for b in o["b"]:
+            dep |= {j for e2, j in user.get(b, {}).items() if e2 != e}
+            user.setdefault(b, {})[e] = i
+        kn = known.setdefault(e, {})
+        o["wait"] = []
+        if o["k"] != "arr":
+            for j in sorted(dep, key=lambda j: -pos[j]):
+                p = ops[j]
+                if p["e"] == e == "T" or kn.get(p["src"], -1) >= pos[j]: continue
+                o["wait"].append(j); p["inc"] = True
+                for k, v in clock[j].items(): kn[k] = max(kn.get(k, -1), v)
+        pos[i] = len(pos)
+        clock[i] = dict(kn)
+        clock[i][o["src"]] = pos[i]
+    for i in seq:
+        o = ops[i]
+        if o["k"] == "dma": o["val"] = 16 * len(o["a"])
+        elif o.get("inc") and o["k"] != "arr":
+            cnt[o["src"]] = o["val"] = cnt.get(o["src"], 0) + 1
+    return seq
+
+
+PLAN = {}
+
+
+def rank_program(g, core, T, topo):
+    rank = T.rank_of(core)
+    if rank is None:
+        return
+    if not PLAN:
+        PLAN["ops"] = build(); PLAN["seq"] = order(PLAN["ops"])
+    ops, seq = PLAN["ops"], PLAN["seq"]
+    n = len(T.cores)
+    Q = {"V": g.vector, "A": g.scalar, "T": g.tensor, "G": g, "S": g.sync}
+    peers = [c for c in T.cores if c != core]
+    turn = sorted(peers, key=lambda c: topo.die(c) == topo.die(core))
+    mask = {c: sum(1 << e for e in topo.engines(core, c)[j::4]) for c, j in zip(turn, (0, 2, 1))}
+    arrive = sum(len(topo.engines(c, core)) // 4 for c in peers)
+    leave = sum(bin(m).count("1") for m in mask.values())
+    sent = 0
+    waited = set()
+    for i in seq:
+        o = ops[i]; k = o["k"]; a = o["a"]
+        if k == "arr": continue
+        q = Q[o["e"]]
+        for j in o["wait"]:
+            p = ops[j]
+            q.wait_ge(T.sem[p["src"]], arrive if p["k"] == "arr" else p["val"]); waited.add(j)
+        x = [real(T, y) for y in a] if k not in ("mm", "dma", "send") else None
+        if k == "ts": r = q.tensor_scalar(*(x[:5] if x[5] is None else x))
+        elif k == "tt": r = q.tensor_tensor(*x)
+        elif k == "cp": r = q.tensor_copy(*x)
+        elif k == "ms": r = q.memset(*x)
+        elif k == "scan": r = q.tensor_tensor_scan(x[0], x[1], x[2], 0.0, x[3], x[4])
+        elif k == "red": r = q.tensor_reduce(x[0], x[1], AX.X, AL.add, negate=x[2])
+        elif k == "act": r = q.activation(*x[:3]) if x[2] == AF.Copy else q.activation(*x[:3], bias=x[3], scale=x[4])
+        elif k == "iota": r = g.iota(*x) if a[0][0] == "PI" else g.iota(*x, allow_small_or_imprecise_dtypes=True)
+        elif k == "mm":
+            for m, (l, rr) in enumerate(a[1]):
+                r = q.matmul(real(T, a[0]), real(T, l), real(T, rr), a[2] and m == 0, a[3] and m == len(a[1]) - 1)
+        elif k == "dma":
+            for oo, ii in a: q.dma_start(real(T, oo), real(T, ii)).then_inc(T.sem[o["src"]], 16)
+            continue
+        else:
+            src, dst, wid, back, sem = a
+            tr = []
+            for d in range(1, n):
+                c = T.cores[(rank - d if back else rank + d) % n]
+                rid, pid, _se = topo.addr(c)
+                s0, d0 = extent(src)[4] + wid * (d - 1), extent(dst)[4] + wid * (d - 1)
+                tr.append(RemoteDMATransfer(dst_ids=[DstId(rid=rid, pnc=pid)], dma_engine_mask=mask[c], remote_sem=T.sem[sem],
+                                            src=T[src[0]][:, s0:s0 + wid], dst=T[dst[0]][:, d0:d0 + wid]))
+            g.remote_dma_fused(tr, local_sem=T.sem.loc); sent += leave
+            continue
+        if o.get("inc"): r.then_inc(T.sem[o["src"]], 1)
+    g.wait_ge(T.sem.loc, sent)
+    for i in seq:
+        if ops[i]["k"] == "dma" and i not in waited: g.wait_ge(T.sem[ops[i]["src"]], ops[i]["val"])

@@ -2,34 +2,40 @@ from concourse.bass import DstId, RemoteDMATransfer
 from concourse.mybir import AluOpType as AL, AxisListType as AX, ActivationFunctionType as AF
 
 V, W, SL, GH = 3328, 4096, 1024, 768
-NC = V // 16
-XR = W + SL + 16
-X0 = [16, 16 + XR]
-LR = W + SL
-L0 = [0, LR]
+HV, NC, HC, HS = V // 2, V // 16, V // 32, SL // 2
+NEW = 3 * HS
+XN, LN = W + NEW + 16, W + NEW
+X0 = [16, 16 + XN, 16 + 2 * XN]
+L0 = [0, LN, 2 * LN]
 M32, M64, M1 = 1.5 * 2 ** 28, 1.5 * 2 ** 29, 1.5 * 2 ** 23
-ABLK = [(0, 2, 3), (0, 3, 3), (0, 4, 3), (1, 2, 3), (1, 3, 3), (1, 4, 3)]
+ABLK = [[(4, 3)], [(3, 3), (4, 3)], [(3, 3), (4, 3)], [(2, 3), (3, 3), (4, 3), (4, 2)]]
+FIN = ["AAAA", "AAAA", "AAAA", "AVAV"]
+RND = "VVVV"
+XUP = [[("A", 104)], [("A", 104)], [("A", 104)], [("V", 52), ("A", 52)]]
 B, F, I, U = "bfloat16", "float32", "int32", "uint16"
-MN = {"C": 1.0, "C8": 8.0, "C16": 16.0, "C128": 128.0, "C512": 512.0, "L0": 0, "L1": 1, "L2": 2, "L3": 3, "FL": 0}
-IDN = {"p": 1.0, "n": -1.0, "h": 0.5, "nh": -0.5, "nf": -2.0 ** 22}
-SB = {"X": ([16 + 2 * XR], B), "LT": ([2 * LR], B), "Q": ([V + 16], B), "MS": ([144 * len(MN)], B), "ID": ([128 * len(IDN)], B),
-      "KY": ([4, 64], F), "GO": ([2, 64], B), "ZP": ([2, 224], B), "ZQ": ([2, 144], B), "JW": ([8, 64], B), "RC": ([8, 65], F)}
-for _d, _s in ((B, "HI1024 LO1024 ZR1024 MK768 SG768 MT16 OM144 BO128 BN128 PA256 ON256 CT512 QT512 D01024 D14096 RR8192 LW416 I11024 I21024 "
-                   "I31024 QS1024 NL208 F1208 WH48 S0768 S1768 G048 G148 N048 N148 LH1024 LG4096 DT2048 MG2048 IN8192 DD4096 SS512 R11024 "
-                   "R51024 R61024 R71024 R81024 YD1024 AB4096 NF64 AC64"),
-               (F, "IT144 IG128 PS16 IS1024 CX208 MM208 G88 MF16 DM256 M216 CC224 T2224 TM208 T3224 TH32 Z1208 Z2208 Z3208 FA208 WT96 RN256 "
-                   "J1256 DG512 K1128 DJ256 JS256 YN832 TA520 TB520 ZA128 ZB128"),
-               (I, "NB1024 SN48 SI96 PI8 LI8 WI192 JI256 JF256 JD768 K264 KD64"), (U, "SU96 BU192 UL208 UX208 WU48 JU1536")):
+MN = {"C": 1.0, "C2": 1.0, "C512": 512.0, "L0": 0, "L1": 1, "L2": 2, "L3": 3, "FL": 10, "H0": 24, "H1": 7}
+IDN = {"p": 1.0, "n": -1.0, "h": 0.5, "nh": -0.5, "s1": 16384.0, "s2": 12288.0, "s3": 8192.0, "s4": 4096.0, "nf": 2.0 ** 23, "x16": 16.0, "m1": -4.0 * M1}
+SB = {"X": ([X0[2] + XN], B), "LT": ([3 * LN], B), "Q": ([2 * (V + 16)], B), "MS": ([144 * len(MN)], B), "ID": ([128 * len(IDN)], B),
+      "KY": ([4, 64], F), "GO": ([2, 32], B), "ZP": ([2, 224], B), "ZQ": ([4, 144], B), "JW": ([8, 32], B), "RC": ([4, 65], F)}
+for _d, _s in ((B, "HI512 LO512 ZR1024 MK1536 SG768 MT16 OM144 BO512 BN128 PA192 ON256 KC128 QT512 D01024 D14096 D21664 RR4096 RL2048 "
+                   "RH1664 LW416 I1512 I2512 I3512 QS1024 LH512 WH96 S0768 S1768 S2768 S3768 G048 G148 G248 G348 N048 N148 N248 N348 LG4096 "
+                   "DT2048 MG1024 IN6144 DD2048 SS384 R1512 R2512 R3512 R4512 YY512 AB2048 XS2464 LS1664 G88 G98 HH128 BB64 NF64 AC64"),
+               (F, "IT144 IG128 II128 IF128 PS32 IS512 CX104 MM208 MF8 DM192 M216 CC224 T2224 TM208 T3224 TH32 Z1104 ZY104 Z2208 Z3104 NL104 TR104 "
+                   "WT144 RN128 ZS1024 K1128 DJ128 JS128 YN416 TA264 ZA64"),
+               (I, "NB512 SN96 SI144 PI8 LI8 WI144 JI128 JF128 JD256 K264 KD64"), (U, "SU288 BU96 UL208 UX104 WU48 JU1280")):
     for _x in _s.split(): SB[_x[:2]] = ([int(_x[2:])], _d)
 SB = {k: ([128] + v[0], v[1]) for k, v in SB.items()}
 SCRATCH = {k: ("sbuf", v[0], v[1]) for k, v in SB.items()}
 for _b in range(8):
     SCRATCH["ps%d" % _b] = ("psum", [128, 512], F)
 EXT = {"xv": ([128, V], B), "cq": ([128, V], B), "nb": ([8, 4 * W], I), "snd": ([128, 48], I), "yx": ([128, V], B), "yn": ([8, 4 * V], F)}
-SEMAPHORES = ["eV", "eA", "eT", "eG", "loc", "ar0", "ar1", "ar2", "ar3"] + ["d%d" % _i for _i in range(30)]
+SEMAPHORES = ["eV", "eA", "eT", "eG", "loc"] + ["ar%d" % _i for _i in range(8)] + ["d%d" % _i for _i in range(60)]
 SZ = {B: 2, F: 4, I: 4, U: 2}
 S_ = slice(None)
-CY, GA, PE, LAT, LOOK, TRIES, NPERT, AMP = 1.04, 1.56, 0.5, 120.0, 150.0, 1500, 10, 15000.0
+HP = [slice(0, 64), slice(64, 128)]
+FIGS = [(0.95, 1.56, 150.0), (0.85, 1.2, 150.0), (1.15, 1.9, 150.0)]
+DLAT, RLAT, LOOK, TRIES, NPERT, RUN, AMP, SEED = 1500.0, 2200.0, 100.0, 1500, 4, 12, 3000.0, 12345
+SHIFT = {"tail0": -20, "tail1": -20, "tail2": -10, "visits0": -20}
 
 
 def shape_of(n):
@@ -67,375 +73,441 @@ def real(T, a):
     return x.indirect(real(T, a[2])) if a[2] else x
 
 
-def build():
-    ops = []
+def price(o, cy, ga):
+    c = o["c"]
+    return c[0] + cy * (c[1] + ga * c[2])
 
-    def add(eng, kind, args, rd, wr, cost, whole=False):
+
+def build():
+    ops, stage = [], ["load0"]
+
+    def add(eng, kind, args, rd, wr, cost, sums=None):
         R, Wr = {}, {}
         for lst, out in ((rd, R), (wr, Wr)):
             for a in lst:
                 if not isinstance(a, tuple): continue
                 for b, o in ((a, out), (a[2], R)):
                     if b:
-                        e = extent(ap(b[0]) if whole and b[0] not in SB else b)
+                        e = extent(b)
                         o[(b[0], e[1])] = o.get((b[0], e[1]), 0) | e[0]
-        ops.append({"e": eng, "k": kind, "a": args, "r": R, "w": Wr, "c": cost})
+        ops.append({"e": eng, "k": kind, "a": args, "r": R, "w": Wr, "c": cost, "s": sums, "g": stage[0]})
 
     def vc(out, *x):
         n = nel(x[0]) if x else nel(out)
-        if x and x[0][2]: return 60 + n * GA * CY
-        return max(64, n * (0.5 if all(SZ[shape_of(a[0])[1]] == 2 for a in (out,) + x) else 1)) * CY
+        if x and x[0][2]: return (55.0, 0, n)
+        return (0.0, max(64, n * (0.5 if all(SZ[shape_of(a[0])[1]] == 2 for a in (out,) + x) else 1)), 0)
 
     def ts(out, x, s1, o0, s2=None, o1=None): add("V", "ts", (out, x, s1, s2, o0, o1), [x, s1, s2], [out], vc(out, x))
     def cp(out, x): add("V", "cp", (out, x), [x], [out], vc(out, x))
     def ms(out, c): add("V", "ms", (out, c), [], [out], vc(out))
     def scan(out, a, b, o0, o1): add("V", "scan", (out, a, b, o0, o1), [a, b], [out], vc(out, a, b))
-    def red(out, x, neg): add("V", "red", (out, x, neg), [x], [out], max(64, nel(x)) * CY)
-    def iota(out, pat, base, cm): add("G", "iota", (out, pat, base, cm), [], [out], 130 + 2 * nel(out) * CY)
+    def red(out, x, neg): add("V", "red", (out, x, neg), [x], [out], (0.0, max(64, nel(x)), 0))
+    def iota(out, pat, base, cm): add("G", "iota", (out, pat, base, cm), [], [out], (130.0, 2 * nel(out), 0))
 
     def tt(out, x, y, o):
-        add("V", "tt", (out, x, y, o), [x, y], [out], vc(out, x) if x[2] else max(64, nel(x) * (2 if x[0] in SB and y[0] in SB else 1)) * CY)
+        add("V", "tt", (out, x, y, o), [x, y], [out], vc(out, x) if x[2] else (0.0, max(64, nel(x) * (2 if x[0] in SB and y[0] in SB else 1)), 0))
 
     def act(out, x, fn, bias=0.0, scale=1.0):
-        add("A", "act", (out, x, fn, bias, scale), [x, bias, scale], [out], 20 + vc(out, x) if x[2] else max(64, nel(x)) * CY)
+        add("A", "act", (out, x, fn, bias, scale), [x, bias, scale], [out], (70.0, 0, nel(x)) if x[2] else (0.0, max(64, nel(x)), 0))
 
-    def mm(out, terms, start=True, stop=True, whole=False):
-        c = sum(max(min(64, nel(l)), nel(r)) * (4 if shape_of(l[0])[1] == F else 1) for l, r in terms) * PE
-        add("T", "mm", (out, terms, start, stop), [x for t in terms for x in t] + ([] if start else [out]), [out], c, whole)
+    def pc(l, r): return 0.5 * max(min(64, nel(l)), nel(r)) * (4 if shape_of(l[0])[1] == F else 1)
 
-    def dma(q, pairs, after=()):
+    def mm(out, terms, start=True, more=False):
+        add("T", "mm", (out, terms, start, True), [x for t in terms for x in t] + ([] if start else [out]), [out],
+            (0.0, sum(pc(l, r) for l, r in terms), 0), "open" if start and more else "new" if start else "add")
+
+    def mms(trip):
+        add("T", "mms", (trip,), [x for t in trip for x in t[1:]], [t[0] for t in trip], (0.0, sum(pc(l, r) for o, l, r in trip), 0), "new")
+
+    def dma(pairs, after=()):
         by = sum(extent(o)[2] * extent(o)[3] * SZ[shape_of(o[0])[1]] for o, i in pairs)
-        add(q, "dma", pairs, [i for o, i in pairs] + list(after), [o for o, i in pairs], (100.0 * len(pairs), by / 250.0 + 40 * len(pairs)))
+        rows = sum(max(extent(o)[3], extent(i)[3]) for o, i in pairs)
+        add("S", "dma", pairs, [i for o, i in pairs] + list(after), [o for o, i in pairs], (60.0 * len(pairs), 0, 0, by / 350.0 + 3.0 * rows))
 
-    def send(src, dst, wid, back, sem):
-        add("G", "send", (src, dst, wid, back, sem), [src], [ap("loc" + sem)], 500.0)
-        add("R" + sem, "arr", (sem,), [ap("loc" + sem)], [dst], 2500.0)
+    def send(src, dst, wid, back, sem, frees=()):
+        add("G", "send", (src, dst, wid, back, sem), [src], [ap("loc" + sem)] + list(frees), (500.0, 0, 0))
+        add("R" + sem, "arr", (sem,), [ap("loc" + sem)], [dst], (RLAT, 0, 0))
 
-    def P(b, a=0, n=512, p=128): return ap("ps%d" % b, slice(0, p), slice(a, a + n))
-    def c(b, a, n): return ap(b, a, a + n)
-    def mast(m, i): return c("MS", 144 * list(MN).index(m) + 15 - i, 128)
+    def fill(b, a, n):
+        for j in range(a, a + n, 512): iota(c(b, j, min(512, a + n - j)), [[0, min(512, a + n - j)]], 0, 0)
+
+    def P(b, a=0, n=512, p=S_, step=1): return ap("ps%d" % b, p, slice(a, a + n * step - step + 1, step))
+    def c(b, a, n, p=S_): return ap(b, p, slice(a, a + n))
+    def mast(m, i, p=S_): return c("MS", 144 * list(MN).index(m) + 15 - i, 128, p)
     def idm(m): return c("ID", 128 * list(IDN).index(m), 128)
-    def ps(j): return c("PS", j, 1)
+    def ps(j, p=S_): return c("PS", j, 1, p)
 
-    def wrap(m, buf, a, n):
-        return [(mast(m, i), ap(buf, S_, slice(a + i, a + 16 * n, 16))) for i in range(16)]
+    def wrap(m, buf, a, n, p=S_):
+        return [(mast(m, i, p), ap(buf, p, slice(a + i, a + 16 * n, 16))) for i in range(16)]
 
     pp, nn, hp, hn = idm("p"), idm("n"), idm("h"), idm("nh")
     eq, mu, ad, su, mx = AL.is_equal, AL.mult, AL.add, AL.subtract, AL.max
     sh, an = AL.arith_shift_right, AL.bitwise_and
-    dma("S", [(ap("NB"), ap("nb"))])
-    dma("S", [(ap("SN"), ap("snd"))])
-    dma("S", [(c("X", X0[0], V), ap("xv"))])
+    H64, H96 = slice(0, 64), slice(0, 96)
+
+    def load(s):
+        rows = slice(64 * s, 64 * s + 64)
+        dma([(ap("NB"), ap("nb", slice(4 * s, 4 * s + 4), S_))])
+        dma([(c("X", X0[s], V, HP[h]), ap("xv", rows, S_)) for h in range(2)])
+        dma([(c("SN", 48 * s, 48, HP[h]), ap("snd", rows, S_)) for h in range(2)])
+        if s: fill("LT", L0[s], W)
+        else:
+            for j in range(4): act(c("LT", L0[s] + 1024 * j, 1024), ap("ZR"), AF.Copy)
+        ts(ap("HI"), ap("NB"), M64, ad, M64, su)
+        tt(ap("LO"), ap("NB"), ap("HI"), su)
+        for j, b in enumerate(("HI", "LO")):
+            dma([(ap("LT", slice(64 * h + j, 64 * h + 64, 4), slice(L0[s], L0[s] + W)), ap(b)) for h in range(2)])
+        dma([(c("Q", (V + 16) * s, V, HP[h]), ap("cq", rows, S_)) for h in range(2)], [ap("LO")])
+        ts(c("SI", 0, 48), c("SN", 48 * s, 48), W - 1, an)
+        ts(c("SI", 48, 48), c("SN", 48 * s, 48), 12, sh)
+        ts(c("SI", 96, 48), c("SI", 0, 48), float(HV), AL.is_ge, 4.0, mu)
+        tt(c("SI", 48, 48), c("SI", 48, 48), c("SI", 96, 48), ad)
+        cp(c("SU", 144 * s, 96), c("SI", 0, 96))
+        ts(c("SU", 144 * s + 96, 48), c("SI", 0, 48), ps(20), ad, HV - 1.0, AL.min)
+        act(c("MK", GH * s, GH), ind(ap("MT"), c("SU", 144 * s + 48, 48)), AF.Copy)
+        mm(P(6 + s, 0, HC), wrap("H0", "X", X0[s], HC) + wrap("H1", "X", X0[s] + HV, HC))
+        ts(c("LW", HC * s, HC), P(6 + s, 0, HC), 0.0, AL.is_lt)
+
     iota(c("PI", 0, 1), [[0, 1]], 0, 1)
     iota(ap("IT"), [[1, 144]], 0, 0)
-    iota(ap("IG"), [[1, 8], [0, 16]], 0, 0)
+    iota(ap("IG"), [[0, 2], [1, 4], [0, 16]], 0, 0)
+    iota(ap("II"), [[0, 8], [1, 16]], 0, 0)
     iota(ap("MM"), [[0, 13], [1, 16]], 0, 0)
-    iota(ap("IS"), [[1, 64], [64, 16]], 0, 0)
-    iota(ap("CX"), [[16, NC]], 0, 1)
-    act(ap("IS"), ap("IS"), AF.Identity, bias=0.5)
+    iota(ap("IS"), [[1, 32], [32, 16]], 0, 0)
+    iota(ap("KC"), [[-128, 4], [0, 32]], 384, 0)
+    iota(ap("CX"), [[16, HC]], 0, 1)
     ms(ap("ZR"), 0.0)
-    ms(c("LT", 0, W), 0.0)
     p0 = c("PI", 0, 1)
-    for j, (o, s) in enumerate([(sh, 4), (an, 15), (sh, 1), (an, 1), (an, 3), (sh, 2)]): ts(c("PI", j + 1, 1), p0, s, o)
-    ts(c("PI", 7, 1), p0, 15, an, 2, sh)
+    for j, (o, s) in enumerate([(sh, 4), (an, 15), (sh, 1), (an, 1), (an, 3), (sh, 2), (sh, 6)]): ts(c("PI", j + 1, 1), p0, s, o)
     cp(c("PS", 0, 8), ap("PI"))
-    ts(ps(8), ps(1), 16.0, mu)
+    ts(ps(8), ps(7), -4.0, mu, ps(1), ad)
     ts(ps(9), ps(5), 2.0, AL.is_lt)
     ts(ps(10), ps(2), 2.0, eq)
     ts(ps(11), ps(4), -1.0, mu, 1.0, ad)
     ts(ps(12), ps(2), 13.0, AL.min)
-    ts(ps(13), ps(6), 4.0, mu, 3.0, ad)
+    ts(ps(13), ps(1), -4.0, mu, ps(6), ad)
+    ts(ps(14), ps(7), -float(HS), mu, W + HS - 1.0, ad)
+    ts(ps(15), ps(1), -16.0, mu)
+    ts(ps(16), ps(7), float(HV), mu, ps(15), ad)
+    ts(ps(17), ps(6), 8.0, mu, 3.0, ad)
+    ts(ps(18), ps(7), -124.0, mu, ps(17), ad)
+    ts(ps(19), ps(7), float(HS), mu)
+    act(ap("IS"), ap("IS"), AF.Identity, bias=ps(19))
+    ts(ps(20), ps(7), -float(HV), mu)
+    ts(ps(21), ps(7), 4.0, mu, ps(13), ad)
+    ts(ps(22), ps(7), 8192.0, mu, float(HV), ad)
+    ts(ps(23), ps(20), 16.0, ad)
+    ts(ps(24), ps(7), 0.0, eq)
     ts(ap("G8"), c("IT", 0, 8), ps(1), eq)
-    ts(ap("MT"), c("IT", 0, 16), ps(7), eq, ps(9), mu)
-    act(c("MF", 0, 4), c("MT", 0, 4), AF.Identity, scale=2.0 ** -15)
+    ts(ap("G9"), ap("IG", S_, slice(0, 128, 16)), ps(8), eq)
+    ts(ap("MT"), c("IT", 0, 16), ps(21), eq, ps(9), mu)
+    ts(c("MF", 0, 4), c("IT", 0, 4), ps(13), eq, ps(9), mu)
     ts(c("MF", 4, 4), c("IT", 0, 4), ps(5), eq)
     ms(ap("MS"), 0.0)
     for j, m in enumerate(MN):
-        act(ap("MS", S_, slice(144 * j + 15, 144 * j + 143, 16)), ap("G8"), AF.Identity, scale=ps(10) if m == "FL" else c("MF", MN[m], 1) if m[0] == "L" else MN[m])
+        act(ap("MS", S_, slice(144 * j + 15, 144 * j + 143, 16)), ap("G9" if m == "C2" else "G8"), AF.Identity,
+            scale=ps(MN[m]) if m[0] in "FH" else c("MF", MN[m], 1) if m[0] == "L" else MN[m])
+    ts(c("HH", 0, 64), c("IT", 0, 64), ps(0), eq)
+    ts(c("HH", 64, 64), c("IT", 64, 64), ps(0), eq)
+    tt(c("HH", 0, 64), c("HH", 0, 64), c("HH", 64, 64), ad)
+    cp(c("HH", 64, 64), c("HH", 0, 64))
     ts(pp, c("IT", 0, 128), ps(0), eq)
-    for m in list(IDN)[1:]: act(idm(m), pp, AF.Identity, scale=IDN[m])
-    ts(ap("OM"), ap("IT"), ps(13), eq, ps(9), mu)
-    ts(ap("BO"), ap("IG"), ps(1), eq)
-    ts(ap("BN"), c("IT", 0, 128), ps(0), AL.is_lt, -1.0, mu)
-    tt(ap("BN"), ap("BN"), ap("BO"), mu)
-    ts(c("PA", 0, 64), c("IT", 0, 64), ps(3), eq, ps(11), mu)
-    ts(c("PA", 64, 64), c("IT", 0, 64), ps(3), eq, ps(4), mu)
-    for j in range(4): ts(c("PA", 128 + 32 * j, 32), c("IT", 0, 32), ps(6), eq, c("MF", 4 + j, 1), mu)
-    ts(c("DM", 0, 64), c("IT", 0, 64), ps(0), eq)
-    ts(c("DM", 64, 64), c("IT", 1, 64), ps(0), eq, -2.0, mu)
-    ts(c("DM", 128, 64), c("IT", 2, 64), ps(0), eq)
+    for m in list(IDN)[1:]:
+        if m != "m1" or "A" in RND: act(idm(m), pp, AF.Identity, scale=IDN[m])
+    act(ap("IF"), pp, AF.Copy)
+    ts(ap("OM"), ap("IT"), ps(18), eq, ps(9), mu)
+    ts(ap("BN"), ap("II"), ps(2), AL.is_lt, -1.0, mu)
+    for h in range(2):
+        ts(c("BO", 128 * h, 128), ap("IG"), ps(8), eq, ps(7 if h else 24), mu)
+        tt(c("BO", 256 + 128 * h, 128), c("BO", 128 * h, 128), ap("BN"), mu)
+    ts(c("PA", 0, 32), c("IT", 0, 32), ps(3), eq, ps(11), mu)
+    ts(c("PA", 32, 32), c("IT", 0, 32), ps(3), eq, ps(4), mu)
+    for j in range(4): ts(c("PA", 64 + 32 * j, 32), c("IT", 0, 32), ps(6), eq, c("MF", 4 + j, 1), mu)
+    ts(c("DM", 0, 64), c("IT", 0, 64), ps(0), eq, 8192.0, mu)
+    ts(c("DM", 64, 64), c("IT", 1, 64), ps(0), eq, -16384.0, mu)
+    ts(c("DM", 128, 64), c("IT", 2, 64), ps(0), eq, 8192.0, mu)
     tt(c("DM", 0, 64), c("DM", 0, 64), c("DM", 64, 64), ad)
     tt(c("DM", 0, 64), c("DM", 0, 64), c("DM", 128, 64), ad)
-    act(c("DM", 192, 64), c("DM", 0, 64), AF.Identity, scale=-1.0)
+    act(c("DM", 64, 64), c("DM", 0, 64), AF.Identity, scale=-1.0)
     ts(ap("M2"), c("IT", 0, 16), ps(12), eq)
     ts(ap("MM"), ap("MM"), ps(2), eq)
-    ts(ap("CX"), ap("CX"), ps(8), su)
+    ts(ap("CX"), ap("CX"), ps(16), ad)
     ms(ap("ON"), 1.0)
-    for t in range(1, 5): ms(c("CT", 128 * (t - 1), 128), (5 - t) / 8.0)
     ms(ap("QT"), -0.25)
     ms(ap("D0"), -1.0)
-    ms(ap("D0", S_, slice(0, 1024, 64)), -128.0)
-    ms(c("X", 0, 16), -64.0)
-    for r in range(2):
-        ms(c("X", X0[r] + W + SL, 16), -64.0)
-        act(c("LT", L0[r] + W, SL), ap("ZR"), AF.Copy)
-    ms(c("Q", V, 16), 1000.0)
+    ms(c("TH", 14, 1), -0.5)
+    for b in range(4): ms(c("X", XN * b, 16), -64.0)
+    for s in range(2):
+        ms(c("XS", (16 + HV + GH) * s, 16), 0.0)
+        ms(c("Q", (V + 16) * s + V, 16), 1000.0)
     for b in ("CC", "T2", "T3"): ms(c(b, NC, 16), 8192.0)
     ms(ap("ZP"), 0.0); ms(ap("ZQ"), 0.0)
-    ms(ap("RC", S_, S_, 64), 0.0)
-    for b in "AB": ms(c("T" + b, 512, 8), 0.0); ms(ap("Z" + b), 0.0)
-    ts(ap("HI"), ap("NB"), M64, ad, M64, su)
-    tt(ap("LO"), ap("NB"), ap("HI"), su)
-    dma("S", [(ap("LT", slice(0, 128, 4), slice(0, W)), ap("HI"))])
-    dma("S", [(ap("LT", slice(1, 128, 4), slice(0, W)), ap("LO"))])
-    dma("S", [(c("Q", 0, V), ap("cq"))], [ap("LO")])
-    dma("S", [(c("LT", LR + V, GH), c("LT", V, GH))] + [(c("D1", 1024 * j, 1024), ap("ZR")) for j in range(4)], [ap("Q")])
-    ts(c("SI", 0, 48), ap("SN"), W - 1, an)
-    ts(c("SI", 48, 48), ap("SN"), 12, sh)
-    cp(ap("SU"), ap("SI"))
-    act(ap("MK"), ind(ap("MT"), c("SU", 48, 48)), AF.Copy)
-    mm(P(4, 0, NC), wrap("C", "X", X0[0], NC))
-    ts(c("LW", 0, NC), P(4, 0, NC), 0.0, AL.is_lt)
+    ms(ap("RC", S_, S_, 64), 0.0); ms(c("TA", 256, 8), 0.0); ms(ap("ZA"), 0.0)
+    for ph in range(4): ms(c("G%d" % ph, 0, 48, HP[1]), 0.0)
+    load(0)
+    fill("D1", 0, 4096); fill("D2", 0, 1664)
+    for b in range(3): fill("X", X0[b] + W, NEW); fill("LT", L0[b] + W, NEW)
 
-    def shown(r):
-        tt(ap("SG"), ind(c("LT", L0[r], V), c("SU", 0, 48)), ap("MK"), mu)
-        w = P(6, 256, 48)
-        mm(w, wrap("C", "SG", 0, 48))
-        off = 16 if r == 0 else GH + SL + 16
-        ts(c("WT", 0, 48), w, float(V), AL.is_ge, -8192.0 if r == 0 else -float(off + V), mu)
+    def low(out, x):
+        ts(out, x, 63, an)
+        ts(out, out, 65.0, mu)
+        ts(out, out, 4, sh, 63, an)
+
+    def head(ph):
+        s, r, b, par = ph % 2, ph // 2, ph % 3, ph % 2
+        xo, lo = X0[b], L0[b]
+        lw, Lw = c("LT", lo, W), c("LW", HC * ph, HC)
+        tt(ap("SG"), ind(ap("LS"), c("SU", 144 * s + 96, 48)) if r else ind(c("LT", lo, V), c("SU", 144 * s, 48)), c("MK", GH * s, GH), mu)
+        w, mb = P(6 + par, 416, 48), 6 + par
+        mm(w, wrap("C2", "SG", 0, 48))
+        ts(c("WT", 0, 48), w, float(V), AL.is_ge, -8192.0, mu)
         tt(c("WT", 48, 48), w, c("WT", 0, 48), ad)
-        ts(ap("WU"), c("WT", 48, 48), float(off), ad)
-        cp(c("WI", 0, 48), w)
-
-    def ramps(ro, do, n, k):
-        scan(ap("RR", slice(0, k), slice(ro, ro + n)), ap("D0", slice(0, k), slice(0, n)), ap("D1", slice(0, k), slice(do, do + n)), ad, mx)
-
-    def pair(hi, lo, k): return (ap("RR", slice(0, k), slice(hi, hi + 64)), ap("RR", slice(0, k), slice(lo, lo + 64)))
-    H = slice(0, 64)
-
-    def steps(bank, tb):
-        act(ap("RC", H, S_, H), P(bank, 0, 512, 64), AF.Copy)
-        tt(ap("T" + tb, H, slice(0, 512)), P(bank, 0, 512, 64), ap("RC", H, S_, slice(1, 65)), su)
-        cp(ap("Z" + tb, H, slice(15, 112, 16)), ap("T" + tb, H, slice(64, 512, 64)))
-
-    def cells(tb, e, a, z):
-        return ([(ap("T" + tb, H, slice(e + j, 512 + j, 4)), ap("DM", H, slice(192 * j + a, 192 * j + z))) for j in range(2)]
-                + [(ap("Z" + tb, H, S_), ap("DM", H, slice(a, z)))] * (e == 3))
-
-    def notices(dg):
-        mm(P(2, 256, 64, 96), [(ap("ZQ", S_, dg, slice(48, 144)), c("PA", 0, 64)), (ap("ZQ", S_, dg, slice(0, 96)), c("PA", 64, 64))])
-        cp(ap("D1", slice(0, 96), slice(0, W, 64)), P(2, 256, 64, 96))
-
-    shown(0)
-    for r in range(2):
-        xo, lo = X0[r], L0[r]
-        xw, lw, Lw = c("X", xo, W), c("LT", lo, W), c("LW", NC * r, NC)
-        sw = c("X", 0, 16 + V) if r == 0 else ap("X", X0[0] + V, X0[1] + V)
-        act(ap("S%d" % r), ind(sw, ap("WU")), AF.Copy)
-        send(ap("S%d" % r), c("X", xo + V, GH), 256, False, "ar%d" % (2 * r))
+        if r == 0:
+            ts(ap("WU"), c("WT", 48, 48), 16.0, ad)
+            act(ap("S%d" % ph), ind(c("X", xo - 16, 16 + V), ap("WU")), AF.Copy)
+        else:
+            ts(c("WT", 96, 48), w, ps(22), AL.is_ge, 4096.0, mu)
+            tt(c("WT", 96, 48), w, c("WT", 96, 48), ad)
+            ts(ap("WU"), c("WT", 96, 48), ps(23), ad, 16.0 + HV + GH, AL.min)
+            act(ap("SG"), ind(ap("XS"), ap("WU")), AF.Copy)
+            for a, n in ((0, 512), (512, 256)):
+                mm(P(par, 0, n), [(ap("HH"), c("SG", a, n))])
+                act(c("S%d" % ph, a, n), P(par, 0, n), AF.Copy)
+        send(ap("S%d" % ph), c("X", xo + V, GH), 256, False, "ar%d" % (2 * ph))
+        cp(c("WI", 0, 48), c("WT", 48, 48))
         ts(c("WI", 48, 48), c("WI", 0, 48), 6, sh)
-        ts(c("WI", 96, 48), c("WI", 0, 48), 15, an)
-        ts(c("WI", 144, 48), c("WI", 0, 48), 4, sh, 3, an)
-        ts(ap("WH"), c("WI", 48, 48), 1.0, ad)
-        ts(c("WI", 96, 48), c("WI", 96, 48), 4.0, mu, 1.0, ad)
-        tt(ap("ZQ", S_, 1, slice(48, 96)), c("WI", 96, 48), c("WI", 144, 48), ad)
-        mm(P(5, 0, NC), [(ap("BO"), Lw)])
-        mm(P(5, 256, NC), [(ap("BN"), Lw)])
-        mm(P(4, 0, NC), [(c("ON", 0, 128), Lw)])
-        scan(c("CC", 0, NC), c("ON", 0, NC), P(5, 0, NC), mu, ad)
+        low(c("WI", 96, 48), c("WI", 0, 48))
+        ts(c("WH", 48 * par, 48), c("WI", 48, 48), 1.0, ad, 0.0, mx)
+        ts(ap("ZQ", S_, 2 * par + 1, slice(48, 96)), c("WI", 96, 48), 1.0, ad)
+        mms([(P(mb, HC * j, HC), c("BO", 128 * j, 128), Lw) for j in range(4)])
+        scan(c("CC", 0, NC), c("ON", 0, NC), P(mb, 0, NC), mu, ad)
         tt(c("TH", 0, 14), ap("CC", S_, slice(15, 224, 16)), c("M2", 0, 14), mu)
-        red(c("TH", 16, 1), c("TH", 0, 14), True)
+        red(c("TH", 16, 1), c("TH", 0, 15), True)
         tt(ap("TM"), c("CC", 0, NC), ap("MM"), mu)
         scan(c("T2", 0, NC), c("ON", 0, NC), ap("TM"), mu, mx)
-        tt(c("T3", 0, NC), P(5, 256, NC), c("CC", 0, NC), ad)
+        tt(c("T3", 0, NC), P(mb, NC, NC), c("CC", 0, NC), ad)
+        act(ap("I1"), ap("IS"), AF.Sign, bias=c("TH", 16, 1))
+        mm(P(2, 384, 32), wrap("C", "I1", 0, 32))
+        ts(c("BU", 0, 32), P(2, 384, 32), 8.0, mu, 143.0, ad)
+        act(c("BB", 0, 32), P(2, 384, 32), AF.Identity, bias=128.0, scale=8.0)
+        tt(ap("I2"), ind(ap("T2"), c("BU", 0, 32)), ap("IS"), AL.is_le)
+        mm(P(2, 416, 32), [(pp, c("BB", 0, 32))] + wrap("C", "I2", 0, 32))
+        cp(c("BU", 32, 32), P(2, 416, 32))
+        act(c("BB", 32, 32), P(2, 416, 32), AF.Copy)
+        tt(ap("I3"), ind(ap("T3"), c("BU", 32, 32)), ap("IS"), AL.is_le)
+        mm(P(2, 448, 32), [(idm("x16"), c("BB", 32, 32))] + wrap("C", "I3", 0, 32))
+        cp(c("BU", 64, 32), P(2, 448, 32))
+        act(ap("LH"), ind(lw, c("BU", 64, 32)), AF.Copy)
+        act(c("QS", HS * par, HS), ind(c("Q", (V + 16) * s, V + 16), c("BU", 64, 32)), AF.Copy)
         for h in range(2):
-            o, b = 512 * h, 32 * h
-            act(c("I1", o, 512), c("IS", o, 512), AF.Sign, bias=c("TH", 16, 1))
-            mm(P(6, b, 32), wrap("C", "I1", o, 32))
-            ts(c("BU", b, 32), P(6, b, 32), 8.0, mu, 143.0, ad)
-            mm(P(7, 0, 32), wrap("C8", "I1", o, 32), True, False, True)
-            mm(P(3, 0, 32), wrap("C128", "I1", o, 32), True, False, True)
-            tt(c("I2", o, 512), ind(ap("T2"), c("BU", b, 32)), c("IS", o, 512), AL.is_le)
-            mm(P(7, 0, 32), wrap("C", "I2", o, 32), False, True, True)
-            ts(c("BU", 64 + b, 32), P(7, 0, 32), 128.0, ad)
-            mm(P(3, 0, 32), wrap("C16", "I2", o, 32), False, False, True)
-            tt(c("I3", o, 512), ind(ap("T3"), c("BU", 64 + b, 32)), c("IS", o, 512), AL.is_le)
-            mm(P(3, 0, 32), wrap("C", "I3", o, 32), False, True, True)
-            ts(c("BU", 128 + b, 32), P(3, 0, 32), 2048.0, ad)
-            act(c("LH", o, 512), ind(lw, c("BU", 128 + b, 32)), AF.Copy)
-            act(c("QS", o, 512), ind(ap("Q"), c("BU", 128 + b, 32)), AF.Copy)
-        red(c("TH", 17, 1), P(4, 0, NC), False)
+            t3 = c("T3", HC * h, HC, HP[h])
+            ts(c("Z1", 0, HC, HP[h]), t3, SL + 0.5, AL.is_le)
+            act(c("ZY", 0, HC, HP[h]), t3, AF.Identity, bias=ps(14, HP[h]))
+        z2 = c("Z2", HC * par, HC)
+        tt(ap("Z1"), ap("Z1"), Lw, mu)
+        tt(z2, ap("ZY"), ap("Z1"), mu)
+        tt(ap("Z1"), z2, ap("CX"), mx)
+        cp(c("UL", HC * par, HC), ap("Z1"))
+        for k in range(4): mm(z(ph, 1, k, 32), wrap("L%d" % k, "LH", 0, 32))
+        for t in range(1, 5):
+            for k in (0, 2): cp(ju(ph, t, k, 64), z(ph, t, k, 64))
+            act(zs(ph, t), z(ph, t), AF.Copy)
+            g = 2048 * (t % 2)
+            for k in range(4): act(c("LG", g + 512 * k, 512), ind(lw, ju(ph, t, k, 32)), AF.Identity, scale=c("MF", k, 1))
+            for k in (0, 2): mm(z(ph, t + 1, k, 64), wrap("C", "LG", g + 512 * k, 64))
+
+    def zs(ph, t): return c("ZS", 512 * (ph % 2) + 128 * (t - 1), 128)
+    def z(ph, t, k=0, n=128): return P(ph % 2, 128 * (t - 1) + 32 * k, n) if t < 5 else P(2, 128 * (ph % 2) + 32 * k, n)
+    def ju(ph, t, k=0, n=128): return c("JU", 640 * (ph % 2) + 128 * (t - 1) + 32 * k, n)
+    rot = [0, 0]
+
+    def count(a, fn, out, bias, scale):
+        mms([(P(2, 256 + i, 8, S_, 16), ap("IN", S_, slice(a + i, a + 2048, 16)), ap("G8")) for i in range(16)])
+        act(out, P(2, 256, 128), fn, bias, scale)
+
+    def limit(r):
+        mm(P(7, 0, HC), [(c("ON", 0, 128), c("LW", HC * (2 * r + s), HC)) for s in range(2)])
+        red(c("TH", 17, 1), P(7, 0, HC), False)
         cp(c("LI", 0, 1), c("TH", 17, 1))
         ts(c("LI", 1, 1), c("LI", 0, 1), 7, an)
-        lim = c("TH", 18, 1)
-        ts(lim, c("LI", 1, 1), 161.0, ad, 512.0, mu)
-        ts(ap("Z1"), c("T3", 0, NC), SL + 0.5, AL.is_le)
-        tt(ap("Z1"), ap("Z1"), Lw, mu)
-        act(ap("Z2"), c("T3", 0, NC), AF.Identity, bias=W - 1.0)
-        tt(ap("Z2"), ap("Z2"), ap("Z1"), mu)
-        tt(ap("Z1"), ap("Z2"), ap("CX"), mx)
-        cp(ap("UL"), ap("Z1"))
-        rot = [0, 0, 0]
-        mm(P(3, 0, 512, 64), [(c("ZR", 0, 64), c("ZR", 0, 512))], True, False, True)
-        for h in range(2):
-            ho, wo, qs = 2048 * h, 128 * h, c("QS", 512 * h, 512)
-            def z(t, k=0, n=128): return P((t - 1) // 2, 256 * ((t - 1) % 2) + wo + 32 * k, n)
-            def ju(t, k=0, n=128): return c("JU", 256 * (t - 1) + wo + 32 * k, n)
-            def dd(k): return c("DD", ho + 512 * k, 512)
-            def hf(b): return c(b, 512 * h, 512)
-            run = c("RN", wo, 128)
+        ts(c("TH", 18 + r, 1), c("LI", 1, 1), 161.0, ad, 512.0, mu)
 
-            def hop(t):
-                if t == 1:
-                    for k in range(4): mm(z(1, k, 32), [(pp, c("CT", 0, 32))] + wrap("L%d" % k, "LH", 512 * h, 32))
-                else:
-                    for k in range(4): act(c("LG", ho + 512 * k, 512), ind(lw, ju(t - 1, k, 32)), AF.Identity, scale=c("MF", k, 1))
-                    for k in (0, 2): mm(z(t, k, 64), ([(pp, c("CT", 128 * (t - 1), 64))] if t < 5 else []) + wrap("C", "LG", ho + 512 * k, 64))
-                if t < 5:
-                    for k in (0, 2): ts(ju(t, k, 64), z(t, k, 64), 2.0 ** 15, mu, -4096.0 * (5 - t), ad)
-                if t == 1: act(c("J1", wo, 128), z(1), AF.Identity, bias=-16384.0, scale=2.0 ** 15)
-
-            def visit(t, k):
-                o = c("IN", W * (t % 2) + ho + 512 * k, 512)
-                if (h, t, k) in ABLK:
-                    m = c("MG", 512 * (rot[1] % 4), 512); bk = P(4 + rot[1] % 2); rot[1] += 1
-                    act(m, ind(xw, ju(t, k, 32)), AF.Copy)
-                    mm(bk, [(pp, m), (nn, qs)])
-                    ts(o, bk, M32, ad, M32, eq)
-                else:
-                    d = c("DT", 512 * (rot[0] % 4), 512) if t < 5 else dd(k)
-                    rot[0] += 1
-                    tt(d, ind(xw, ju(t if t < 5 else 6, k, 32)), qs, su)
-                    ts(o, d, M32, ad, M32, eq)
-                if k == 3:
-                    n = P(2, 256 + 128 * (rot[2] % 2), 128); rot[2] += 1
-                    mm(n, wrap("C", "IN", W * (t % 2) + ho, 128))
-                    s = c("SS", 256 * (t % 2) + wo, 128)
-                    act(s, n, AF.Sign, bias=-8.5)
-                    if t == 1: tt(run, z(1), s, ad)
-                    elif t < 5:
-                        tt(z(t), z(t), s, ad)
-                        tt(run, z(t), run, mx)
-                    if t == 4:
-                        tt(run, z(5), run, mx)
-                        ts(c("JI", wo, 128), run, 2.0 ** 15, mu)
-                        ts(c("JF", wo, 128), c("JI", wo, 128), W - 1, an)
-                        cp(ju(6), c("JF", wo, 128))
-
-            hop(1)
-            for t in range(1, 5):
-                hop(t + 1)
-                for k in range(4): visit(t, k)
-            ts(c("JD", 2 * wo, 128), c("JF", wo, 128), 6, sh)
-            ts(c("JD", 2 * wo + 128, 128), c("JF", wo, 128), 15, an)
-            ts(c("JD", 512 + wo, 128), c("JF", wo, 128), 4, sh, 3, an)
-            for j in range(8):
-                ts(c("DG", 2 * wo + 32 * j, 32), c("JD", 2 * wo + 32 * j, 32), 1.0 + 3 * (j // 4), mu, 1.0 + 128 * (3 - j % 4) + 2.0 ** 22, ad)
-            tt(c("DG", 2 * wo + 128, 128), c("DG", 2 * wo + 128, 128), c("JD", 512 + wo, 128), ad)
-            tt(c("DJ", wo, 128), c("JF", wo, 128), c("J1", wo, 128), su)
-            visit(5, 0); visit(5, 1)
-            mm(P(6), [(pp, dd(0)), (nn, dd(1))])
-            act(hf("R1"), P(6), AF.Relu)
-            visit(5, 2)
-            mm(P(7), [(pp, dd(1)), (pp, hf("R1")), (nn, dd(2))])
-            act(hf("R5"), P(7), AF.Relu)
-            mm(P(6), [(pp, hf("R1")), (nn, dd(0)), (pp, dd(2))])
-            act(hf("R6"), P(6), AF.Relu)
-            visit(5, 3)
-            mm(P(7 - 3 * h), [(pp, dd(2)), (pp, hf("R5")), (nn, dd(3))])
-            act(hf("R7"), P(7 - 3 * h), AF.Relu)
-            mm(P(6), [(nn, dd(2)), (pp, hf("R6")), (pp, dd(3))])
-            if h: ts(hf("R8"), P(6), 0.0, mx)
-            else: act(hf("R8"), P(6), AF.Relu)
-            mm(P(7), [(pp, ap("QT")), (hp, dd(0)), (hp, dd(1)), (hp, dd(2))], True, False, True)
-            mm(P(7), [(hn, dd(3))], False, False, True)
-            mm(P(7), [(hn, hf("R7")), (hp, hf("R8"))], False, True, True)
-            ts(hf("YD"), P(7), M1, ad, M1, su)
+    def visits(ph):
+        xw, qs = c("X", X0[ph % 3], W), c("QS", HS * (ph % 2), HS)
+        for t in range(1, 5):
             for k in range(4):
-                bk = P(4 + k if h else 6 + k % 2)
-                mm(bk, [(pp, dd(k)), (nn, hf("YD"))])
-                act(c("AB", ho + 512 * k, 512), bk, AF.Abs)
-            D = P(6, 0, 128)
-            mm(D, [(idm("nf"), c("SS", 256 + wo, 128))], True, False, True)
-            for k in (0, 2): mm(P(6, 32 * k, 64), wrap("C512", "AB", ho + 512 * k, 64), False, k == 2, True)
-            for dg in range(2): tt(ap("KY", S_, S_, slice(32 * dg, 32 * dg + 32)), D, c("DG", 2 * wo + 128 * dg, 128), ad)
-            tt(ap("K1"), ap("KY", S_, slice(0, 2), S_), ap("KY", S_, slice(2, 4), S_), mx)
-            tt(ap("K2"), c("K1", 0, 64), c("K1", 64, 64), mx)
-            go = ap("GO", S_, S_, slice(32 * h, 32 * h + 32))
-            ts(ap("KD"), ap("K2"), 127, an)
-            ts(go, ap("K2"), lim, AL.is_lt)
-            ts(ap("NF"), ap("K2"), 2.0 ** 22, AL.is_lt)
-            tt(ap("AC"), ap("NF"), go, su)
-            tt(ap("ZP", S_, S_, slice(96, 128)), ap("KD"), ap("AC"), mu)
-            for dg in range(2):
-                mm(P(7, 32 * dg, 32), [(ap("ZP", S_, dg, slice(96 - 32 * j, 224 - 32 * j)), c("PA", 128 + 32 * j, 32)) for j in range(4)])
-            cp(ap("D1", S_, slice(0, W, 64)), P(7, 0, 64))
-            for q in range(2):
-                ramps(W * h + 1024 * q, 1024 * q, 1024, 128); ramps(W * h + 2048 + 1024 * q, 2048 + 1024 * q, 1024, 128)
-                for gg in range(4 * q, 4 * q + 4):
-                    mm(P(3, 64 * gg, 64, 64), [pair(W * h + 64 * j, W * h + 2048 + 64 * j, 128) for j in range(4 * gg, 4 * gg + 4)], False, h == 1 and gg == 7, True)
-            for j in range(2): tt(c("JS", wo + 64 * j, 64), c("DJ", wo + 64 * j, 64), go, mu)
-            tt(c("JS", wo, 128), c("JS", wo, 128), c("J1", wo, 128), ad)
-            jh, jl = (ap("JW", S_, slice(4 * j, 4 * j + 4), slice(32 * h, 32 * h + 32)) for j in range(2))
-            ts(jh, c("JS", wo, 128), M64, ad, M64, su)
-            tt(jl, c("JS", wo, 128), jh, su)
-        steps(3, "A")
-        for e in range(4): mm(P(2, 12 * e, 12), cells("A", e, 52, 64))
-        for e in range(4): ts(ap("G%d" % r, S_, slice(e, 48, 4)), P(2, 12 * e, 12), 0.5, AL.is_gt)
-        send(ap("G%d" % r), ap("N%d" % r), 16, True, "ar%d" % (2 * r + 1))
-        mm(P(0, 0, 256), [(c("ZR", 0, 128), c("ZR", 0, 256))], True, False, True)
-        for e in range(4): mm(P(0, 64 * e, 52), cells("A", e, 0, 52), False, False, True)
-        notices(1)
-        for q in range(4): ramps(1024 * q, 1024 * q, 1024, 96)
-        jrow = lambda j: ap("LT", slice(j, 128, 16), slice(lo + W, lo + LR))
-        dma("S", [(jrow(2), ap("GO", S_, 0, S_))] + [(jrow(4 * (j % 4) + j // 4), ap("JW", S_, j, S_)) for j in range(8)])
-        ln = L0[1 - r]
+                o = c("IN", 2048 * (t % 2) + 512 * k, 512)
+                if (t, k) in ABLK[ph]:
+                    m = c("MG", 512 * (rot[1] % 2), 512); rot[1] += 1
+                    act(m, ind(xw, ju(ph, t, k, 32)), AF.Copy)
+                    mm(P(3), [(pp, m), (nn, qs)])
+                    ts(o, P(3), M32, ad, M32, eq)
+                else:
+                    d = c("DT", 512 * (rot[0] % 4), 512); rot[0] += 1
+                    tt(d, ind(xw, ju(ph, t, k, 32)), qs, su)
+                    ts(o, d, M32, ad, M32, eq)
+            sg = c("SS", 128 * (t % 2), 128)
+            count(2048 * (t % 2), AF.Sign, sg, -8.5, 1.0)
+            mm(z(ph, t), [(ap("IF"), zs(ph, t)), (sg, idm("s%d" % t))])
+            if t == 1: act(ap("RN"), z(ph, 1), AF.Copy)
+            else: tt(ap("RN") if t < 4 else ap("JI"), z(ph, t), ap("RN"), mx)
+            if t == 3: tt(ap("RN"), z(ph, 5), ap("RN"), mx)
+        ts(ap("JF"), ap("JI"), W - 1, an)
+        cp(ju(ph, 5), ap("JF"))
+
+    def verdict(ph):
+        par, xo, lo = ph % 2, X0[ph % 3], L0[ph % 3]
+        xw, qs = c("X", xo, W), c("QS", HS * par, HS)
+        m = [c("DD", 512 * k, 512) for k in range(4)]
+        R1, R2, R3, R4, Y = (ap(x) for x in ("R1", "R2", "R3", "R4", "YY"))
+        for k in range(4):
+            if FIN[ph][k] == "A": act(m[k], ind(xw, ju(ph, 5, k, 32)), AF.Copy)
+            else: cp(m[k], ind(xw, ju(ph, 5, k, 32)))
+        ts(c("JD", 0, 128), ap("JF"), 6, sh)
+        low(c("JD", 128, 128), ap("JF"))
+        tt(ap("DJ"), ap("JF"), zs(ph, 1), su)
+        mm(P(4), [(pp, m[0]), (nn, m[1])])
+        act(R1, P(4), AF.Relu)
+        mm(P(5), [(pp, m[2]), (nn, m[3])])
+        act(R2, P(5), AF.Relu)
+        mm(P(par), [(pp, m[1]), (nn, m[3])], True, True)
+        mm(P(par), [(pp, R1), (nn, R2)], False)
+        act(R3, P(par), AF.Relu)
+        mm(P(4), [(pp, m[0]), (nn, R1), (nn, m[2])], True, True)
+        mm(P(4), [(pp, R2)], False)
+        act(R4, P(4), AF.Relu)
+        mm(P(5), [(pp, ap("QT")), (hp, m[1]), (hp, m[2]), (hp, R1), (hn, R2)], True, True)
+        mm(P(5), [(hn, R3)], False)
+        mm(P(5), [(hp, R4)] + [(idm("m1"), ap("QT"))] * (RND[ph] == "A"), False)
+        if RND[ph] == "A": act(Y, P(5), AF.Identity, -M1)
+        else: ts(Y, P(5), M1, ad, M1, su)
+        for k in range(4):
+            mm(P(3), [(pp, m[k]), (nn, qs)])
+            ts(c("IN", 4096 + 512 * k, 512), P(3), M32, ad, M32, eq)
+        count(4096, AF.Relu, c("SS", 256, 128), 8.5, -1.0)
+        for k in range(4):
+            bk = P((par, 4, 3, 5)[k])
+            mm(bk, [(pp, m[k])], True, True)
+            mm(bk, [(nn, Y)], False)
+            act(c("AB", 512 * k, 512), bk, AF.Abs)
+        D = P(6 + par, 0, 128)
+        mm(D, [(pp, ap("KC")), (pp, c("ON", 0, 128)), (c("SS", 256, 128), idm("nf"))], True, True)
+        for k in (0, 2): mm(P(6 + par, 32 * k, 64), wrap("C512", "AB", 512 * k, 64), False, True)
+        for dg in range(2): tt(ap("KY", S_, S_, slice(32 * dg, 32 * dg + 32)), D, c("JD", 128 * dg, 128), ad)
+        tt(ap("K1"), ap("KY", S_, slice(0, 2), S_), ap("KY", S_, slice(2, 4), S_), mx)
+        tt(ap("K2"), c("K1", 0, 64), c("K1", 64, 64), mx)
+        ts(ap("KD"), ap("K2"), 127, an)
+        ts(ap("GO"), ap("K2"), c("TH", 18 + ph // 2, 1), AL.is_lt)
+        ts(ap("NF"), ap("K2"), 2.0 ** 22, AL.is_lt)
+        tt(ap("AC"), ap("NF"), ap("GO"), su)
+        tt(ap("ZP", S_, S_, slice(96, 128)), ap("KD"), ap("AC"), mu)
+        for j in range(2): tt(c("JS", 64 * j, 64), c("DJ", 64 * j, 64), ap("GO"), mu)
+        tt(ap("JS"), ap("JS"), zs(ph, 1), ad)
+        jh, jl = (ap("JW", S_, slice(4 * j, 4 * j + 4), S_) for j in range(2))
+        ts(jh, ap("JS"), M64, ad, M64, su)
+        tt(jl, ap("JS"), jh, su)
+        jrow = lambda j: ap("LT", slice(j, 128, 16), slice(lo + W + HS, lo + W + 2 * HS))
+        dma([(jrow(2), ap("GO", S_, 0, S_))] + [(jrow(4 * (j % 4) + j // 4), ap("JW", S_, j, S_)) for j in range(8)])
+        mms([(P(5, 32 * i, 32), pp, ap("YY", S_, slice(i, HS, 16))) for i in range(16)])
+        act(c("X", xo + W + HS, HS), P(5), AF.Copy)
+        for b, o in (("X", xo), ("LT", lo)):
+            dma([(c(b, o + W + 2 * HS * (1 - h), HS, HP[h]), c(b, o + W + HS, HS, HP[1 - h])) for h in range(2)])
+
+    def ramps(out, ro, d, do, n, p):
+        scan(c(out, ro, n, p), c("D0", 0, n, p), c(d, do, n, p), ad, mx)
+
+    def steps(b):
+        act(ap("RC", H64, S_, H64), P(b, 0, 256, H64), AF.Copy)
+        tt(c("TA", 0, 256, H64), P(b, 0, 256, H64), ap("RC", H64, S_, slice(1, 65)), su)
+        cp(ap("ZA", H64, slice(15, 63, 16)), ap("TA", H64, slice(64, 256, 64)))
+
+    def cells(e, a, n):
+        return ([(ap("TA", H64, slice(e + j, 253 + e + j, 4)), c("DM", 64 * j + a, n, H64)) for j in range(2)]
+                + [(ap("ZA", H64, S_), c("DM", a, n, H64))] * (e == 3))
+
+    def notices(par, dg, o):
+        zq = lambda a: ap("ZQ", H64, 2 * par + dg, slice(a, a + 96))
+        mm(P(6 + par, o, 32, H96), [(zq(48), c("PA", 0, 32, H64)), (zq(0), c("PA", 32, 32, H64))])
+
+    def tail(ph):
+        s, r, par = ph % 2, ph // 2, ph % 2
+        xo, lo, xn, ln = X0[ph % 3], L0[ph % 3], X0[(ph + 2) % 3], L0[(ph + 2) % 3]
+        mb = 6 + par
+        for dg in range(2):
+            mm(P(mb, 128 + 32 * dg, 32), [(ap("ZP", S_, dg, slice(96 - 32 * j, 224 - 32 * j)), c("PA", 64 + 32 * j, 32)) for j in range(4)])
+        cp(ap("D1", S_, slice(0, W, 64)), P(mb, 128, 64))
+        mm(P(par, 0, 256, H64), [(c("ZR", 0, 64), c("ZR", 0, 256))], True, True)
         for h in range(2):
-            for i in range(8 * h, 8 * h + 8):
-                mm(P(4 + h, 64 * (i % 8), 64), [(pp, ap("YD", S_, slice(i, SL, 16))), (pp, ap("QS", S_, slice(i, SL, 16)))])
-            act(c("X", xo + W + 512 * h, 512), P(4 + h), AF.Copy)
-        for h in range(2):
-            a = 104 * h
-            act(c("LT", ln + 16 * a, 1664), ind(c("LT", lo, LR), c("UL", a, 104)), AF.Copy)
-            mm(P(6 + h, 0, 104), wrap("FL", "LT", ln + 16 * a, 104))
-            tt(c("Z3", a, 104), P(6 + h, 0, 104), c("Z2", a, 104), mu)
-            if r == 0: tt(c("NL", a, 104), P(6 + h, 0, 104), c("LW", a, 104), AL.is_lt)
-        tt(ap("Z3"), ap("Z3"), ap("CX"), mx)
-        tt(ap("ZQ", S_, 0, slice(48, 96)), ap("N%d" % r), ap("WH"), mu)
-        notices(0)
-        for q in range(4):
-            ramps(W + 1024 * q, 1024 * q, 1024, 96)
-            for gg in (2 * q, 2 * q + 1): mm(P(1, 64 * gg, 64, 64), [pair(W + 64 * j, 64 * j, 96) for j in range(8 * gg, 8 * gg + 8)])
-        if r == 0: shown(1)
-        else:
-            for h in range(2):
-                mm(P(4 + h, 0, 416), [(c("OM", 3 - e, 128), c("LT", ln + 832 * e + 416 * h, 416)) for e in range(4)])
-                act(c("YN", 416 * h, 416), P(4 + h, 0, 416), AF.Copy)
-            dma("S", [(ap("yn"), ap("YN"))])
-        steps(1, "B")
-        for e in range(4): mm(P(0, 64 * e, 52), cells("B", e, 0, 52), False, e == 3, True)
-        for e in range(4): ts(ap("FA", S_, slice(e, NC, 4)), P(0, 64 * e, 52), 0.5, AL.is_gt, float(W + SL), mu)
+            for dg in range(2): ramps("RR", 2048 * dg + 1024 * h, "D1", 2048 * dg + 1024 * h, 1024, S_)
+            for q in range(4):
+                mm(P(par, 64 * q, 64, H64), [(c("RR", 64 * j, 64), c("RR", 2048 + 64 * j, 64)) for j in range(16 * h + 4 * q, 16 * h + 4 * q + 4)], False)
+        steps(par)
+        for e in range(4): mm(P(mb, 192 + e, 12, H64, 4), cells(e, 52, 12))
+        ts(c("G%d" % ph, 0, 48, H64), P(mb, 192, 48, H64), 0.5, AL.is_gt)
+        send(ap("G%d" % ph), ap("N%d" % ph), 16, True, "ar%d" % (2 * ph + 1), [c("X", X0[0] + V, GH)] * (ph == 1))
+        mm(P(par, 0, 256, H64), [(c("IF", 0, 64, H64), ap("RC", H64, S_, H64))], True, True)
+        notices(par, 1, 240)
+        cp(ap("D1", H96, slice(0, 2048, 64)), P(mb, 240, 32, H96))
+        for q in range(2): ramps("RL", 1024 * q, "D1", 1024 * q, 1024, H96)
+        act(ap("LS"), ind(c("LT", lo, LN), c("UL", HC * par, HC)), AF.Copy)
+        mm(P(mb, 408, HC), wrap("FL", "LS", 0, HC))
+        tt(ap("Z3"), P(mb, 408, HC), c("Z2", HC * par, HC), mu)
         if r == 0:
-            ts(ap("F1"), ap("FA"), 1.0, AL.min)
-            tt(c("LW", NC, NC), ap("F1"), ap("NL"), mx)
-        tt(ap("Z3"), ap("Z3"), ap("FA"), mx)
-        cp(ap("UX"), ap("Z3"))
-        xn = X0[1 - r]
-        cuts = [0, 16, NC] if r == 0 else [0, 60, 120, 164, NC]
-        for j in range(len(cuts) - 1):
-            a, n = cuts[j], cuts[j + 1] - cuts[j]
-            o, x = c("X", xn + 16 * a, 16 * n), ind(c("X", xo, XR), c("UX", a, n))
-            if j % 2: act(o, x, AF.Copy)
+            dma([(c("LT", ln + HV * h, HV, HP[j]), c("LS", 0, HV, HP[h])) for h in range(2) for j in range(2)])
+            dma([(c("LT", ln + V, GH), c("LT", lo + V, GH))])
+            dma([(c("XS", 16 + HV, GH), c("X", xo + V, GH))])
+            tt(ap("NL"), ap("Z3"), c("LW", HC * ph, HC), AL.is_lt)
+            act(ap("TR"), ap("NL"), AF.Identity, bias=8000.0, scale=-9000.0)
+        tt(ap("Z3"), ap("Z3"), ap("CX"), mx)
+        tt(ap("ZQ", H64, 2 * par, slice(48, 96)), c("N%d" % ph, 0, 48, H64), c("WH", 48 * par, 48, H64), mu)
+        notices(par, 0, 272)
+        cp(ap("D2", H96, slice(0, 1664, 52)), P(mb, 272, 32, H96))
+        for q in range(2):
+            ramps("RH", 832 * q, "D2", 832 * q, 832, H96)
+            for u in (2 * q, 2 * q + 1):
+                mm(P(par, 64 * u, 64, slice(0, 52)), [(c("RH", 52 * j, 52, H96), c("RL", 64 * j, 64, H96)) for j in range(8 * u, 8 * u + 8)], False)
+        steps(par)
+        fa = P(mb, 304, HC)
+        mm(fa, [(c("ZR", 0, 128), c("ZR", 0, HC))], True, True)
+        for h in range(2):
+            for e in range(4): mm(P(mb, 304 + e, 26, HP[h], 4), cells(e, 26 * h, 26), False, True)
+        mm(fa, [(ap("IF"), ap("Z3"))], False, True)
+        ts(ap("UX"), fa, float(W + NEW), AL.min)
+        if r == 0: tt(c("LW", HC * (ph + 2), HC), fa, ap("TR"), AL.is_gt)
+        else:
+            yb = 5 if ph == 3 else par
+            mm(P(yb, 0, 416), [(c("OM", 3 - e, 128), c("LS", 416 * e, 416)) for e in range(4)])
+            act(ap("YN"), P(yb, 0, 416), AF.Copy)
+            dma([(ap("yn", slice(4 * s, 4 * s + 4), S_), ap("YN"))])
+        a = 0
+        for e, n in XUP[ph]:
+            o, x = c("XS", 16 + 16 * a, 16 * n), ind(c("X", xo, XN), c("UX", a, n))
+            if e == "A": act(o, x, AF.Copy)
             else: cp(o, x)
-            if r == 1: dma("S", [(c("yx", 16 * a, 16 * n), o)])
+            xs = [c("XS", 16 + 16 * a, 16 * n, HP[h]) for h in range(2)]
+            if r == 0: dma([(c("X", xn + HV * h + 16 * a, 16 * n, HP[j]), xs[h]) for h in range(2) for j in range(2)])
+            else: dma([(ap("yx", slice(64 * s, 64 * s + 64), slice(HV * h + 16 * a, HV * h + 16 * (a + n))), xs[h]) for h in range(2)])
+            a += n
+
+    todo = [(head, 0), (load, 1), (limit, 0), (head, 1), (visits, 0), (verdict, 0)]
+    for ph in range(1, 4):
+        todo += [(visits, ph), (tail, ph - 1)] + [(limit, 1)] * (ph == 2) + [(head, ph + 1)] * (ph < 3) + [(verdict, ph)]
+    names = {head: "head", load: "load", limit: "limit", visits: "visits", verdict: "verdict", tail: "tail"}
+    for f, ph in todo + [(tail, 3)]:
+        stage[0] = names[f] + str(ph); f(ph)
     return ops
 
 
-def order(ops):
-    n = len(ops)
-    last = {}
+def depend(ops):
+    last, news, adds, opened = {}, {}, {}, {}
     for i, o in enumerate(ops):
         dep = set()
+        if o["s"]:
+            bk = list(o["w"])[0][0]
+            if o["s"] != "add": dep.update(adds.get(bk, []))
+            if o["s"] == "open": dep.update(news.get(bk, [])); opened[bk] = i
+            o["sum"] = opened.get(bk)
+            (adds if o["s"] == "add" else news).setdefault(bk, []).append(i)
         for (nm, pm), m in o["r"].items():
             dep.update(x[0] for x in last.get(nm, []) if x[3] and x[1] & m and x[2] & pm)
         for (nm, pm), m in o["w"].items():
@@ -444,53 +516,151 @@ def order(ops):
         for w, key in ((False, "r"), (True, "w")):
             for (nm, pm), m in o[key].items(): last.setdefault(nm, []).append((i, m, pm, w))
         dep.discard(i)
-        o["d"] = dep
-        o["b"] = {x[0] for x in list(o["r"]) + list(o["w"]) if x[0][:2] == "ps"}
+        o["d"] = sorted(dep)
+        o["b"] = sorted({x[0] for x in list(o["r"]) + list(o["w"]) if x[0][:2] == "ps"})
+
+
+def span(ops, seq, fig, tm=None):
+    cy, ga, lat = fig
+    free, bank, fin, pipe = {}, {}, {}, 0.0
+    for i in seq:
+        o = ops[i]; e = o["e"]
+        s = free.get(e, 0.0)
+        for j in o["d"]:
+            y = fin[j] + (0.0 if ops[j]["e"] == e == "T" else lat)
+            if y > s: s = y
+        for b in o["b"]:
+            for e2, y in bank.setdefault(b, {}).items():
+                if e2 != e and y + lat > s: s = y + lat
+        c = price(o, cy, ga)
+        free[e] = fin[i] = s + c
+        if o["k"] == "dma": pipe = fin[i] = max(pipe, s + c + DLAT) + o["c"][3]
+        for b in o["b"]: bank[b][e] = fin[i]
+        if tm is not None: tm[i] = (s, fin[i])
+    return max(fin.values())
+
+
+def order(ops):
+    depend(ops)
+    n = len(ops)
+    cy, ga, lat = FIGS[0]
     succ = [[] for _ in ops]
     for i, o in enumerate(ops):
         for j in o["d"]: succ[j].append(i)
-    full = [(o["c"][0] + o["c"][1] + 1800.0) if o["k"] == "dma" else o["c"] for o in ops]
-    best, x = None, 12345
-    base = [0.0] * n
-    for i in range(n - 1, -1, -1): base[i] = full[i] + max([base[j] + LAT for j in succ[i]], default=0.0)
-    for it in range(TRIES):
-        pr = list(best[3]) if best else base
-        for _k in range(NPERT if it else 0):
-            x = (x * 1103515245 + 12345) % 2 ** 31
-            j = (x >> 8) % n
-            x = (x * 1103515245 + 12345) % 2 ** 31
-            pr[j] += AMP * (x / 2 ** 30 - 1)
-        left = [len(o["d"]) for o in ops]
-        ready = {i: 0.0 for i in range(n) if left[i] == 0}
-        free, bank, fin, sq, tm, pipe = {}, {}, [0.0] * n, [], {}, 0.0
+    cost = [price(o, cy, ga) for o in ops]
+    full = [cost[i] + (o["c"][3] + DLAT if o["k"] == "dma" else 0.0) for i, o in enumerate(ops)]
+    eng = [o["e"] for o in ops]
+    pred = [o["d"] for o in ops]
+
+    def place(key, back):
+        pre, suc = (succ, pred) if back else (pred, succ)
+        left = [len(p) for p in pre]
+        ready = sorted((key[i], i) for i in range(n) if left[i] == 0)
+        line, st = {}, [0.0] * n
         while ready:
-            est = {}
-            for i, s in ready.items():
-                o = ops[i]
-                s = max(s, free.get(o["e"], 0.0))
-                for b in o["b"]:
-                    for e, y in bank.get(b, {}).items():
-                        if e != o["e"]: s = max(s, y + LAT)
-                est[i] = s
-            i0 = min(est, key=lambda i: (est[i], -pr[i]))
-            e0 = ops[i0]["e"]
-            i = max((i for i in est if ops[i]["e"] == e0 and est[i] <= est[i0] + min(LOOK, full[i0])), key=lambda i: (pr[i], -i))
-            o = ops[i]; s = est[i]
-            if o["k"] == "dma":
-                free[e0] = s + o["c"][0]
-                pipe = fin[i] = max(pipe, s + o["c"][0] + 1800.0) + o["c"][1]
-            else: free[e0] = fin[i] = s + o["c"]
-            tm[i] = (s, fin[i])
-            for b in o["b"]: bank.setdefault(b, {})[e0] = fin[i]
-            sq.append(i); del ready[i]
+            i = ready.pop(0)[1]; e = eng[i]
+            s = max([st[j] + full[j] + (0.0 if eng[j] == e == "T" else lat) for j in pre[i]], default=0.0)
+            use = [(e, 0.0, cost[i], 0.0)] + [(b, 0.0, cost[i], lat) for b in ops[i]["b"]]
+            if full[i] > cost[i]: use.append(("D", cost[i] + DLAT, full[i], 0.0))
+            if back: use = [(r, full[i] - z, full[i] - a, p) for r, a, z, p in use]
+            moved = True
+            while moved:
+                moved = False
+                for r, a, z, p in use:
+                    ln = line.setdefault(r, [])
+                    lo, hi = 0, len(ln)
+                    while lo < hi:
+                        mid = (lo + hi) // 2
+                        if ln[mid][1] + p <= s + a: lo = mid + 1
+                        else: hi = mid
+                    while lo < len(ln) and ln[lo][0] < s + z + p:
+                        q = 0.0 if ln[lo][2] == e else p
+                        if ln[lo][0] < s + z + q - 1e-6 and ln[lo][1] + q > s + a + 1e-6: s = ln[lo][1] + q - a; moved = True
+                        lo += 1
+            st[i] = s
+            for r, a, z, p in use:
+                ln = line[r]; j = len(ln)
+                while j and ln[j - 1][0] > s + a: j -= 1
+                ln.insert(j, (s + a, s + z, e))
+            for j in suc[i]:
+                left[j] -= 1
+                if left[j] == 0:
+                    y, lo = (key[j], j), len(ready)
+                    while lo and ready[lo - 1] > y: lo -= 1
+                    ready.insert(lo, y)
+        return st
+
+    base = [0.0] * n
+    for i in range(n - 1, -1, -1): base[i] = min([base[j] - lat for j in succ[i]], default=0.0) - full[i]
+
+    def run(key):
+        left = [len(p) for p in pred]
+        ready, free, bank, fin, st, pipe = {}, {}, {}, [0.0] * n, [0.0] * n, 0.0
+        for i in range(n):
+            if left[i] == 0: ready.setdefault(eng[i], {})[i] = 0.0
+        for _k in range(n):
+            first = None
+            for e, rd in ready.items():
+                f, est = free.get(e, 0.0), {}
+                for i, s in rd.items():
+                    if f > s: s = f
+                    for b in ops[i]["b"]:
+                        for e2, y in bank.setdefault(b, {}).items():
+                            if e2 != e and y + lat > s: s = y + lat
+                    est[i] = s
+                if est:
+                    m = min(est.values())
+                    if first is None or m < first[0]: first = (m, e, est)
+            m, e, est = first
+            i = min((key[i], i) for i in est if est[i] <= m + LOOK)[1]
+            st[i] = est[i]
+            free[e] = fin[i] = st[i] + cost[i]
+            if full[i] > cost[i]: pipe = fin[i] = max(pipe, fin[i] + DLAT) + ops[i]["c"][3]
+            for b in ops[i]["b"]: bank[b][e] = fin[i]
+            del ready[e][i]
             for j in succ[i]:
                 left[j] -= 1
-                if left[j] == 0: ready[j] = max(fin[y] + (0.0 if ops[y]["e"] == ops[j]["e"] == "T" else LAT) for y in ops[j]["d"])
-        if best is None or max(fin) <= best[0]: best = (max(fin), sq, tm, pr)
-    seq = best[1]
+                if left[j] == 0: ready.setdefault(eng[j], {})[j] = max(fin[y] + (0.0 if eng[y] == eng[j] == "T" else lat) for y in pred[j])
+        return st
+
+    parts = sorted({(o["g"], o["e"]) for o in ops}) + sorted({(o["g"], "") for o in ops})
+    seed = [SEED]
+
+    def rnd():
+        seed[0] = (seed[0] * 1103515245 + 12345) % 2 ** 31
+        return (seed[0] >> 8) / 2 ** 23
+
+    best, unit = None, None
+    for it in range(TRIES):
+        key = list(best[2]) if best else [base[i] + 1000.0 * SHIFT.get(ops[i]["g"], 0) for i in range(n)]
+        if it and rnd() < 0.5:
+            g, e = parts[int(rnd() * len(parts))]
+            d = 4 * AMP * (2 * rnd() - 1)
+            for i in range(n):
+                if ops[i]["g"] == g and e in ("", eng[i]): key[i] += d
+        elif it:
+            for _k in range(NPERT):
+                j, d = int(rnd() * n), AMP * (2 * rnd() - 1)
+                for i in range(j, min(n, j + 1 + int(rnd() * RUN))): key[i] += d
+        st = run(key)
+        sq = sorted(range(n), key=lambda i: (st[i], i))
+        t = [span(ops, sq, FIGS[0])]
+        if best and t[0] > best[3] * 1.01: continue
+        t += [span(ops, sq, f) for f in FIGS[1:]]
+        unit = unit or t
+        val = sum(a / b for a, b in zip(t, unit))
+        if best is None or val <= best[0]: best = (val, sq, key, t[0], st)
+    bk = place([-best[4][i] - full[i] for i in range(n)], True)
+    st = place([-bk[i] - full[i] for i in range(n)], False)
+    sq = sorted(range(n), key=lambda i: (st[i], i))
+    seq = sq if sum(span(ops, sq, f) / u for f, u in zip(FIGS, unit)) < best[0] else best[1]
+    ends = {}
+    for i in seq:
+        if ops[i]["s"] in ("open", "add"): ends[ops[i]["sum"]] = i; ops[i]["a"] = ops[i]["a"][:3] + (False,)
+    for i in ends.values(): ops[i]["a"] = ops[i]["a"][:3] + (True,)
     pos, cnt, clock, known, user, nd = {}, {}, {}, {}, {}, 0
     for i in seq:
-        o = ops[i]; e = o["e"]; o["t"] = best[2][i]
+        o = ops[i]; e = o["e"]
         if o["k"] == "dma": o["src"] = "d%d" % nd; nd += 1
         else: o["src"] = o["a"][0] if o["k"] == "arr" else "e" + e
         dep = set(o["d"])
@@ -502,7 +672,7 @@ def order(ops):
         if o["k"] != "arr":
             for j in sorted(dep, key=lambda j: -pos[j]):
                 p = ops[j]
-                if p["e"] == e == "T" or kn.get(p["src"], -1) >= pos[j]: continue
+                if p["e"] == e == "T" or p["k"] == "send" or kn.get(p["src"], -1) >= pos[j]: continue
                 o["wait"].append(j); p["inc"] = True
                 for k, v in clock[j].items(): kn[k] = max(kn.get(k, -1), v)
         pos[i] = len(pos)
@@ -542,7 +712,7 @@ def rank_program(g, core, T, topo):
         for j in o["wait"]:
             p = ops[j]
             q.wait_ge(T.sem[p["src"]], arrive if p["k"] == "arr" else p["val"]); waited.add(j)
-        x = [real(T, y) for y in a] if k not in ("mm", "dma", "send") else None
+        x = [real(T, y) for y in a] if k not in ("mm", "mms", "dma", "send") else None
         if k == "ts": r = q.tensor_scalar(*(x[:5] if x[5] is None else x))
         elif k == "tt": r = q.tensor_tensor(*x)
         elif k == "cp": r = q.tensor_copy(*x)
@@ -554,6 +724,8 @@ def rank_program(g, core, T, topo):
         elif k == "mm":
             for m, (l, rr) in enumerate(a[1]):
                 r = q.matmul(real(T, a[0]), real(T, l), real(T, rr), a[2] and m == 0, a[3] and m == len(a[1]) - 1)
+        elif k == "mms":
+            for oo, l, rr in a[0]: r = q.matmul(real(T, oo), real(T, l), real(T, rr), True, True)
         elif k == "dma":
             for oo, ii in a: q.dma_start(real(T, oo), real(T, ii)).then_inc(T.sem[o["src"]], 16)
             continue

@@ -1,3 +1,4 @@
+import math
 from concourse.bass import DstId, RemoteDMATransfer
 from concourse.mybir import AluOpType as AL, AxisListType as AX, ActivationFunctionType as AF
 
@@ -8,21 +9,23 @@ XN, LN = W + NEW + 16, W + NEW
 X0 = [16, 16 + XN, 16 + 2 * XN]
 L0 = [0, LN, 2 * LN]
 M32, M64, M1 = 1.5 * 2 ** 28, 1.5 * 2 ** 29, 1.5 * 2 ** 23
-ABLK = [[(4, 3)], [(3, 3), (4, 3)], [(3, 3), (4, 3)], [(2, 3), (3, 3), (4, 3), (4, 2)]]
-FIN = ["AAAA", "AAAA", "AAAA", "AVAV"]
+ABLK = [[(3, 3), (4, 3)], [(2, 3), (3, 3), (4, 3)], [(4, 3)], [(3, 3), (4, 3)]]
+FIN = ["AVAV", "AVAV", "AAAA", "AVAV"]
+REL = ["AAAA", "AAAA", "AAAA", "AVAV"]
 RND = "VVVV"
-XUP = [[("A", 104)], [("A", 104)], [("A", 104)], [("V", 52), ("A", 52)]]
+XUP = [[("V", 52), ("A", 52)], [("A", 104)], [("A", 104)], [("V", 52), ("A", 52)]]
+ARA = [(0, 0), (0, 0), (0, 0), (0, 0)]
 B, F, I, U = "bfloat16", "float32", "int32", "uint16"
-MN = {"C": 1.0, "C2": 1.0, "C512": 512.0, "L0": 0, "L1": 1, "L2": 2, "L3": 3, "FL": 10, "H0": 24, "H1": 7}
-IDN = {"p": 1.0, "n": -1.0, "h": 0.5, "nh": -0.5, "s1": 16384.0, "s2": 12288.0, "s3": 8192.0, "s4": 4096.0, "nf": 2.0 ** 23, "x16": 16.0, "m1": -4.0 * M1}
+MN = {"C": 1.0, "C2": 1.0, "CD": 1024.0, "L0": 0, "L1": 1, "L2": 2, "L3": 3, "H0": 24, "H1": 7}
+IDN = {"p": 1.0, "n": -1.0, "h": 0.5, "nh": -0.5, "s1": 16384.0, "s2": 12288.0, "s3": 8192.0, "s4": 4096.0, "x16": 16.0, "m1": -4.0 * M1}
 SB = {"X": ([X0[2] + XN], B), "LT": ([3 * LN], B), "Q": ([2 * (V + 16)], B), "MS": ([144 * len(MN)], B), "ID": ([128 * len(IDN)], B),
-      "KY": ([4, 64], F), "GO": ([2, 32], B), "ZP": ([2, 224], B), "ZQ": ([4, 144], B), "JW": ([8, 32], B), "RC": ([4, 65], F)}
-for _d, _s in ((B, "HI512 LO512 ZR1024 MK1536 SG768 MT16 OM144 BO512 BN128 PA192 ON256 KC128 QT512 D01024 D14096 D21664 RR4096 RL2048 "
-                   "RH1664 LW416 I1512 I2512 I3512 QS1024 LH512 WH96 S0768 S1768 S2768 S3768 G048 G148 G248 G348 N048 N148 N248 N348 LG4096 "
-                   "DT2048 MG1024 IN6144 DD2048 SS384 R1512 R2512 R3512 R4512 YY512 AB2048 XS2464 LS1664 G88 G98 HH128 BB64 NF64 AC64"),
-               (F, "IT144 IG128 II128 IF128 PS32 IS512 CX104 MM208 MF8 DM192 M216 CC224 T2224 TM208 T3224 TH32 Z1104 ZY104 Z2208 Z3104 NL104 TR104 "
-                   "WT144 RN128 ZS1024 K1128 DJ128 JS128 YN416 TA264 ZA64"),
-               (I, "NB512 SN96 SI144 PI8 LI8 WI144 JI128 JF128 JD256 K264 KD64"), (U, "SU288 BU96 UL208 UX104 WU48 JU1280")):
+      "ZP": ([2, 224], B), "ZQ": ([4, 144], B), "JW": ([8, 32], B), "RC": ([8, 66], F), "TB": ([8, 64], F)}
+for _d, _s in ((B, "ZR1024 MK1536 SG768 MT16 OM144 BO512 BN128 PA192 ON256 KC128 QT512 D01024 D14096 D21728 RR4096 RL2048 "
+                   "RH1728 LW416 I1512 I2512 I3512 QS1024 LH512 WH96 S0768 S1768 S2768 S3768 G048 G148 G248 G348 N048 N148 N248 N348 LG4096 "
+                   "DT2048 MG1024 IN6144 DD2048 SS384 R1512 R2512 R3512 R4512 YY512 AB2048 XS2464 LS1664 G88 G98 HH128 BB64 RK64 NI64"),
+               (F, "IT144 IG128 II128 IF128 PS32 IS512 CX104 MM208 MF8 DM64 M216 CC224 T2224 TM208 T3224 TH32 Z1104 ZY104 Z2208 Z3104 NL104 TR104 "
+                   "TL208 TX208 LC208 WT144 RN128 ZS1024 K164 KY128 YN416 VD128 LV128"),
+               (I, "NB1024 SN96 SI144 PI16 LI8 WI144 JI128 JF128 JD256 K264 KD64 VI96"), (U, "SU288 BU96 UL208 UX208 WU48 JU1280")):
     for _x in _s.split(): SB[_x[:2]] = ([int(_x[2:])], _d)
 SB = {k: ([128] + v[0], v[1]) for k, v in SB.items()}
 SCRATCH = {k: ("sbuf", v[0], v[1]) for k, v in SB.items()}
@@ -33,9 +36,8 @@ SEMAPHORES = ["eV", "eA", "eT", "eG", "loc"] + ["ar%d" % _i for _i in range(8)] 
 SZ = {B: 2, F: 4, I: 4, U: 2}
 S_ = slice(None)
 HP = [slice(0, 64), slice(64, 128)]
-FIGS = [(0.95, 1.56, 150.0), (0.85, 1.2, 150.0), (1.15, 1.9, 150.0)]
-DLAT, RLAT, LOOK, TRIES, NPERT, RUN, AMP, SEED = 1500.0, 2200.0, 100.0, 1500, 4, 12, 3000.0, 12345
-SHIFT = {"tail0": -20, "tail1": -20, "tail2": -10, "visits0": -20}
+FIGS = [(0.92, 1.56, 160.0, 1.0), (0.85, 1.25, 170.0, 1.1), (1.15, 1.85, 160.0, 1.0)]
+DLAT, FIRST, TRIES, RUN, AMP, WARM, SEED = 1500.0, 2500.0, 4000, 24, 3000.0, 200.0, 12345
 
 
 def shape_of(n):
@@ -116,8 +118,9 @@ def build():
         add("T", "mm", (out, terms, start, True), [x for t in terms for x in t] + ([] if start else [out]), [out],
             (0.0, sum(pc(l, r) for l, r in terms), 0), "open" if start and more else "new" if start else "add")
 
-    def mms(trip):
-        add("T", "mms", (trip,), [x for t in trip for x in t[1:]], [t[0] for t in trip], (0.0, sum(pc(l, r) for o, l, r in trip), 0), "new")
+    def mms(trip, start=True):
+        add("T", "mms", (trip, None, start, start), [x for t in trip for x in t[start:]], [t[0] for t in trip],
+            (0.0, sum(pc(l, r) for o, l, r in trip), 0), "new" if start else "add")
 
     def dma(pairs, after=()):
         by = sum(extent(o)[2] * extent(o)[3] * SZ[shape_of(o[0])[1]] for o, i in pairs)
@@ -125,11 +128,14 @@ def build():
         add("S", "dma", pairs, [i for o, i in pairs] + list(after), [o for o, i in pairs], (60.0 * len(pairs), 0, 0, by / 350.0 + 3.0 * rows))
 
     def send(src, dst, wid, back, sem, frees=()):
-        add("G", "send", (src, dst, wid, back, sem), [src], [ap("loc" + sem)] + list(frees), (500.0, 0, 0))
-        add("R" + sem, "arr", (sem,), [ap("loc" + sem)], [dst], (RLAT, 0, 0))
+        add("G", "send", (src, dst, wid, back, sem), [src], [ap("loc" + sem)] + list(frees), (500.0 + FIRST * (sem == "ar0"), 0, 0))
+        add("R" + sem, "arr", (sem,), [ap("loc" + sem)], [dst], (0.0, 0, 0, 600.0 + 4.0 * wid))
+
+    def const(out, v): iota(out, [[0, nel(out)]], v, 0)
+    def diag(x, j, v): add("G", "sel", (x, x, [[-1, nel(x)]], AL.not_equal, v, j, 1), [x], [x], (170.0, 2 * nel(x), 0))
 
     def fill(b, a, n):
-        for j in range(a, a + n, 512): iota(c(b, j, min(512, a + n - j)), [[0, min(512, a + n - j)]], 0, 0)
+        for j in range(a, a + n, 512): const(c(b, j, min(512, a + n - j)), 0)
 
     def P(b, a=0, n=512, p=S_, step=1): return ap("ps%d" % b, p, slice(a, a + n * step - step + 1, step))
     def c(b, a, n, p=S_): return ap(b, p, slice(a, a + n))
@@ -143,21 +149,23 @@ def build():
     pp, nn, hp, hn = idm("p"), idm("n"), idm("h"), idm("nh")
     eq, mu, ad, su, mx = AL.is_equal, AL.mult, AL.add, AL.subtract, AL.max
     sh, an = AL.arith_shift_right, AL.bitwise_and
-    H64, H96 = slice(0, 64), slice(0, 96)
+    H54, H64, H96 = slice(0, 54), slice(0, 64), slice(0, 96)
 
     def load(s):
-        rows = slice(64 * s, 64 * s + 64)
-        dma([(ap("NB"), ap("nb", slice(4 * s, 4 * s + 4), S_))])
-        dma([(c("X", X0[s], V, HP[h]), ap("xv", rows, S_)) for h in range(2)])
+        rows, nb = slice(64 * s, 64 * s + 64), c("NB", 512 * s, 512)
+        dma([(nb, ap("nb", slice(4 * s, 4 * s + 4), S_))])
+        for j in range(2):
+            dma([(c("X", X0[s] + HV * (h ^ j), HV, HP[h]), ap("xv", rows, slice(HV * (h ^ j), HV * (h ^ j) + HV))) for h in range(2)])
         dma([(c("SN", 48 * s, 48, HP[h]), ap("snd", rows, S_)) for h in range(2)])
         if s: fill("LT", L0[s], W)
         else:
             for j in range(4): act(c("LT", L0[s] + 1024 * j, 1024), ap("ZR"), AF.Copy)
-        ts(ap("HI"), ap("NB"), M64, ad, M64, su)
-        tt(ap("LO"), ap("NB"), ap("HI"), su)
-        for j, b in enumerate(("HI", "LO")):
-            dma([(ap("LT", slice(64 * h + j, 64 * h + 64, 4), slice(L0[s], L0[s] + W)), ap(b)) for h in range(2)])
-        dma([(c("Q", (V + 16) * s, V, HP[h]), ap("cq", rows, S_)) for h in range(2)], [ap("LO")])
+        hi, lo = c("DD", 1024 * s, 512), c("DD", 1024 * s + 512, 512)
+        ts(hi, nb, M64, ad, M64, su)
+        tt(lo, nb, hi, su)
+        for j, b in enumerate((hi, lo)):
+            dma([(ap("LT", slice(64 * h + j, 64 * h + 64, 4), slice(L0[s], L0[s] + W)), b) for h in range(2)])
+        dma([(c("Q", (V + 16) * s, V, HP[h]), ap("cq", rows, S_)) for h in range(2)])
         ts(c("SI", 0, 48), c("SN", 48 * s, 48), W - 1, an)
         ts(c("SI", 48, 48), c("SN", 48 * s, 48), 12, sh)
         ts(c("SI", 96, 48), c("SI", 0, 48), float(HV), AL.is_ge, 4.0, mu)
@@ -179,25 +187,28 @@ def build():
     ms(ap("ZR"), 0.0)
     p0 = c("PI", 0, 1)
     for j, (o, s) in enumerate([(sh, 4), (an, 15), (sh, 1), (an, 1), (an, 3), (sh, 2), (sh, 6)]): ts(c("PI", j + 1, 1), p0, s, o)
-    cp(c("PS", 0, 8), ap("PI"))
-    ts(ps(8), ps(7), -4.0, mu, ps(1), ad)
+    cp(c("PS", 0, 8), c("PI", 0, 8))
+    ts(c("PI", 8, 1), p0, 31, an)
+    cp(ps(25), c("PI", 8, 1))
+    for j in range(2): ts(c("RK", 32 * j, 32), c("IT", 0, 32), ps(25), eq)
+    def lin(j, i, a, b): act(ps(j), ps(i), AF.Identity, b, a)
+    lin(8, 7, -4.0, ps(1))
     ts(ps(9), ps(5), 2.0, AL.is_lt)
-    ts(ps(10), ps(2), 2.0, eq)
-    ts(ps(11), ps(4), -1.0, mu, 1.0, ad)
+    lin(11, 4, -1.0, 1.0)
     ts(ps(12), ps(2), 13.0, AL.min)
-    ts(ps(13), ps(1), -4.0, mu, ps(6), ad)
-    ts(ps(14), ps(7), -float(HS), mu, W + HS - 1.0, ad)
-    ts(ps(15), ps(1), -16.0, mu)
-    ts(ps(16), ps(7), float(HV), mu, ps(15), ad)
-    ts(ps(17), ps(6), 8.0, mu, 3.0, ad)
-    ts(ps(18), ps(7), -124.0, mu, ps(17), ad)
-    ts(ps(19), ps(7), float(HS), mu)
+    lin(13, 1, -4.0, ps(6))
+    lin(14, 7, -float(HS), W + HS - 1.0)
+    lin(15, 1, -16.0, 0.0)
+    lin(16, 7, float(HV), ps(15))
+    lin(17, 6, 8.0, 3.0)
+    lin(18, 7, -124.0, ps(17))
+    lin(19, 7, float(HS), 0.0)
     act(ap("IS"), ap("IS"), AF.Identity, bias=ps(19))
-    ts(ps(20), ps(7), -float(HV), mu)
-    ts(ps(21), ps(7), 4.0, mu, ps(13), ad)
-    ts(ps(22), ps(7), 8192.0, mu, float(HV), ad)
-    ts(ps(23), ps(20), 16.0, ad)
-    ts(ps(24), ps(7), 0.0, eq)
+    lin(20, 7, -float(HV), 0.0)
+    lin(21, 7, 4.0, ps(13))
+    lin(22, 7, 8192.0, float(HV))
+    lin(23, 7, -float(HV), 16.0)
+    lin(24, 7, -1.0, 1.0)
     ts(ap("G8"), c("IT", 0, 8), ps(1), eq)
     ts(ap("G9"), ap("IG", S_, slice(0, 128, 16)), ps(8), eq)
     ts(ap("MT"), c("IT", 0, 16), ps(21), eq, ps(9), mu)
@@ -207,10 +218,6 @@ def build():
     for j, m in enumerate(MN):
         act(ap("MS", S_, slice(144 * j + 15, 144 * j + 143, 16)), ap("G9" if m == "C2" else "G8"), AF.Identity,
             scale=ps(MN[m]) if m[0] in "FH" else c("MF", MN[m], 1) if m[0] == "L" else MN[m])
-    ts(c("HH", 0, 64), c("IT", 0, 64), ps(0), eq)
-    ts(c("HH", 64, 64), c("IT", 64, 64), ps(0), eq)
-    tt(c("HH", 0, 64), c("HH", 0, 64), c("HH", 64, 64), ad)
-    cp(c("HH", 64, 64), c("HH", 0, 64))
     ts(pp, c("IT", 0, 128), ps(0), eq)
     for m in list(IDN)[1:]:
         if m != "m1" or "A" in RND: act(idm(m), pp, AF.Identity, scale=IDN[m])
@@ -222,36 +229,31 @@ def build():
         tt(c("BO", 256 + 128 * h, 128), c("BO", 128 * h, 128), ap("BN"), mu)
     ts(c("PA", 0, 32), c("IT", 0, 32), ps(3), eq, ps(11), mu)
     ts(c("PA", 32, 32), c("IT", 0, 32), ps(3), eq, ps(4), mu)
-    for j in range(4): ts(c("PA", 64 + 32 * j, 32), c("IT", 0, 32), ps(6), eq, c("MF", 4 + j, 1), mu)
-    ts(c("DM", 0, 64), c("IT", 0, 64), ps(0), eq, 8192.0, mu)
-    ts(c("DM", 64, 64), c("IT", 1, 64), ps(0), eq, -16384.0, mu)
-    ts(c("DM", 128, 64), c("IT", 2, 64), ps(0), eq, 8192.0, mu)
-    tt(c("DM", 0, 64), c("DM", 0, 64), c("DM", 64, 64), ad)
-    tt(c("DM", 0, 64), c("DM", 0, 64), c("DM", 128, 64), ad)
-    act(c("DM", 64, 64), c("DM", 0, 64), AF.Identity, scale=-1.0)
+    lin(26, 8, 8.0, ps(21))
+    for j in range(4): ts(c("PA", 64 + 32 * j, 32), c("IT", 0, 32), ps(26), eq, c("MF", 4 + j, 1), mu)
     ts(ap("M2"), c("IT", 0, 16), ps(12), eq)
     ts(ap("MM"), ap("MM"), ps(2), eq)
-    ts(ap("CX"), ap("CX"), ps(16), ad)
-    ms(ap("ON"), 1.0)
-    ms(ap("QT"), -0.25)
-    ms(ap("D0"), -1.0)
+    act(ap("CX"), ap("CX"), AF.Identity, ps(16))
+    act(ap("QT"), c("ZR", 0, 512), AF.Identity, -0.25)
     ms(c("TH", 14, 1), -0.5)
-    for b in range(4): ms(c("X", XN * b, 16), -64.0)
-    for s in range(2):
-        ms(c("XS", (16 + HV + GH) * s, 16), 0.0)
-        ms(c("Q", (V + 16) * s + V, 16), 1000.0)
-    for b in ("CC", "T2", "T3"): ms(c(b, NC, 16), 8192.0)
-    ms(ap("ZP"), 0.0); ms(ap("ZQ"), 0.0)
-    ms(ap("RC", S_, S_, 64), 0.0); ms(c("TA", 256, 8), 0.0); ms(ap("ZA"), 0.0)
-    for ph in range(4): ms(c("G%d" % ph, 0, 48, HP[1]), 0.0)
+    const(ap("ON"), 1)
+    for b in ("CC", "T2", "T3"): const(c(b, NC, 16), 8192)
+    for b in range(4): const(c("X", XN * b, 16), -64)
+    for s in range(2): const(c("Q", (V + 16) * s + V, 16), 1000)
     load(0)
-    fill("D1", 0, 4096); fill("D2", 0, 1664)
+    stage[0] = "fill"
+    for s in range(2): const(c("XS", (16 + HV + GH) * s, 16), 0)
+    for b in ("ZP", "ZQ", "G0", "G1", "G2", "G3", "DM", "HH"): const(ap(b), 0)
+    const(ap("RC", S_, S_, slice(64, 66)), 0)
+    iota(ap("NI"), [[-1, 64]], 0, 0)
+    for j in range(2): const(c("D0", 512 * j, 512), -1)
+    const(ap("TB"), 0)
+    for h in range(2):
+        if h: add("G", "sel", (ap("DM"), ap("DM"), [[0, 64]], AL.is_gt, 0.0, 64, -1), [ap("DM")], [ap("DM")], (170.0, 128, 0))
+        for j, v in enumerate((8192.0, -16384.0, 8192.0)): diag(ap("DM"), -j - 64 * h, v)
+    for j in (-64, 0, 64): diag(ap("HH"), j, 1.0)
+    fill("D1", 0, 4096); fill("D2", 0, 1728)
     for b in range(3): fill("X", X0[b] + W, NEW); fill("LT", L0[b] + W, NEW)
-
-    def low(out, x):
-        ts(out, x, 63, an)
-        ts(out, out, 65.0, mu)
-        ts(out, out, 4, sh, 63, an)
 
     def head(ph):
         s, r, b, par = ph % 2, ph // 2, ph % 3, ph % 2
@@ -276,7 +278,7 @@ def build():
         send(ap("S%d" % ph), c("X", xo + V, GH), 256, False, "ar%d" % (2 * ph))
         cp(c("WI", 0, 48), c("WT", 48, 48))
         ts(c("WI", 48, 48), c("WI", 0, 48), 6, sh)
-        low(c("WI", 96, 48), c("WI", 0, 48))
+        ts(c("WI", 96, 48), c("WI", 0, 48), 63, an)
         ts(c("WH", 48 * par, 48), c("WI", 48, 48), 1.0, ad, 0.0, mx)
         ts(ap("ZQ", S_, 2 * par + 1, slice(48, 96)), c("WI", 96, 48), 1.0, ad)
         mms([(P(mb, HC * j, HC), c("BO", 128 * j, 128), Lw) for j in range(4)])
@@ -299,16 +301,18 @@ def build():
         cp(c("BU", 64, 32), P(2, 448, 32))
         act(ap("LH"), ind(lw, c("BU", 64, 32)), AF.Copy)
         act(c("QS", HS * par, HS), ind(c("Q", (V + 16) * s, V + 16), c("BU", 64, 32)), AF.Copy)
-        for h in range(2):
-            t3 = c("T3", HC * h, HC, HP[h])
-            ts(c("Z1", 0, HC, HP[h]), t3, SL + 0.5, AL.is_le)
-            act(c("ZY", 0, HC, HP[h]), t3, AF.Identity, bias=ps(14, HP[h]))
-        z2 = c("Z2", HC * par, HC)
-        tt(ap("Z1"), ap("Z1"), Lw, mu)
-        tt(z2, ap("ZY"), ap("Z1"), mu)
-        tt(ap("Z1"), z2, ap("CX"), mx)
-        cp(c("UL", HC * par, HC), ap("Z1"))
+        for h in range(2): act(c("ZY", 0, HC, HP[h]), c("T3", HC * h, HC, HP[h]), AF.Identity, bias=ps(14, HP[h]))
+        tt(ap("Z1"), ap("ZY"), Lw, mu)
+        tt(c("TL", HC * par, HC), ap("Z1"), ap("CX"), mx)
+        act(ap("ZY"), Lw, AF.Identity, bias=float(W + NEW), scale=-float(W + NEW))
+        tt(c("TX", HC * par, HC), ap("ZY"), ap("Z1"), mx)
+        if r == 0: tt(c("LC", HC * par, HC), ap("ZY"), ap("CX"), mx)
+        cp(c("VI", 0, 32), P(2, 448, 32))
+        ts(c("VI", 32, 32), c("VI", 0, 32), 6, sh)
+        ts(c("VI", 64, 32), c("VI", 0, 32), 63, an)
+        ts(c("VD", 64 * par, 64), c("VI", 32, 64), 1.0, ad)
         for k in range(4): mm(z(ph, 1, k, 32), wrap("L%d" % k, "LH", 0, 32))
+        stage[0] = "links%d" % ph
         for t in range(1, 5):
             for k in (0, 2): cp(ju(ph, t, k, 64), z(ph, t, k, 64))
             act(zs(ph, t), z(ph, t), AF.Copy)
@@ -330,7 +334,7 @@ def build():
         red(c("TH", 17, 1), P(7, 0, HC), False)
         cp(c("LI", 0, 1), c("TH", 17, 1))
         ts(c("LI", 1, 1), c("LI", 0, 1), 7, an)
-        ts(c("TH", 18 + r, 1), c("LI", 1, 1), 161.0, ad, 512.0, mu)
+        ts(c("TH", 18 + r, 1), c("LI", 1, 1), 160.5, ad, 1024.0, mu)
 
     def visits(ph):
         xw, qs = c("X", X0[ph % 3], W), c("QS", HS * (ph % 2), HS)
@@ -360,22 +364,26 @@ def build():
         xw, qs = c("X", xo, W), c("QS", HS * par, HS)
         m = [c("DD", 512 * k, 512) for k in range(4)]
         R1, R2, R3, R4, Y = (ap(x) for x in ("R1", "R2", "R3", "R4", "YY"))
+
+        def relu(j, out, x):
+            if REL[ph][j] == "A": act(out, x, AF.Relu)
+            else: ts(out, x, 0.0, mx)
+
         for k in range(4):
             if FIN[ph][k] == "A": act(m[k], ind(xw, ju(ph, 5, k, 32)), AF.Copy)
             else: cp(m[k], ind(xw, ju(ph, 5, k, 32)))
         ts(c("JD", 0, 128), ap("JF"), 6, sh)
-        low(c("JD", 128, 128), ap("JF"))
-        tt(ap("DJ"), ap("JF"), zs(ph, 1), su)
+        ts(c("JD", 128, 128), ap("JF"), 63, an)
         mm(P(4), [(pp, m[0]), (nn, m[1])])
-        act(R1, P(4), AF.Relu)
+        relu(0, R1, P(4))
         mm(P(5), [(pp, m[2]), (nn, m[3])])
-        act(R2, P(5), AF.Relu)
+        relu(1, R2, P(5))
         mm(P(par), [(pp, m[1]), (nn, m[3])], True, True)
         mm(P(par), [(pp, R1), (nn, R2)], False)
-        act(R3, P(par), AF.Relu)
+        relu(2, R3, P(par))
         mm(P(4), [(pp, m[0]), (nn, R1), (nn, m[2])], True, True)
         mm(P(4), [(pp, R2)], False)
-        act(R4, P(4), AF.Relu)
+        relu(3, R4, P(4))
         mm(P(5), [(pp, ap("QT")), (hp, m[1]), (hp, m[2]), (hp, R1), (hn, R2)], True, True)
         mm(P(5), [(hn, R3)], False)
         mm(P(5), [(hp, R4)] + [(idm("m1"), ap("QT"))] * (RND[ph] == "A"), False)
@@ -384,30 +392,32 @@ def build():
         for k in range(4):
             mm(P(3), [(pp, m[k]), (nn, qs)])
             ts(c("IN", 4096 + 512 * k, 512), P(3), M32, ad, M32, eq)
-        count(4096, AF.Relu, c("SS", 256, 128), 8.5, -1.0)
+        count(4096, AF.Sign, c("SS", 256, 128), 8.5, -1.0)
         for k in range(4):
-            bk = P((par, 4, 3, 5)[k])
+            bk = P((par, 4, 5, par)[k])
             mm(bk, [(pp, m[k])], True, True)
             mm(bk, [(nn, Y)], False)
             act(c("AB", 512 * k, 512), bk, AF.Abs)
-        D = P(6 + par, 0, 128)
-        mm(D, [(pp, ap("KC")), (pp, c("ON", 0, 128)), (c("SS", 256, 128), idm("nf"))], True, True)
-        for k in (0, 2): mm(P(6 + par, 32 * k, 64), wrap("C512", "AB", 512 * k, 64), False, True)
-        for dg in range(2): tt(ap("KY", S_, S_, slice(32 * dg, 32 * dg + 32)), D, c("JD", 128 * dg, 128), ad)
-        tt(ap("K1"), ap("KY", S_, slice(0, 2), S_), ap("KY", S_, slice(2, 4), S_), mx)
-        tt(ap("K2"), c("K1", 0, 64), c("K1", 64, 64), mx)
+        D, nf = P(6 + par, 0, 128), P(2, 384, 64)
+        mm(nf, [(c("SS", 256, 128), ap("RK"))])
+        ts(c("LV", 0, 64), nf, -3.5, AL.is_gt, 2.0 ** 30, mu)
+        ts(c("LV", 64, 64), c("VD", 64 * par, 64), c("TH", 18 + ph // 2, 1), ad)
+        tt(c("LV", 0, 64), c("LV", 0, 64), c("LV", 64, 64), ad)
+        mm(D, [(pp, ap("KC")), (pp, c("ON", 0, 128))], True, True)
+        for k in (0, 2): mm(P(6 + par, 32 * k, 64), wrap("CD", "AB", 512 * k, 64), False, True)
+        for dg in range(2):
+            tt(P(6 + par, 256 + 64 * dg, 64), P(6 + par, 0, 64), c("JD", 128 * dg, 64), ad)
+            tt(c("KY", 64 * dg, 64), P(6 + par, 64, 64), c("JD", 128 * dg + 64, 64), ad)
+        tt(P(6 + par, 0, 128), P(6 + par, 256, 128), ap("KY"), mx)
+        for dg in range(2): tt(c("K1", 32 * dg, 32), P(6 + par, 64 * dg, 32), c("LV", 32 * dg, 32), mx)
+        for dg in range(2): tt(c("K2", 32 * dg, 32), P(6 + par, 64 * dg + 32, 32), c("K1", 32 * dg, 32), mx)
         ts(ap("KD"), ap("K2"), 127, an)
-        ts(ap("GO"), ap("K2"), c("TH", 18 + ph // 2, 1), AL.is_lt)
-        ts(ap("NF"), ap("K2"), 2.0 ** 22, AL.is_lt)
-        tt(ap("AC"), ap("NF"), ap("GO"), su)
-        tt(ap("ZP", S_, S_, slice(96, 128)), ap("KD"), ap("AC"), mu)
-        for j in range(2): tt(c("JS", 64 * j, 64), c("DJ", 64 * j, 64), ap("GO"), mu)
-        tt(ap("JS"), ap("JS"), zs(ph, 1), ad)
+        cp(ap("ZP", S_, S_, slice(96, 128)), ap("KD"))
         jh, jl = (ap("JW", S_, slice(4 * j, 4 * j + 4), S_) for j in range(2))
-        ts(jh, ap("JS"), M64, ad, M64, su)
-        tt(jl, ap("JS"), jh, su)
+        ts(jh, ap("JF"), M64, ad, M64, su)
+        tt(jl, ap("JF"), jh, su)
         jrow = lambda j: ap("LT", slice(j, 128, 16), slice(lo + W + HS, lo + W + 2 * HS))
-        dma([(jrow(2), ap("GO", S_, 0, S_))] + [(jrow(4 * (j % 4) + j // 4), ap("JW", S_, j, S_)) for j in range(8)])
+        dma([(jrow(4 * (j % 4) + j // 4), ap("JW", S_, j, S_)) for j in range(8)])
         mms([(P(5, 32 * i, 32), pp, ap("YY", S_, slice(i, HS, 16))) for i in range(16)])
         act(c("X", xo + W + HS, HS), P(5), AF.Copy)
         for b, o in (("X", xo), ("LT", lo)):
@@ -416,14 +426,28 @@ def build():
     def ramps(out, ro, d, do, n, p):
         scan(c(out, ro, n, p), c("D0", 0, n, p), c(d, do, n, p), ad, mx)
 
-    def steps(b):
-        act(ap("RC", H64, S_, H64), P(b, 0, 256, H64), AF.Copy)
-        tt(c("TA", 0, 256, H64), P(b, 0, 256, H64), ap("RC", H64, S_, slice(1, 65)), su)
-        cp(ap("ZA", H64, slice(15, 63, 16)), ap("TA", H64, slice(64, 256, 64)))
+    def slopes(out, d, wid, n, na, p):
+        for a in range(0, n - na, 16): ramps(out, wid * a, d, wid * a, wid * min(16, n - na - a), p)
+        for j in range(n - na, n): act(c(out, wid * j, wid, p), c("NI", 0, wid, p), AF.Relu, c(d, wid * j, 1, p))
 
-    def cells(e, a, n):
-        return ([(ap("TA", H64, slice(e + j, 253 + e + j, 4)), c("DM", 64 * j + a, n, H64)) for j in range(2)]
-                + [(ap("ZA", H64, S_), c("DM", a, n, H64))] * (e == 3))
+    def sums(b, q, n): return P(b, 64 * (q % 2), 64, slice(64 * (q // 2), 64 * (q // 2) + n))
+
+    def steps(b):
+        act(ap("RC", S_, slice(4 * b, 4 * b + 2), H64), P(b, 0, 128), AF.Identity, 0.0, -2.0)
+        act(ap("RC", S_, slice(4 * b + 2, 4 * b + 4), H64), P(b, 0, 128), AF.Copy)
+        tt(P(b, 128, 128), P(b, 0, 128), ap("RC", S_, slice(4 * b, 4 * b + 2), slice(1, 65)), ad)
+        for q in range(4):
+            p = HP[q // 2]
+            tt(ap("TB", p, slice(4 * b, 4 * b + 4), slice(16 * q, 16 * q + 16)), P(b, 128 + 64 * (q % 2), 64, p), ap("RC", p, 4 * b + 2 + q % 2, slice(2, 66)), ad)
+
+    def cells(b, o, h, a, n):
+        return [(P(6 + b, o + e, n, HP[h], 4), ap("TB", S_, 4 * b + e, S_), c("DM", a, n)) for e in range(4)]
+
+    def marks(b, a, x):
+        mm(P(6 + b, a, HC), [(c("ZR", 0, 128), c("ZR", 0, HC))], True, True)
+        for h in range(2): mms(cells(b, a, h, 26 * h, 26), False)
+        mm(P(6 + b, a, HC), [(ap("IF"), x)], False)
+        return P(6 + b, a, HC)
 
     def notices(par, dg, o):
         zq = lambda a: ap("ZQ", H64, 2 * par + dg, slice(a, a + 96))
@@ -436,57 +460,49 @@ def build():
         for dg in range(2):
             mm(P(mb, 128 + 32 * dg, 32), [(ap("ZP", S_, dg, slice(96 - 32 * j, 224 - 32 * j)), c("PA", 64 + 32 * j, 32)) for j in range(4)])
         cp(ap("D1", S_, slice(0, W, 64)), P(mb, 128, 64))
-        mm(P(par, 0, 256, H64), [(c("ZR", 0, 64), c("ZR", 0, 256))], True, True)
-        for h in range(2):
-            for dg in range(2): ramps("RR", 2048 * dg + 1024 * h, "D1", 2048 * dg + 1024 * h, 1024, S_)
-            for q in range(4):
-                mm(P(par, 64 * q, 64, H64), [(c("RR", 64 * j, 64), c("RR", 2048 + 64 * j, 64)) for j in range(16 * h + 4 * q, 16 * h + 4 * q + 4)], False)
+        slopes("RR", "D1", 64, 64, ARA[ph][0], S_)
+        for q in range(4): mm(sums(par, q, 64), [(c("RR", 64 * j, 64), c("RR", 2048 + 64 * j, 64)) for j in range(8 * q, 8 * q + 8)])
         steps(par)
-        for e in range(4): mm(P(mb, 192 + e, 12, H64, 4), cells(e, 52, 12))
+        mms(cells(par, 192, 0, 52, 12))
         ts(c("G%d" % ph, 0, 48, H64), P(mb, 192, 48, H64), 0.5, AL.is_gt)
         send(ap("G%d" % ph), ap("N%d" % ph), 16, True, "ar%d" % (2 * ph + 1), [c("X", X0[0] + V, GH)] * (ph == 1))
-        mm(P(par, 0, 256, H64), [(c("IF", 0, 64, H64), ap("RC", H64, S_, H64))], True, True)
         notices(par, 1, 240)
         cp(ap("D1", H96, slice(0, 2048, 64)), P(mb, 240, 32, H96))
         for q in range(2): ramps("RL", 1024 * q, "D1", 1024 * q, 1024, H96)
-        act(ap("LS"), ind(c("LT", lo, LN), c("UL", HC * par, HC)), AF.Copy)
-        mm(P(mb, 408, HC), wrap("FL", "LS", 0, HC))
-        tt(ap("Z3"), P(mb, 408, HC), c("Z2", HC * par, HC), mu)
+        fo = marks(par, 408, ap("CX"))
+        z2, ul, (ls, l0), (xs, x0) = c("Z2", HC * par, HC), c("UL", HC * par, HC), *((("LS", 0), ("XS", 16)) if ph < 3 else (("LG", 0), ("LG", 2048)))
+        tt(ap("Z3"), fo, c("TL", HC * par, HC), AL.min)
+        cp(ul, ap("Z3"))
+        tt(z2, fo, c("TX", HC * par, HC), AL.min)
+        act(c(ls, l0, HV), ind(c("LT", lo, LN), ul), AF.Copy)
         if r == 0:
             dma([(c("LT", ln + HV * h, HV, HP[j]), c("LS", 0, HV, HP[h])) for h in range(2) for j in range(2)])
             dma([(c("LT", ln + V, GH), c("LT", lo + V, GH))])
             dma([(c("XS", 16 + HV, GH), c("X", xo + V, GH))])
-            tt(ap("NL"), ap("Z3"), c("LW", HC * ph, HC), AL.is_lt)
+            tt(ap("NL"), z2, c("LC", HC * par, HC), eq)
             act(ap("TR"), ap("NL"), AF.Identity, bias=8000.0, scale=-9000.0)
-        tt(ap("Z3"), ap("Z3"), ap("CX"), mx)
         tt(ap("ZQ", H64, 2 * par, slice(48, 96)), c("N%d" % ph, 0, 48, H64), c("WH", 48 * par, 48, H64), mu)
         notices(par, 0, 272)
-        cp(ap("D2", H96, slice(0, 1664, 52)), P(mb, 272, 32, H96))
-        for q in range(2):
-            ramps("RH", 832 * q, "D2", 832 * q, 832, H96)
-            for u in (2 * q, 2 * q + 1):
-                mm(P(par, 64 * u, 64, slice(0, 52)), [(c("RH", 52 * j, 52, H96), c("RL", 64 * j, 64, H96)) for j in range(8 * u, 8 * u + 8)], False)
+        cp(ap("D2", H96, slice(0, 1728, 54)), P(mb, 272, 32, H96))
+        slopes("RH", "D2", 54, 32, ARA[ph][1], H96)
+        for q in range(4): mm(sums(par, q, 54), [(c("RH", 54 * j, 54, H96), c("RL", 64 * j, 64, H96)) for j in range(8 * q, 8 * q + 8)])
         steps(par)
-        fa = P(mb, 304, HC)
-        mm(fa, [(c("ZR", 0, 128), c("ZR", 0, HC))], True, True)
-        for h in range(2):
-            for e in range(4): mm(P(mb, 304 + e, 26, HP[h], 4), cells(e, 26 * h, 26), False, True)
-        mm(fa, [(ap("IF"), ap("Z3"))], False, True)
-        ts(ap("UX"), fa, float(W + NEW), AL.min)
+        fa = marks(par, 304, z2)
+        ts(c("UX", HC * par, HC), fa, float(W + NEW), AL.min)
         if r == 0: tt(c("LW", HC * (ph + 2), HC), fa, ap("TR"), AL.is_gt)
         else:
             yb = 5 if ph == 3 else par
-            mm(P(yb, 0, 416), [(c("OM", 3 - e, 128), c("LS", 416 * e, 416)) for e in range(4)])
+            mm(P(yb, 0, 416), [(c("OM", 3 - e, 128), c(ls, l0 + 416 * e, 416)) for e in range(4)])
             act(ap("YN"), P(yb, 0, 416), AF.Copy)
             dma([(ap("yn", slice(4 * s, 4 * s + 4), S_), ap("YN"))])
         a = 0
         for e, n in XUP[ph]:
-            o, x = c("XS", 16 + 16 * a, 16 * n), ind(c("X", xo, XN), c("UX", a, n))
+            o, x = c(xs, x0 + 16 * a, 16 * n), ind(c("X", xo, XN), c("UX", HC * par + a, n))
             if e == "A": act(o, x, AF.Copy)
             else: cp(o, x)
-            xs = [c("XS", 16 + 16 * a, 16 * n, HP[h]) for h in range(2)]
-            if r == 0: dma([(c("X", xn + HV * h + 16 * a, 16 * n, HP[j]), xs[h]) for h in range(2) for j in range(2)])
-            else: dma([(ap("yx", slice(64 * s, 64 * s + 64), slice(HV * h + 16 * a, HV * h + 16 * (a + n))), xs[h]) for h in range(2)])
+            o = [c(xs, x0 + 16 * a, 16 * n, HP[h]) for h in range(2)]
+            if r == 0: dma([(c("X", xn + HV * h + 16 * a, 16 * n, HP[j]), o[h]) for h in range(2) for j in range(2)])
+            else: dma([(ap("yx", slice(64 * s, 64 * s + 64), slice(HV * h + 16 * a, HV * h + 16 * (a + n))), o[h]) for h in range(2)])
             a += n
 
     todo = [(head, 0), (load, 1), (limit, 0), (head, 1), (visits, 0), (verdict, 0)]
@@ -502,14 +518,17 @@ def depend(ops):
     last, news, adds, opened = {}, {}, {}, {}
     for i, o in enumerate(ops):
         dep = set()
-        if o["s"]:
-            bk = list(o["w"])[0][0]
+        o["b"] = sorted({x[0] for x in list(o["r"]) + list(o["w"]) if x[0][:2] == "ps"})
+        for bk in o["b"] if o["s"] else []:
             if o["s"] != "add": dep.update(adds.get(bk, []))
-            if o["s"] == "open": dep.update(news.get(bk, [])); opened[bk] = i
+            if o["s"] == "open": dep.update(news.get(bk, [])); opened[bk] = i; news[bk] = []; adds[bk] = []
             o["sum"] = opened.get(bk)
             (adds if o["s"] == "add" else news).setdefault(bk, []).append(i)
         for (nm, pm), m in o["r"].items():
             dep.update(x[0] for x in last.get(nm, []) if x[3] and x[1] & m and x[2] & pm)
+        if not o["s"]:
+            for j in list(dep):
+                if ops[j]["s"] in ("open", "add"): dep.update(x for x in adds.get(ops[j]["b"][0], []) if ops[x]["sum"] == ops[j]["sum"])
         for (nm, pm), m in o["w"].items():
             dep.update(x[0] for x in last.get(nm, []) if x[1] & m and x[2] & pm)
             last[nm] = [x for x in last.get(nm, []) if x[1] & ~m or x[2] & ~pm]
@@ -517,143 +536,130 @@ def depend(ops):
             for (nm, pm), m in o[key].items(): last.setdefault(nm, []).append((i, m, pm, w))
         dep.discard(i)
         o["d"] = sorted(dep)
-        o["b"] = sorted({x[0] for x in list(o["r"]) + list(o["w"]) if x[0][:2] == "ps"})
+        o["p"] = [(j, not ops[j]["e"] == o["e"] == "T") for j in o["d"]]
 
 
 def span(ops, seq, fig, tm=None):
-    cy, ga, lat = fig
-    free, bank, fin, pipe = {}, {}, {}, 0.0
+    cy, ga, lat, dm = fig
+    free, bank, fin, pipe = {}, {}, [0.0] * len(ops), 0.0
     for i in seq:
-        o = ops[i]; e = o["e"]
+        o = ops[i]; e = o["e"]; c = o["c"]
         s = free.get(e, 0.0)
-        for j in o["d"]:
-            y = fin[j] + (0.0 if ops[j]["e"] == e == "T" else lat)
+        for j, far in o["p"]:
+            y = fin[j] + far * lat
             if y > s: s = y
         for b in o["b"]:
-            for e2, y in bank.setdefault(b, {}).items():
-                if e2 != e and y + lat > s: s = y + lat
-        c = price(o, cy, ga)
-        free[e] = fin[i] = s + c
-        if o["k"] == "dma": pipe = fin[i] = max(pipe, s + c + DLAT) + o["c"][3]
-        for b in o["b"]: bank[b][e] = fin[i]
-        if tm is not None: tm[i] = (s, fin[i])
-    return max(fin.values())
+            e2, y = bank.get(b, (e, 0.0))
+            if e2 != e and y + lat > s: s = y + lat
+        free[e] = y = s + c[0] + cy * (c[1] + ga * c[2])
+        if len(c) > 3: pipe = y = max(pipe, y + dm * DLAT) + dm * c[3]
+        fin[i] = y
+        for b in o["b"]: bank[b] = (e, y)
+        if tm is not None: tm[i] = (s, y)
+    return max(fin)
 
 
 def order(ops):
     depend(ops)
     n = len(ops)
-    cy, ga, lat = FIGS[0]
+    cy, ga, lat, dm = FIGS[0]
     succ = [[] for _ in ops]
     for i, o in enumerate(ops):
         for j in o["d"]: succ[j].append(i)
     cost = [price(o, cy, ga) for o in ops]
-    full = [cost[i] + (o["c"][3] + DLAT if o["k"] == "dma" else 0.0) for i, o in enumerate(ops)]
+    full = [cost[i] + (dm * (o["c"][3] + DLAT) if len(o["c"]) > 3 else 0.0) for i, o in enumerate(ops)]
     eng = [o["e"] for o in ops]
     pred = [o["d"] for o in ops]
 
     def place(key, back):
-        pre, suc = (succ, pred) if back else (pred, succ)
-        left = [len(p) for p in pre]
-        ready = sorted((key[i], i) for i in range(n) if left[i] == 0)
-        line, st = {}, [0.0] * n
+        suc, left = after[back], list(count[back])
+        ready = sorted(((key[i], i) for i in range(n) if left[i] == 0), reverse=True)
+        line, st = {r: [] for r in names}, [0.0] * n
         while ready:
-            i = ready.pop(0)[1]; e = eng[i]
-            s = max([st[j] + full[j] + (0.0 if eng[j] == e == "T" else lat) for j in pre[i]], default=0.0)
-            use = [(e, 0.0, cost[i], 0.0)] + [(b, 0.0, cost[i], lat) for b in ops[i]["b"]]
-            if full[i] > cost[i]: use.append(("D", cost[i] + DLAT, full[i], 0.0))
-            if back: use = [(r, full[i] - z, full[i] - a, p) for r, a, z, p in use]
+            i = ready.pop()[1]; e = eng[i]; s = st[i]; use = uses[back][i]
             moved = True
             while moved:
                 moved = False
                 for r, a, z, p in use:
-                    ln = line.setdefault(r, [])
-                    lo, hi = 0, len(ln)
+                    ln = line[r]; m = len(ln)
+                    if not m or ln[-1][1] + p <= s + a: continue
+                    lo, hi = 0, m
                     while lo < hi:
                         mid = (lo + hi) // 2
                         if ln[mid][1] + p <= s + a: lo = mid + 1
                         else: hi = mid
-                    while lo < len(ln) and ln[lo][0] < s + z + p:
-                        q = 0.0 if ln[lo][2] == e else p
-                        if ln[lo][0] < s + z + q - 1e-6 and ln[lo][1] + q > s + a + 1e-6: s = ln[lo][1] + q - a; moved = True
+                    while lo < m:
+                        x = ln[lo]
+                        if x[0] >= s + z + p: break
+                        q = 0.0 if x[2] == e else p
+                        if x[0] < s + z + q - 1e-6 and x[1] + q > s + a + 1e-6: s = x[1] + q - a; moved = len(use) > 1
                         lo += 1
             st[i] = s
             for r, a, z, p in use:
                 ln = line[r]; j = len(ln)
                 while j and ln[j - 1][0] > s + a: j -= 1
                 ln.insert(j, (s + a, s + z, e))
-            for j in suc[i]:
+            for j, gap in suc[i]:
+                if s + gap > st[j]: st[j] = s + gap
                 left[j] -= 1
                 if left[j] == 0:
                     y, lo = (key[j], j), len(ready)
-                    while lo and ready[lo - 1] > y: lo -= 1
+                    while lo and ready[lo - 1] < y: lo -= 1
                     ready.insert(lo, y)
         return st
 
+    after = [[[(j, full[i] + (0.0 if eng[j] == eng[i] == "T" else lat)) for j in x[i]] for i in range(n)] for x in (succ, pred)]
+    count = [[len(p) for p in x] for x in (pred, succ)]
+    uses = [[(eng[i], 0.0, cost[i], 0.0)] + [(b, 0.0, cost[i], lat) for b in ops[i]["b"]]
+            + [("D", cost[i] + dm * DLAT, full[i], 0.0)] * (full[i] > cost[i]) for i in range(n)]
+    uses = [uses, [[(r, full[i] - z, full[i] - a, p) for r, a, z, p in u] for i, u in enumerate(uses)]]
+    names = {r[0] for u in uses[0] for r in u}
     base = [0.0] * n
     for i in range(n - 1, -1, -1): base[i] = min([base[j] - lat for j in succ[i]], default=0.0) - full[i]
 
-    def run(key):
-        left = [len(p) for p in pred]
-        ready, free, bank, fin, st, pipe = {}, {}, {}, [0.0] * n, [0.0] * n, 0.0
-        for i in range(n):
-            if left[i] == 0: ready.setdefault(eng[i], {})[i] = 0.0
-        for _k in range(n):
-            first = None
-            for e, rd in ready.items():
-                f, est = free.get(e, 0.0), {}
-                for i, s in rd.items():
-                    if f > s: s = f
-                    for b in ops[i]["b"]:
-                        for e2, y in bank.setdefault(b, {}).items():
-                            if e2 != e and y + lat > s: s = y + lat
-                    est[i] = s
-                if est:
-                    m = min(est.values())
-                    if first is None or m < first[0]: first = (m, e, est)
-            m, e, est = first
-            i = min((key[i], i) for i in est if est[i] <= m + LOOK)[1]
-            st[i] = est[i]
-            free[e] = fin[i] = st[i] + cost[i]
-            if full[i] > cost[i]: pipe = fin[i] = max(pipe, fin[i] + DLAT) + ops[i]["c"][3]
-            for b in ops[i]["b"]: bank[b][e] = fin[i]
-            del ready[e][i]
-            for j in succ[i]:
-                left[j] -= 1
-                if left[j] == 0: ready.setdefault(eng[j], {})[j] = max(fin[y] + (0.0 if eng[y] == eng[j] == "T" else lat) for y in pred[j])
-        return st
-
-    parts = sorted({(o["g"], o["e"]) for o in ops}) + sorted({(o["g"], "") for o in ops})
+    parts = {}
+    for i, o in enumerate(ops):
+        for g in (o["g"], o["g"] + o["e"]): parts.setdefault(g, []).append(i)
+    parts = [parts[g] for g in sorted(parts)]
     seed = [SEED]
 
     def rnd():
         seed[0] = (seed[0] * 1103515245 + 12345) % 2 ** 31
         return (seed[0] >> 8) / 2 ** 23
 
-    best, unit = None, None
+    def bell(): return 2 * (rnd() + rnd() + rnd() - 1.5)
+
+    busy = [i for i in range(n) if eng[i] in "VA"]
+    work = sum(cost[i] for i in busy)
+    cur, best, unit = (None, base), None, None
     for it in range(TRIES):
-        key = list(best[2]) if best else [base[i] + 1000.0 * SHIFT.get(ops[i]["g"], 0) for i in range(n)]
-        if it and rnd() < 0.5:
-            g, e = parts[int(rnd() * len(parts))]
-            d = 4 * AMP * (2 * rnd() - 1)
-            for i in range(n):
-                if ops[i]["g"] == g and e in ("", eng[i]): key[i] += d
-        elif it:
-            for _k in range(NPERT):
-                j, d = int(rnd() * n), AMP * (2 * rnd() - 1)
+        key, u = list(cur[1]), rnd() if it else 2
+        if u < 0.3:
+            d = 1.5 * AMP * bell()
+            for i in parts[int(rnd() * len(parts))]: key[i] += d
+        elif u < 0.6:
+            j, d, far, up = int(rnd() * n), AMP * abs(bell()), AMP * (1, 2.7, 5)[int(3 * rnd())], rnd() < 0.5
+            seen, todo = {j}, [j]
+            while todo:
+                for y in (pred if up else succ)[todo.pop()]:
+                    if y not in seen and abs(key[y] - key[j]) < far: seen.add(y); todo.append(y)
+            for y in seen: key[y] += -d if up else d
+        elif u < 1:
+            for _k in range((1, 2, 4)[int(3 * rnd())]):
+                j, d = int(rnd() * n), AMP * bell()
                 for i in range(j, min(n, j + 1 + int(rnd() * RUN))): key[i] += d
-        st = run(key)
+        st = place(key, False)
+        bk = place([-st[i] - full[i] for i in range(n)], True)
+        st = place([-bk[i] - full[i] for i in range(n)], False)
+        t, mid = max(st[i] + full[i] for i in range(n)), sum(st[i] * cost[i] for i in busy) / work
+        if it and t + mid > cur[2] + 4 * WARM: continue
         sq = sorted(range(n), key=lambda i: (st[i], i))
-        t = [span(ops, sq, FIGS[0])]
-        if best and t[0] > best[3] * 1.01: continue
-        t += [span(ops, sq, f) for f in FIGS[1:]]
-        unit = unit or t
-        val = sum(a / b for a, b in zip(t, unit))
-        if best is None or val <= best[0]: best = (val, sq, key, t[0], st)
-    bk = place([-best[4][i] - full[i] for i in range(n)], True)
-    st = place([-bk[i] - full[i] for i in range(n)], False)
-    sq = sorted(range(n), key=lambda i: (st[i], i))
-    seq = sq if sum(span(ops, sq, f) / u for f, u in zip(FIGS, unit)) < best[0] else best[1]
+        ts = [t] + [span(ops, sq, f) for f in FIGS[1:]]
+        unit = unit or ts
+        val = sum(a / b for a, b in zip(ts, unit)) * unit[0] / len(FIGS)
+        if best is None or val <= best[0]: best = (val, sq)
+        if not it or val + mid <= cur[0] - WARM * (1 - it / TRIES) * math.log(1 - rnd()): cur = (val + mid, st, t + mid)
+    seq = best[1]
     ends = {}
     for i in seq:
         if ops[i]["s"] in ("open", "add"): ends[ops[i]["sum"]] = i; ops[i]["a"] = ops[i]["a"][:3] + (False,)
@@ -721,11 +727,12 @@ def rank_program(g, core, T, topo):
         elif k == "red": r = q.tensor_reduce(x[0], x[1], AX.X, AL.add, negate=x[2])
         elif k == "act": r = q.activation(*x[:3]) if x[2] == AF.Copy else q.activation(*x[:3], bias=x[3], scale=x[4])
         elif k == "iota": r = g.iota(*x) if a[0][0] == "PI" else g.iota(*x, allow_small_or_imprecise_dtypes=True)
+        elif k == "sel": r = g.affine_select(*x)
         elif k == "mm":
             for m, (l, rr) in enumerate(a[1]):
                 r = q.matmul(real(T, a[0]), real(T, l), real(T, rr), a[2] and m == 0, a[3] and m == len(a[1]) - 1)
         elif k == "mms":
-            for oo, l, rr in a[0]: r = q.matmul(real(T, oo), real(T, l), real(T, rr), True, True)
+            for oo, l, rr in a[0]: r = q.matmul(real(T, oo), real(T, l), real(T, rr), a[2], a[2])
         elif k == "dma":
             for oo, ii in a: q.dma_start(real(T, oo), real(T, ii)).then_inc(T.sem[o["src"]], 16)
             continue

import math
from concourse.bass import DstId, RemoteDMATransfer
from concourse.mybir import AluOpType as AL, AxisListType as AX, ActivationFunctionType as AF

V, W, SL, GH = 3328, 4096, 1024, 768
HV, NC, HC, HS = V // 2, V // 16, V // 32, SL // 2
NEW = 3 * HS
XN, LN = W + NEW + 16, W + NEW
X0 = [16, 16 + XN, 16 + 2 * XN]
L0 = [0, LN, 2 * LN]
M32, M64, M1 = 1.5 * 2 ** 28, 1.5 * 2 ** 29, 1.5 * 2 ** 23
ABLK = [[(3, 3), (4, 3)], [(2, 3), (3, 3), (4, 3)], [(4, 3)], [(3, 3), (4, 3)]]
FIN = ["AVAV", "AVAV", "AAAA", "AVAV"]
REL = ["AAAA", "AAAA", "AAAA", "AVAV"]
RND = "VVVV"
XUP = [[("V", 52), ("A", 52)], [("A", 104)], [("A", 104)], [("V", 52), ("A", 52)]]
ARA = [(0, 0), (0, 0), (0, 0), (0, 0)]
B, F, I, U = "bfloat16", "float32", "int32", "uint16"
MN = {"C": 1.0, "C2": 1.0, "CD": 1024.0, "L0": 0, "L1": 1, "L2": 2, "L3": 3, "H0": 24, "H1": 7}
IDN = {"p": 1.0, "n": -1.0, "h": 0.5, "nh": -0.5, "s1": 16384.0, "s2": 12288.0, "s3": 8192.0, "s4": 4096.0, "x16": 16.0, "m1": -4.0 * M1}
SB = {"X": ([X0[2] + XN], B), "LT": ([3 * LN], B), "Q": ([2 * (V + 16)], B), "MS": ([144 * len(MN)], B), "ID": ([128 * len(IDN)], B),
      "ZP": ([2, 224], B), "ZQ": ([4, 144], B), "JW": ([8, 32], B), "RC": ([8, 66], F), "TB": ([8, 64], F)}
for _d, _s in ((B, "ZR1024 MK1536 SG768 MT16 OM144 BO512 BN128 PA192 ON256 KC128 QT512 D01024 D14096 D21728 RR4096 RL2048 "
                   "RH1728 LW416 I1512 I2512 I3512 QS1024 LH512 WH96 S0768 S1768 S2768 S3768 G048 G148 G248 G348 N048 N148 N248 N348 LG4096 "
                   "DT2048 MG1024 IN6144 DD2048 SS384 R1512 R2512 R3512 R4512 YY512 AB2048 XS2464 LS1664 G88 G98 HH128 BB64 RK64 NI64"),
               (F, "IT144 IG128 II128 IF128 PS32 IS512 CX104 MM208 MF8 DM64 M216 CC224 T2224 TM208 T3224 TH32 Z1104 ZY104 Z2208 Z3104 NL104 TR104 "
                   "TL208 TX208 LC208 WT144 RN128 ZS1024 K164 KY128 YN416 VD128 LV128"),
               (I, "NB1024 SN96 SI144 PI16 LI8 WI144 JI128 JF128 JD256 K264 KD64 VI96"), (U, "SU288 BU96 UL208 UX208 WU48 JU1280")):
    for _x in _s.split(): SB[_x[:2]] = ([int(_x[2:])], _d)
SB = {k: ([128] + v[0], v[1]) for k, v in SB.items()}
SCRATCH = {k: ("sbuf", v[0], v[1]) for k, v in SB.items()}
for _b in range(8):
    SCRATCH["ps%d" % _b] = ("psum", [128, 512], F)
EXT = {"xv": ([128, V], B), "cq": ([128, V], B), "nb": ([8, 4 * W], I), "snd": ([128, 48], I), "yx": ([128, V], B), "yn": ([8, 4 * V], F)}
SEMAPHORES = ["eV", "eA", "eT", "eG", "loc"] + ["ar%d" % _i for _i in range(8)] + ["d%d" % _i for _i in range(60)]
SZ = {B: 2, F: 4, I: 4, U: 2}
S_ = slice(None)
HP = [slice(0, 64), slice(64, 128)]
FIGS = [(0.92, 1.56, 160.0, 1.0), (0.85, 1.25, 170.0, 1.1), (1.15, 1.85, 160.0, 1.0)]
DLAT, FIRST, TRIES, RUN, AMP, WARM, SEED = 1500.0, 2500.0, 4000, 24, 3000.0, 200.0, 12345


def shape_of(n):
    return SB.get(n) or EXT.get(n) or ([128, 512], F)


def ap(n, *ix):
    if len(ix) == 2 and isinstance(ix[0], int) and isinstance(ix[1], int): ix = (S_, slice(ix[0], ix[1]))
    return (n, ix or (S_,), None)


def ind(win, off):
    return (win[0], win[1], off)


def extent(a):
    shp = shape_of(a[0])[0]
    ix = list(a[1]) + [S_] * (len(shp) - len(a[1]))
    rs = [range(s)[x] if isinstance(x, slice) else range(x, x + 1) for s, x in zip(shp, ix)]
    r = rs[-1]
    m = ((1 << len(r)) - 1) << r[0] if r.step == 1 else sum(1 << j for j in r)
    n, lo = len(r), r[0]
    if len(shp) == 3:
        m = sum(m << (shp[2] * j) for j in rs[1]); n *= len(rs[1]); lo += shp[2] * rs[1][0]
    return m, sum(1 << j for j in rs[0]), n, len(rs[0]), lo


def nel(a):
    return 16 * extent(a[2])[2] if a[2] else extent(a)[2]


def real(T, a):
    if not isinstance(a, tuple): return a
    x = T[a[0]][a[1] if len(a[1]) > 1 else a[1][0]]
    return x.indirect(real(T, a[2])) if a[2] else x


def price(o, cy, ga):
    c = o["c"]
    return c[0] + cy * (c[1] + ga * c[2])


def build():
    ops, stage = [], ["load0"]

    def add(eng, kind, args, rd, wr, cost, sums=None):
        R, Wr = {}, {}
        for lst, out in ((rd, R), (wr, Wr)):
            for a in lst:
                if not isinstance(a, tuple): continue
                for b, o in ((a, out), (a[2], R)):
                    if b:
                        e = extent(b)
                        o[(b[0], e[1])] = o.get((b[0], e[1]), 0) | e[0]
        ops.append({"e": eng, "k": kind, "a": args, "r": R, "w": Wr, "c": cost, "s": sums, "g": stage[0]})

    def vc(out, *x):
        n = nel(x[0]) if x else nel(out)
        if x and x[0][2]: return (55.0, 0, n)
        return (0.0, max(64, n * (0.5 if all(SZ[shape_of(a[0])[1]] == 2 for a in (out,) + x) else 1)), 0)

    def ts(out, x, s1, o0, s2=None, o1=None): add("V", "ts", (out, x, s1, s2, o0, o1), [x, s1, s2], [out], vc(out, x))
    def cp(out, x): add("V", "cp", (out, x), [x], [out], vc(out, x))
    def ms(out, c): add("V", "ms", (out, c), [], [out], vc(out))
    def scan(out, a, b, o0, o1): add("V", "scan", (out, a, b, o0, o1), [a, b], [out], vc(out, a, b))
    def red(out, x, neg): add("V", "red", (out, x, neg), [x], [out], (0.0, max(64, nel(x)), 0))
    def iota(out, pat, base, cm): add("G", "iota", (out, pat, base, cm), [], [out], (130.0, 2 * nel(out), 0))

    def tt(out, x, y, o):
        add("V", "tt", (out, x, y, o), [x, y], [out], vc(out, x) if x[2] else (0.0, max(64, nel(x) * (2 if x[0] in SB and y[0] in SB else 1)), 0))

    def act(out, x, fn, bias=0.0, scale=1.0):
        add("A", "act", (out, x, fn, bias, scale), [x, bias, scale], [out], (70.0, 0, nel(x)) if x[2] else (0.0, max(64, nel(x)), 0))

    def pc(l, r): return 0.5 * max(min(64, nel(l)), nel(r)) * (4 if shape_of(l[0])[1] == F else 1)

    def mm(out, terms, start=True, more=False):
        add("T", "mm", (out, terms, start, True), [x for t in terms for x in t] + ([] if start else [out]), [out],
            (0.0, sum(pc(l, r) for l, r in terms), 0), "open" if start and more else "new" if start else "add")

    def mms(trip, start=True):
        add("T", "mms", (trip, None, start, start), [x for t in trip for x in t[start:]], [t[0] for t in trip],
            (0.0, sum(pc(l, r) for o, l, r in trip), 0), "new" if start else "add")

    def dma(pairs, after=()):
        by = sum(extent(o)[2] * extent(o)[3] * SZ[shape_of(o[0])[1]] for o, i in pairs)
        rows = sum(max(extent(o)[3], extent(i)[3]) for o, i in pairs)
        add("S", "dma", pairs, [i for o, i in pairs] + list(after), [o for o, i in pairs], (60.0 * len(pairs), 0, 0, by / 350.0 + 3.0 * rows))

    def send(src, dst, wid, back, sem, frees=()):
        add("G", "send", (src, dst, wid, back, sem), [src], [ap("loc" + sem)] + list(frees), (500.0 + FIRST * (sem == "ar0"), 0, 0))
        add("R" + sem, "arr", (sem,), [ap("loc" + sem)], [dst], (0.0, 0, 0, 600.0 + 4.0 * wid))

    def const(out, v): iota(out, [[0, nel(out)]], v, 0)
    def diag(x, j, v): add("G", "sel", (x, x, [[-1, nel(x)]], AL.not_equal, v, j, 1), [x], [x], (170.0, 2 * nel(x), 0))

    def fill(b, a, n):
        for j in range(a, a + n, 512): const(c(b, j, min(512, a + n - j)), 0)

    def P(b, a=0, n=512, p=S_, step=1): return ap("ps%d" % b, p, slice(a, a + n * step - step + 1, step))
    def c(b, a, n, p=S_): return ap(b, p, slice(a, a + n))
    def mast(m, i, p=S_): return c("MS", 144 * list(MN).index(m) + 15 - i, 128, p)
    def idm(m): return c("ID", 128 * list(IDN).index(m), 128)
    def ps(j, p=S_): return c("PS", j, 1, p)

    def wrap(m, buf, a, n, p=S_):
        return [(mast(m, i, p), ap(buf, p, slice(a + i, a + 16 * n, 16))) for i in range(16)]

    pp, nn, hp, hn = idm("p"), idm("n"), idm("h"), idm("nh")
    eq, mu, ad, su, mx = AL.is_equal, AL.mult, AL.add, AL.subtract, AL.max
    sh, an = AL.arith_shift_right, AL.bitwise_and
    H54, H64, H96 = slice(0, 54), slice(0, 64), slice(0, 96)

    def load(s):
        rows, nb = slice(64 * s, 64 * s + 64), c("NB", 512 * s, 512)
        dma([(nb, ap("nb", slice(4 * s, 4 * s + 4), S_))])
        for j in range(2):
            dma([(c("X", X0[s] + HV * (h ^ j), HV, HP[h]), ap("xv", rows, slice(HV * (h ^ j), HV * (h ^ j) + HV))) for h in range(2)])
        dma([(c("SN", 48 * s, 48, HP[h]), ap("snd", rows, S_)) for h in range(2)])
        if s: fill("LT", L0[s], W)
        else:
            for j in range(4): act(c("LT", L0[s] + 1024 * j, 1024), ap("ZR"), AF.Copy)
        hi, lo = c("DD", 1024 * s, 512), c("DD", 1024 * s + 512, 512)
        ts(hi, nb, M64, ad, M64, su)
        tt(lo, nb, hi, su)
        for j, b in enumerate((hi, lo)):
            dma([(ap("LT", slice(64 * h + j, 64 * h + 64, 4), slice(L0[s], L0[s] + W)), b) for h in range(2)])
        dma([(c("Q", (V + 16) * s, V, HP[h]), ap("cq", rows, S_)) for h in range(2)])
        ts(c("SI", 0, 48), c("SN", 48 * s, 48), W - 1, an)
        ts(c("SI", 48, 48), c("SN", 48 * s, 48), 12, sh)
        ts(c("SI", 96, 48), c("SI", 0, 48), float(HV), AL.is_ge, 4.0, mu)
        tt(c("SI", 48, 48), c("SI", 48, 48), c("SI", 96, 48), ad)
        cp(c("SU", 144 * s, 96), c("SI", 0, 96))
        ts(c("SU", 144 * s + 96, 48), c("SI", 0, 48), ps(20), ad, HV - 1.0, AL.min)
        act(c("MK", GH * s, GH), ind(ap("MT"), c("SU", 144 * s + 48, 48)), AF.Copy)
        mm(P(6 + s, 0, HC), wrap("H0", "X", X0[s], HC) + wrap("H1", "X", X0[s] + HV, HC))
        ts(c("LW", HC * s, HC), P(6 + s, 0, HC), 0.0, AL.is_lt)

    iota(c("PI", 0, 1), [[0, 1]], 0, 1)
    iota(ap("IT"), [[1, 144]], 0, 0)
    iota(ap("IG"), [[0, 2], [1, 4], [0, 16]], 0, 0)
    iota(ap("II"), [[0, 8], [1, 16]], 0, 0)
    iota(ap("MM"), [[0, 13], [1, 16]], 0, 0)
    iota(ap("IS"), [[1, 32], [32, 16]], 0, 0)
    iota(ap("KC"), [[-128, 4], [0, 32]], 384, 0)
    iota(ap("CX"), [[16, HC]], 0, 1)
    ms(ap("ZR"), 0.0)
    p0 = c("PI", 0, 1)
    for j, (o, s) in enumerate([(sh, 4), (an, 15), (sh, 1), (an, 1), (an, 3), (sh, 2), (sh, 6)]): ts(c("PI", j + 1, 1), p0, s, o)
    cp(c("PS", 0, 8), c("PI", 0, 8))
    ts(c("PI", 8, 1), p0, 31, an)
    cp(ps(25), c("PI", 8, 1))
    for j in range(2): ts(c("RK", 32 * j, 32), c("IT", 0, 32), ps(25), eq)
    def lin(j, i, a, b): act(ps(j), ps(i), AF.Identity, b, a)
    lin(8, 7, -4.0, ps(1))
    ts(ps(9), ps(5), 2.0, AL.is_lt)
    lin(11, 4, -1.0, 1.0)
    ts(ps(12), ps(2), 13.0, AL.min)
    lin(13, 1, -4.0, ps(6))
    lin(14, 7, -float(HS), W + HS - 1.0)
    lin(15, 1, -16.0, 0.0)
    lin(16, 7, float(HV), ps(15))
    lin(17, 6, 8.0, 3.0)
    lin(18, 7, -124.0, ps(17))
    lin(19, 7, float(HS), 0.0)
    act(ap("IS"), ap("IS"), AF.Identity, bias=ps(19))
    lin(20, 7, -float(HV), 0.0)
    lin(21, 7, 4.0, ps(13))
    lin(22, 7, 8192.0, float(HV))
    lin(23, 7, -float(HV), 16.0)
    lin(24, 7, -1.0, 1.0)
    ts(ap("G8"), c("IT", 0, 8), ps(1), eq)
    ts(ap("G9"), ap("IG", S_, slice(0, 128, 16)), ps(8), eq)
    ts(ap("MT"), c("IT", 0, 16), ps(21), eq, ps(9), mu)
    ts(c("MF", 0, 4), c("IT", 0, 4), ps(13), eq, ps(9), mu)
    ts(c("MF", 4, 4), c("IT", 0, 4), ps(5), eq)
    ms(ap("MS"), 0.0)
    for j, m in enumerate(MN):
        act(ap("MS", S_, slice(144 * j + 15, 144 * j + 143, 16)), ap("G9" if m == "C2" else "G8"), AF.Identity,
            scale=ps(MN[m]) if m[0] in "FH" else c("MF", MN[m], 1) if m[0] == "L" else MN[m])
    ts(pp, c("IT", 0, 128), ps(0), eq)
    for m in list(IDN)[1:]:
        if m != "m1" or "A" in RND: act(idm(m), pp, AF.Identity, scale=IDN[m])
    act(ap("IF"), pp, AF.Copy)
    ts(ap("OM"), ap("IT"), ps(18), eq, ps(9), mu)
    ts(ap("BN"), ap("II"), ps(2), AL.is_lt, -1.0, mu)
    for h in range(2):
        ts(c("BO", 128 * h, 128), ap("IG"), ps(8), eq, ps(7 if h else 24), mu)
        tt(c("BO", 256 + 128 * h, 128), c("BO", 128 * h, 128), ap("BN"), mu)
    ts(c("PA", 0, 32), c("IT", 0, 32), ps(3), eq, ps(11), mu)
    ts(c("PA", 32, 32), c("IT", 0, 32), ps(3), eq, ps(4), mu)
    lin(26, 8, 8.0, ps(21))
    for j in range(4): ts(c("PA", 64 + 32 * j, 32), c("IT", 0, 32), ps(26), eq, c("MF", 4 + j, 1), mu)
    ts(ap("M2"), c("IT", 0, 16), ps(12), eq)
    ts(ap("MM"), ap("MM"), ps(2), eq)
    act(ap("CX"), ap("CX"), AF.Identity, ps(16))
    act(ap("QT"), c("ZR", 0, 512), AF.Identity, -0.25)
    ms(c("TH", 14, 1), -0.5)
    const(ap("ON"), 1)
    for b in ("CC", "T2", "T3"): const(c(b, NC, 16), 8192)
    for b in range(4): const(c("X", XN * b, 16), -64)
    for s in range(2): const(c("Q", (V + 16) * s + V, 16), 1000)
    load(0)
    stage[0] = "fill"
    for s in range(2): const(c("XS", (16 + HV + GH) * s, 16), 0)
    for b in ("ZP", "ZQ", "G0", "G1", "G2", "G3", "DM", "HH"): const(ap(b), 0)
    const(ap("RC", S_, S_, slice(64, 66)), 0)
    iota(ap("NI"), [[-1, 64]], 0, 0)
    for j in range(2): const(c("D0", 512 * j, 512), -1)
    const(ap("TB"), 0)
    for h in range(2):
        if h: add("G", "sel", (ap("DM"), ap("DM"), [[0, 64]], AL.is_gt, 0.0, 64, -1), [ap("DM")], [ap("DM")], (170.0, 128, 0))
        for j, v in enumerate((8192.0, -16384.0, 8192.0)): diag(ap("DM"), -j - 64 * h, v)
    for j in (-64, 0, 64): diag(ap("HH"), j, 1.0)
    fill("D1", 0, 4096); fill("D2", 0, 1728)
    for b in range(3): fill("X", X0[b] + W, NEW); fill("LT", L0[b] + W, NEW)

    def head(ph):
        s, r, b, par = ph % 2, ph // 2, ph % 3, ph % 2
        xo, lo = X0[b], L0[b]
        lw, Lw = c("LT", lo, W), c("LW", HC * ph, HC)
        tt(ap("SG"), ind(ap("LS"), c("SU", 144 * s + 96, 48)) if r else ind(c("LT", lo, V), c("SU", 144 * s, 48)), c("MK", GH * s, GH), mu)
        w, mb = P(6 + par, 416, 48), 6 + par
        mm(w, wrap("C2", "SG", 0, 48))
        ts(c("WT", 0, 48), w, float(V), AL.is_ge, -8192.0, mu)
        tt(c("WT", 48, 48), w, c("WT", 0, 48), ad)
        if r == 0:
            ts(ap("WU"), c("WT", 48, 48), 16.0, ad)
            act(ap("S%d" % ph), ind(c("X", xo - 16, 16 + V), ap("WU")), AF.Copy)
        else:
            ts(c("WT", 96, 48), w, ps(22), AL.is_ge, 4096.0, mu)
            tt(c("WT", 96, 48), w, c("WT", 96, 48), ad)
            ts(ap("WU"), c("WT", 96, 48), ps(23), ad, 16.0 + HV + GH, AL.min)
            act(ap("SG"), ind(ap("XS"), ap("WU")), AF.Copy)
            for a, n in ((0, 512), (512, 256)):
                mm(P(par, 0, n), [(ap("HH"), c("SG", a, n))])
                act(c("S%d" % ph, a, n), P(par, 0, n), AF.Copy)
        send(ap("S%d" % ph), c("X", xo + V, GH), 256, False, "ar%d" % (2 * ph))
        cp(c("WI", 0, 48), c("WT", 48, 48))
        ts(c("WI", 48, 48), c("WI", 0, 48), 6, sh)
        ts(c("WI", 96, 48), c("WI", 0, 48), 63, an)
        ts(c("WH", 48 * par, 48), c("WI", 48, 48), 1.0, ad, 0.0, mx)
        ts(ap("ZQ", S_, 2 * par + 1, slice(48, 96)), c("WI", 96, 48), 1.0, ad)
        mms([(P(mb, HC * j, HC), c("BO", 128 * j, 128), Lw) for j in range(4)])
        scan(c("CC", 0, NC), c("ON", 0, NC), P(mb, 0, NC), mu, ad)
        tt(c("TH", 0, 14), ap("CC", S_, slice(15, 224, 16)), c("M2", 0, 14), mu)
        red(c("TH", 16, 1), c("TH", 0, 15), True)
        tt(ap("TM"), c("CC", 0, NC), ap("MM"), mu)
        scan(c("T2", 0, NC), c("ON", 0, NC), ap("TM"), mu, mx)
        tt(c("T3", 0, NC), P(mb, NC, NC), c("CC", 0, NC), ad)
        act(ap("I1"), ap("IS"), AF.Sign, bias=c("TH", 16, 1))
        mm(P(2, 384, 32), wrap("C", "I1", 0, 32))
        ts(c("BU", 0, 32), P(2, 384, 32), 8.0, mu, 143.0, ad)
        act(c("BB", 0, 32), P(2, 384, 32), AF.Identity, bias=128.0, scale=8.0)
        tt(ap("I2"), ind(ap("T2"), c("BU", 0, 32)), ap("IS"), AL.is_le)
        mm(P(2, 416, 32), [(pp, c("BB", 0, 32))] + wrap("C", "I2", 0, 32))
        cp(c("BU", 32, 32), P(2, 416, 32))
        act(c("BB", 32, 32), P(2, 416, 32), AF.Copy)
        tt(ap("I3"), ind(ap("T3"), c("BU", 32, 32)), ap("IS"), AL.is_le)
        mm(P(2, 448, 32), [(idm("x16"), c("BB", 32, 32))] + wrap("C", "I3", 0, 32))
        cp(c("BU", 64, 32), P(2, 448, 32))
        act(ap("LH"), ind(lw, c("BU", 64, 32)), AF.Copy)
        act(c("QS", HS * par, HS), ind(c("Q", (V + 16) * s, V + 16), c("BU", 64, 32)), AF.Copy)
        for h in range(2): act(c("ZY", 0, HC, HP[h]), c("T3", HC * h, HC, HP[h]), AF.Identity, bias=ps(14, HP[h]))
        tt(ap("Z1"), ap("ZY"), Lw, mu)
        tt(c("TL", HC * par, HC), ap("Z1"), ap("CX"), mx)
        act(ap("ZY"), Lw, AF.Identity, bias=float(W + NEW), scale=-float(W + NEW))
        tt(c("TX", HC * par, HC), ap("ZY"), ap("Z1"), mx)
        if r == 0: tt(c("LC", HC * par, HC), ap("ZY"), ap("CX"), mx)
        cp(c("VI", 0, 32), P(2, 448, 32))
        ts(c("VI", 32, 32), c("VI", 0, 32), 6, sh)
        ts(c("VI", 64, 32), c("VI", 0, 32), 63, an)
        ts(c("VD", 64 * par, 64), c("VI", 32, 64), 1.0, ad)
        for k in range(4): mm(z(ph, 1, k, 32), wrap("L%d" % k, "LH", 0, 32))
        stage[0] = "links%d" % ph
        for t in range(1, 5):
            for k in (0, 2): cp(ju(ph, t, k, 64), z(ph, t, k, 64))
            act(zs(ph, t), z(ph, t), AF.Copy)
            g = 2048 * (t % 2)
            for k in range(4): act(c("LG", g + 512 * k, 512), ind(lw, ju(ph, t, k, 32)), AF.Identity, scale=c("MF", k, 1))
            for k in (0, 2): mm(z(ph, t + 1, k, 64), wrap("C", "LG", g + 512 * k, 64))

    def zs(ph, t): return c("ZS", 512 * (ph % 2) + 128 * (t - 1), 128)
    def z(ph, t, k=0, n=128): return P(ph % 2, 128 * (t - 1) + 32 * k, n) if t < 5 else P(2, 128 * (ph % 2) + 32 * k, n)
    def ju(ph, t, k=0, n=128): return c("JU", 640 * (ph % 2) + 128 * (t - 1) + 32 * k, n)
    rot = [0, 0]

    def count(a, fn, out, bias, scale):
        mms([(P(2, 256 + i, 8, S_, 16), ap("IN", S_, slice(a + i, a + 2048, 16)), ap("G8")) for i in range(16)])
        act(out, P(2, 256, 128), fn, bias, scale)

    def limit(r):
        mm(P(7, 0, HC), [(c("ON", 0, 128), c("LW", HC * (2 * r + s), HC)) for s in range(2)])
        red(c("TH", 17, 1), P(7, 0, HC), False)
        cp(c("LI", 0, 1), c("TH", 17, 1))
        ts(c("LI", 1, 1), c("LI", 0, 1), 7, an)
        ts(c("TH", 18 + r, 1), c("LI", 1, 1), 160.5, ad, 1024.0, mu)

    def visits(ph):
        xw, qs = c("X", X0[ph % 3], W), c("QS", HS * (ph % 2), HS)
        for t in range(1, 5):
            for k in range(4):
                o = c("IN", 2048 * (t % 2) + 512 * k, 512)
                if (t, k) in ABLK[ph]:
                    m = c("MG", 512 * (rot[1] % 2), 512); rot[1] += 1
                    act(m, ind(xw, ju(ph, t, k, 32)), AF.Copy)
                    mm(P(3), [(pp, m), (nn, qs)])
                    ts(o, P(3), M32, ad, M32, eq)
                else:
                    d = c("DT", 512 * (rot[0] % 4), 512); rot[0] += 1
                    tt(d, ind(xw, ju(ph, t, k, 32)), qs, su)
                    ts(o, d, M32, ad, M32, eq)
            sg = c("SS", 128 * (t % 2), 128)
            count(2048 * (t % 2), AF.Sign, sg, -8.5, 1.0)
            mm(z(ph, t), [(ap("IF"), zs(ph, t)), (sg, idm("s%d" % t))])
            if t == 1: act(ap("RN"), z(ph, 1), AF.Copy)
            else: tt(ap("RN") if t < 4 else ap("JI"), z(ph, t), ap("RN"), mx)
            if t == 3: tt(ap("RN"), z(ph, 5), ap("RN"), mx)
        ts(ap("JF"), ap("JI"), W - 1, an)
        cp(ju(ph, 5), ap("JF"))

    def verdict(ph):
        par, xo, lo = ph % 2, X0[ph % 3], L0[ph % 3]
        xw, qs = c("X", xo, W), c("QS", HS * par, HS)
        m = [c("DD", 512 * k, 512) for k in range(4)]
        R1, R2, R3, R4, Y = (ap(x) for x in ("R1", "R2", "R3", "R4", "YY"))

        def relu(j, out, x):
            if REL[ph][j] == "A": act(out, x, AF.Relu)
            else: ts(out, x, 0.0, mx)

        for k in range(4):
            if FIN[ph][k] == "A": act(m[k], ind(xw, ju(ph, 5, k, 32)), AF.Copy)
            else: cp(m[k], ind(xw, ju(ph, 5, k, 32)))
        ts(c("JD", 0, 128), ap("JF"), 6, sh)
        ts(c("JD", 128, 128), ap("JF"), 63, an)
        mm(P(4), [(pp, m[0]), (nn, m[1])])
        relu(0, R1, P(4))
        mm(P(5), [(pp, m[2]), (nn, m[3])])
        relu(1, R2, P(5))
        mm(P(par), [(pp, m[1]), (nn, m[3])], True, True)
        mm(P(par), [(pp, R1), (nn, R2)], False)
        relu(2, R3, P(par))
        mm(P(4), [(pp, m[0]), (nn, R1), (nn, m[2])], True, True)
        mm(P(4), [(pp, R2)], False)
        relu(3, R4, P(4))
        mm(P(5), [(pp, ap("QT")), (hp, m[1]), (hp, m[2]), (hp, R1), (hn, R2)], True, True)
        mm(P(5), [(hn, R3)], False)
        mm(P(5), [(hp, R4)] + [(idm("m1"), ap("QT"))] * (RND[ph] == "A"), False)
        if RND[ph] == "A": act(Y, P(5), AF.Identity, -M1)
        else: ts(Y, P(5), M1, ad, M1, su)
        for k in range(4):
            mm(P(3), [(pp, m[k]), (nn, qs)])
            ts(c("IN", 4096 + 512 * k, 512), P(3), M32, ad, M32, eq)
        count(4096, AF.Sign, c("SS", 256, 128), 8.5, -1.0)
        for k in range(4):
            bk = P((par, 4, 5, par)[k])
            mm(bk, [(pp, m[k])], True, True)
            mm(bk, [(nn, Y)], False)
            act(c("AB", 512 * k, 512), bk, AF.Abs)
        D, nf = P(6 + par, 0, 128), P(2, 384, 64)
        mm(nf, [(c("SS", 256, 128), ap("RK"))])
        ts(c("LV", 0, 64), nf, -3.5, AL.is_gt, 2.0 ** 30, mu)
        ts(c("LV", 64, 64), c("VD", 64 * par, 64), c("TH", 18 + ph // 2, 1), ad)
        tt(c("LV", 0, 64), c("LV", 0, 64), c("LV", 64, 64), ad)
        mm(D, [(pp, ap("KC")), (pp, c("ON", 0, 128))], True, True)
        for k in (0, 2): mm(P(6 + par, 32 * k, 64), wrap("CD", "AB", 512 * k, 64), False, True)
        for dg in range(2):
            tt(P(6 + par, 256 + 64 * dg, 64), P(6 + par, 0, 64), c("JD", 128 * dg, 64), ad)
            tt(c("KY", 64 * dg, 64), P(6 + par, 64, 64), c("JD", 128 * dg + 64, 64), ad)
        tt(P(6 + par, 0, 128), P(6 + par, 256, 128), ap("KY"), mx)
        for dg in range(2): tt(c("K1", 32 * dg, 32), P(6 + par, 64 * dg, 32), c("LV", 32 * dg, 32), mx)
        for dg in range(2): tt(c("K2", 32 * dg, 32), P(6 + par, 64 * dg + 32, 32), c("K1", 32 * dg, 32), mx)
        ts(ap("KD"), ap("K2"), 127, an)
        cp(ap("ZP", S_, S_, slice(96, 128)), ap("KD"))
        jh, jl = (ap("JW", S_, slice(4 * j, 4 * j + 4), S_) for j in range(2))
        ts(jh, ap("JF"), M64, ad, M64, su)
        tt(jl, ap("JF"), jh, su)
        jrow = lambda j: ap("LT", slice(j, 128, 16), slice(lo + W + HS, lo + W + 2 * HS))
        dma([(jrow(4 * (j % 4) + j // 4), ap("JW", S_, j, S_)) for j in range(8)])
        mms([(P(5, 32 * i, 32), pp, ap("YY", S_, slice(i, HS, 16))) for i in range(16)])
        act(c("X", xo + W + HS, HS), P(5), AF.Copy)
        for b, o in (("X", xo), ("LT", lo)):
            dma([(c(b, o + W + 2 * HS * (1 - h), HS, HP[h]), c(b, o + W + HS, HS, HP[1 - h])) for h in range(2)])

    def ramps(out, ro, d, do, n, p):
        scan(c(out, ro, n, p), c("D0", 0, n, p), c(d, do, n, p), ad, mx)

    def slopes(out, d, wid, n, na, p):
        for a in range(0, n - na, 16): ramps(out, wid * a, d, wid * a, wid * min(16, n - na - a), p)
        for j in range(n - na, n): act(c(out, wid * j, wid, p), c("NI", 0, wid, p), AF.Relu, c(d, wid * j, 1, p))

    def sums(b, q, n): return P(b, 64 * (q % 2), 64, slice(64 * (q // 2), 64 * (q // 2) + n))

    def steps(b):
        act(ap("RC", S_, slice(4 * b, 4 * b + 2), H64), P(b, 0, 128), AF.Identity, 0.0, -2.0)
        act(ap("RC", S_, slice(4 * b + 2, 4 * b + 4), H64), P(b, 0, 128), AF.Copy)
        tt(P(b, 128, 128), P(b, 0, 128), ap("RC", S_, slice(4 * b, 4 * b + 2), slice(1, 65)), ad)
        for q in range(4):
            p = HP[q // 2]
            tt(ap("TB", p, slice(4 * b, 4 * b + 4), slice(16 * q, 16 * q + 16)), P(b, 128 + 64 * (q % 2), 64, p), ap("RC", p, 4 * b + 2 + q % 2, slice(2, 66)), ad)

    def cells(b, o, h, a, n):
        return [(P(6 + b, o + e, n, HP[h], 4), ap("TB", S_, 4 * b + e, S_), c("DM", a, n)) for e in range(4)]

    def marks(b, a, x):
        mm(P(6 + b, a, HC), [(c("ZR", 0, 128), c("ZR", 0, HC))], True, True)
        for h in range(2): mms(cells(b, a, h, 26 * h, 26), False)
        mm(P(6 + b, a, HC), [(ap("IF"), x)], False)
        return P(6 + b, a, HC)

    def notices(par, dg, o):
        zq = lambda a: ap("ZQ", H64, 2 * par + dg, slice(a, a + 96))
        mm(P(6 + par, o, 32, H96), [(zq(48), c("PA", 0, 32, H64)), (zq(0), c("PA", 32, 32, H64))])

    def tail(ph):
        s, r, par = ph % 2, ph // 2, ph % 2
        xo, lo, xn, ln = X0[ph % 3], L0[ph % 3], X0[(ph + 2) % 3], L0[(ph + 2) % 3]
        mb = 6 + par
        for dg in range(2):
            mm(P(mb, 128 + 32 * dg, 32), [(ap("ZP", S_, dg, slice(96 - 32 * j, 224 - 32 * j)), c("PA", 64 + 32 * j, 32)) for j in range(4)])
        cp(ap("D1", S_, slice(0, W, 64)), P(mb, 128, 64))
        slopes("RR", "D1", 64, 64, ARA[ph][0], S_)
        for q in range(4): mm(sums(par, q, 64), [(c("RR", 64 * j, 64), c("RR", 2048 + 64 * j, 64)) for j in range(8 * q, 8 * q + 8)])
        steps(par)
        mms(cells(par, 192, 0, 52, 12))
        ts(c("G%d" % ph, 0, 48, H64), P(mb, 192, 48, H64), 0.5, AL.is_gt)
        send(ap("G%d" % ph), ap("N%d" % ph), 16, True, "ar%d" % (2 * ph + 1), [c("X", X0[0] + V, GH)] * (ph == 1))
        notices(par, 1, 240)
        cp(ap("D1", H96, slice(0, 2048, 64)), P(mb, 240, 32, H96))
        for q in range(2): ramps("RL", 1024 * q, "D1", 1024 * q, 1024, H96)
        fo = marks(par, 408, ap("CX"))
        z2, ul, (ls, l0), (xs, x0) = c("Z2", HC * par, HC), c("UL", HC * par, HC), *((("LS", 0), ("XS", 16)) if ph < 3 else (("LG", 0), ("LG", 2048)))
        tt(ap("Z3"), fo, c("TL", HC * par, HC), AL.min)
        cp(ul, ap("Z3"))
        tt(z2, fo, c("TX", HC * par, HC), AL.min)
        act(c(ls, l0, HV), ind(c("LT", lo, LN), ul), AF.Copy)
        if r == 0:
            dma([(c("LT", ln + HV * h, HV, HP[j]), c("LS", 0, HV, HP[h])) for h in range(2) for j in range(2)])
            dma([(c("LT", ln + V, GH), c("LT", lo + V, GH))])
            dma([(c("XS", 16 + HV, GH), c("X", xo + V, GH))])
            tt(ap("NL"), z2, c("LC", HC * par, HC), eq)
            act(ap("TR"), ap("NL"), AF.Identity, bias=8000.0, scale=-9000.0)
        tt(ap("ZQ", H64, 2 * par, slice(48, 96)), c("N%d" % ph, 0, 48, H64), c("WH", 48 * par, 48, H64), mu)
        notices(par, 0, 272)
        cp(ap("D2", H96, slice(0, 1728, 54)), P(mb, 272, 32, H96))
        slopes("RH", "D2", 54, 32, ARA[ph][1], H96)
        for q in range(4): mm(sums(par, q, 54), [(c("RH", 54 * j, 54, H96), c("RL", 64 * j, 64, H96)) for j in range(8 * q, 8 * q + 8)])
        steps(par)
        fa = marks(par, 304, z2)
        ts(c("UX", HC * par, HC), fa, float(W + NEW), AL.min)
        if r == 0: tt(c("LW", HC * (ph + 2), HC), fa, ap("TR"), AL.is_gt)
        else:
            yb = 5 if ph == 3 else par
            mm(P(yb, 0, 416), [(c("OM", 3 - e, 128), c(ls, l0 + 416 * e, 416)) for e in range(4)])
            act(ap("YN"), P(yb, 0, 416), AF.Copy)
            dma([(ap("yn", slice(4 * s, 4 * s + 4), S_), ap("YN"))])
        a = 0
        for e, n in XUP[ph]:
            o, x = c(xs, x0 + 16 * a, 16 * n), ind(c("X", xo, XN), c("UX", HC * par + a, n))
            if e == "A": act(o, x, AF.Copy)
            else: cp(o, x)
            o = [c(xs, x0 + 16 * a, 16 * n, HP[h]) for h in range(2)]
            if r == 0: dma([(c("X", xn + HV * h + 16 * a, 16 * n, HP[j]), o[h]) for h in range(2) for j in range(2)])
            else: dma([(ap("yx", slice(64 * s, 64 * s + 64), slice(HV * h + 16 * a, HV * h + 16 * (a + n))), o[h]) for h in range(2)])
            a += n

    todo = [(head, 0), (load, 1), (limit, 0), (head, 1), (visits, 0), (verdict, 0)]
    for ph in range(1, 4):
        todo += [(visits, ph), (tail, ph - 1)] + [(limit, 1)] * (ph == 2) + [(head, ph + 1)] * (ph < 3) + [(verdict, ph)]
    names = {head: "head", load: "load", limit: "limit", visits: "visits", verdict: "verdict", tail: "tail"}
    for f, ph in todo + [(tail, 3)]:
        stage[0] = names[f] + str(ph); f(ph)
    return ops


def depend(ops):
    last, news, adds, opened = {}, {}, {}, {}
    for i, o in enumerate(ops):
        dep = set()
        o["b"] = sorted({x[0] for x in list(o["r"]) + list(o["w"]) if x[0][:2] == "ps"})
        for bk in o["b"] if o["s"] else []:
            if o["s"] != "add": dep.update(adds.get(bk, []))
            if o["s"] == "open": dep.update(news.get(bk, [])); opened[bk] = i; news[bk] = []; adds[bk] = []
            o["sum"] = opened.get(bk)
            (adds if o["s"] == "add" else news).setdefault(bk, []).append(i)
        for (nm, pm), m in o["r"].items():
            dep.update(x[0] for x in last.get(nm, []) if x[3] and x[1] & m and x[2] & pm)
        if not o["s"]:
            for j in list(dep):
                if ops[j]["s"] in ("open", "add"): dep.update(x for x in adds.get(ops[j]["b"][0], []) if ops[x]["sum"] == ops[j]["sum"])
        for (nm, pm), m in o["w"].items():
            dep.update(x[0] for x in last.get(nm, []) if x[1] & m and x[2] & pm)
            last[nm] = [x for x in last.get(nm, []) if x[1] & ~m or x[2] & ~pm]
        for w, key in ((False, "r"), (True, "w")):
            for (nm, pm), m in o[key].items(): last.setdefault(nm, []).append((i, m, pm, w))
        dep.discard(i)
        o["d"] = sorted(dep)
        o["p"] = [(j, not ops[j]["e"] == o["e"] == "T") for j in o["d"]]


def span(ops, seq, fig, tm=None):
    cy, ga, lat, dm = fig
    free, bank, fin, pipe = {}, {}, [0.0] * len(ops), 0.0
    for i in seq:
        o = ops[i]; e = o["e"]; c = o["c"]
        s = free.get(e, 0.0)
        for j, far in o["p"]:
            y = fin[j] + far * lat
            if y > s: s = y
        for b in o["b"]:
            e2, y = bank.get(b, (e, 0.0))
            if e2 != e and y + lat > s: s = y + lat
        free[e] = y = s + c[0] + cy * (c[1] + ga * c[2])
        if len(c) > 3: pipe = y = max(pipe, y + dm * DLAT) + dm * c[3]
        fin[i] = y
        for b in o["b"]: bank[b] = (e, y)
        if tm is not None: tm[i] = (s, y)
    return max(fin)


def order(ops):
    depend(ops)
    n = len(ops)
    cy, ga, lat, dm = FIGS[0]
    succ = [[] for _ in ops]
    for i, o in enumerate(ops):
        for j in o["d"]: succ[j].append(i)
    cost = [price(o, cy, ga) for o in ops]
    full = [cost[i] + (dm * (o["c"][3] + DLAT) if len(o["c"]) > 3 else 0.0) for i, o in enumerate(ops)]
    eng = [o["e"] for o in ops]
    pred = [o["d"] for o in ops]

    def place(key, back):
        suc, left = after[back], list(count[back])
        ready = sorted(((key[i], i) for i in range(n) if left[i] == 0), reverse=True)
        line, st = {r: [] for r in names}, [0.0] * n
        while ready:
            i = ready.pop()[1]; e = eng[i]; s = st[i]; use = uses[back][i]
            moved = True
            while moved:
                moved = False
                for r, a, z, p in use:
                    ln = line[r]; m = len(ln)
                    if not m or ln[-1][1] + p <= s + a: continue
                    lo, hi = 0, m
                    while lo < hi:
                        mid = (lo + hi) // 2
                        if ln[mid][1] + p <= s + a: lo = mid + 1
                        else: hi = mid
                    while lo < m:
                        x = ln[lo]
                        if x[0] >= s + z + p: break
                        q = 0.0 if x[2] == e else p
                        if x[0] < s + z + q - 1e-6 and x[1] + q > s + a + 1e-6: s = x[1] + q - a; moved = len(use) > 1
                        lo += 1
            st[i] = s
            for r, a, z, p in use:
                ln = line[r]; j = len(ln)
                while j and ln[j - 1][0] > s + a: j -= 1
                ln.insert(j, (s + a, s + z, e))
            for j, gap in suc[i]:
                if s + gap > st[j]: st[j] = s + gap
                left[j] -= 1
                if left[j] == 0:
                    y, lo = (key[j], j), len(ready)
                    while lo and ready[lo - 1] < y: lo -= 1
                    ready.insert(lo, y)
        return st

    after = [[[(j, full[i] + (0.0 if eng[j] == eng[i] == "T" else lat)) for j in x[i]] for i in range(n)] for x in (succ, pred)]
    count = [[len(p) for p in x] for x in (pred, succ)]
    uses = [[(eng[i], 0.0, cost[i], 0.0)] + [(b, 0.0, cost[i], lat) for b in ops[i]["b"]]
            + [("D", cost[i] + dm * DLAT, full[i], 0.0)] * (full[i] > cost[i]) for i in range(n)]
    uses = [uses, [[(r, full[i] - z, full[i] - a, p) for r, a, z, p in u] for i, u in enumerate(uses)]]
    names = {r[0] for u in uses[0] for r in u}
    base = [0.0] * n
    for i in range(n - 1, -1, -1): base[i] = min([base[j] - lat for j in succ[i]], default=0.0) - full[i]

    parts = {}
    for i, o in enumerate(ops):
        for g in (o["g"], o["g"] + o["e"]): parts.setdefault(g, []).append(i)
    parts = [parts[g] for g in sorted(parts)]
    seed = [SEED]

    def rnd():
        seed[0] = (seed[0] * 1103515245 + 12345) % 2 ** 31
        return (seed[0] >> 8) / 2 ** 23

    def bell(): return 2 * (rnd() + rnd() + rnd() - 1.5)

    busy = [i for i in range(n) if eng[i] in "VA"]
    work = sum(cost[i] for i in busy)
    cur, best, unit = (None, base), None, None
    for it in range(TRIES):
        key, u = list(cur[1]), rnd() if it else 2
        if u < 0.3:
            d = 1.5 * AMP * bell()
            for i in parts[int(rnd() * len(parts))]: key[i] += d
        elif u < 0.6:
            j, d, far, up = int(rnd() * n), AMP * abs(bell()), AMP * (1, 2.7, 5)[int(3 * rnd())], rnd() < 0.5
            seen, todo = {j}, [j]
            while todo:
                for y in (pred if up else succ)[todo.pop()]:
                    if y not in seen and abs(key[y] - key[j]) < far: seen.add(y); todo.append(y)
            for y in seen: key[y] += -d if up else d
        elif u < 1:
            for _k in range((1, 2, 4)[int(3 * rnd())]):
                j, d = int(rnd() * n), AMP * bell()
                for i in range(j, min(n, j + 1 + int(rnd() * RUN))): key[i] += d
        st = place(key, False)
        bk = place([-st[i] - full[i] for i in range(n)], True)
        st = place([-bk[i] - full[i] for i in range(n)], False)
        t, mid = max(st[i] + full[i] for i in range(n)), sum(st[i] * cost[i] for i in busy) / work
        if it and t + mid > cur[2] + 4 * WARM: continue
        sq = sorted(range(n), key=lambda i: (st[i], i))
        ts = [t] + [span(ops, sq, f) for f in FIGS[1:]]
        unit = unit or ts
        val = sum(a / b for a, b in zip(ts, unit)) * unit[0] / len(FIGS)
        if best is None or val <= best[0]: best = (val, sq)
        if not it or val + mid <= cur[0] - WARM * (1 - it / TRIES) * math.log(1 - rnd()): cur = (val + mid, st, t + mid)
    seq = best[1]
    ends = {}
    for i in seq:
        if ops[i]["s"] in ("open", "add"): ends[ops[i]["sum"]] = i; ops[i]["a"] = ops[i]["a"][:3] + (False,)
    for i in ends.values(): ops[i]["a"] = ops[i]["a"][:3] + (True,)
    pos, cnt, clock, known, user, nd = {}, {}, {}, {}, {}, 0
    for i in seq:
        o = ops[i]; e = o["e"]
        if o["k"] == "dma": o["src"] = "d%d" % nd; nd += 1
        else: o["src"] = o["a"][0] if o["k"] == "arr" else "e" + e
        dep = set(o["d"])
        for b in o["b"]:
            dep |= {j for e2, j in user.get(b, {}).items() if e2 != e}
            user.setdefault(b, {})[e] = i
        kn = known.setdefault(e, {})
        o["wait"] = []
        if o["k"] != "arr":
            for j in sorted(dep, key=lambda j: -pos[j]):
                p = ops[j]
                if p["e"] == e == "T" or p["k"] == "send" or kn.get(p["src"], -1) >= pos[j]: continue
                o["wait"].append(j); p["inc"] = True
                for k, v in clock[j].items(): kn[k] = max(kn.get(k, -1), v)
        pos[i] = len(pos)
        clock[i] = dict(kn)
        clock[i][o["src"]] = pos[i]
    for i in seq:
        o = ops[i]
        if o["k"] == "dma": o["val"] = 16 * len(o["a"])
        elif o.get("inc") and o["k"] != "arr":
            cnt[o["src"]] = o["val"] = cnt.get(o["src"], 0) + 1
    return seq


PLAN = {}


def rank_program(g, core, T, topo):
    rank = T.rank_of(core)
    if rank is None:
        return
    if not PLAN:
        PLAN["ops"] = build(); PLAN["seq"] = order(PLAN["ops"])
    ops, seq = PLAN["ops"], PLAN["seq"]
    n = len(T.cores)
    Q = {"V": g.vector, "A": g.scalar, "T": g.tensor, "G": g, "S": g.sync}
    peers = [c for c in T.cores if c != core]
    turn = sorted(peers, key=lambda c: topo.die(c) == topo.die(core))
    mask = {c: sum(1 << e for e in topo.engines(core, c)[j::4]) for c, j in zip(turn, (0, 2, 1))}
    arrive = sum(len(topo.engines(c, core)) // 4 for c in peers)
    leave = sum(bin(m).count("1") for m in mask.values())
    sent = 0
    waited = set()
    for i in seq:
        o = ops[i]; k = o["k"]; a = o["a"]
        if k == "arr": continue
        q = Q[o["e"]]
        for j in o["wait"]:
            p = ops[j]
            q.wait_ge(T.sem[p["src"]], arrive if p["k"] == "arr" else p["val"]); waited.add(j)
        x = [real(T, y) for y in a] if k not in ("mm", "mms", "dma", "send") else None
        if k == "ts": r = q.tensor_scalar(*(x[:5] if x[5] is None else x))
        elif k == "tt": r = q.tensor_tensor(*x)
        elif k == "cp": r = q.tensor_copy(*x)
        elif k == "ms": r = q.memset(*x)
        elif k == "scan": r = q.tensor_tensor_scan(x[0], x[1], x[2], 0.0, x[3], x[4])
        elif k == "red": r = q.tensor_reduce(x[0], x[1], AX.X, AL.add, negate=x[2])
        elif k == "act": r = q.activation(*x[:3]) if x[2] == AF.Copy else q.activation(*x[:3], bias=x[3], scale=x[4])
        elif k == "iota": r = g.iota(*x) if a[0][0] == "PI" else g.iota(*x, allow_small_or_imprecise_dtypes=True)
        elif k == "sel": r = g.affine_select(*x)
        elif k == "mm":
            for m, (l, rr) in enumerate(a[1]):
                r = q.matmul(real(T, a[0]), real(T, l), real(T, rr), a[2] and m == 0, a[3] and m == len(a[1]) - 1)
        elif k == "mms":
            for oo, l, rr in a[0]: r = q.matmul(real(T, oo), real(T, l), real(T, rr), a[2], a[2])
        elif k == "dma":
            for oo, ii in a: q.dma_start(real(T, oo), real(T, ii)).then_inc(T.sem[o["src"]], 16)
            continue
        else:
            src, dst, wid, back, sem = a
            tr = []
            for d in range(1, n):
                c = T.cores[(rank - d if back else rank + d) % n]
                rid, pid, _se = topo.addr(c)
                s0, d0 = extent(src)[4] + wid * (d - 1), extent(dst)[4] + wid * (d - 1)
                tr.append(RemoteDMATransfer(dst_ids=[DstId(rid=rid, pnc=pid)], dma_engine_mask=mask[c], remote_sem=T.sem[sem],
                                            src=T[src[0]][:, s0:s0 + wid], dst=T[dst[0]][:, d0:d0 + wid]))
            g.remote_dma_fused(tr, local_sem=T.sem.loc); sent += leave
            continue
        if o.get("inc"): r.then_inc(T.sem[o["src"]], 1)
    g.wait_ge(T.sem.loc, sent)
    for i in seq:
        if ops[i]["k"] == "dma" and i not in waited: g.wait_ge(T.sem[ops[i]["src"]], ops[i]["val"])
